import numpy as np
import ml_dtypes


def mxq(x, axis, fmt="e4m3"):
    dtype, down = {"e4m3": (ml_dtypes.float8_e4m3fn, 7), "e5m2": (ml_dtypes.float8_e5m2, 14)}[fmt]
    v = np.moveaxis(np.asarray(x, np.float32).astype(ml_dtypes.bfloat16).astype(np.float64), axis, -1)
    blocks = v.reshape(v.shape[:-1] + (-1, 32))
    amax = np.abs(blocks).max(-1, keepdims=True)
    byte = np.maximum(np.where(amax > 0, np.frexp(amax)[1] - 1 + 127, 0) - down, 1)
    scale = np.exp2(byte - 127.0)
    codes = (blocks / scale).astype(np.float32).astype(dtype).astype(np.float64)
    return np.moveaxis((codes * scale).reshape(v.shape), -1, axis)


WIDE = False


def mx_kscale(k):
    if not WIDE:
        return np.ones(k)
    levels = np.array([10, -10, 5, -5, 0])
    if k % 512:
        return np.exp2(np.random.permutation(np.resize(levels, k // 32))).repeat(32)
    a = np.empty((k // 512, 16))
    for p in range(k // 512):
        a[p, :8] = np.random.permutation(np.resize(levels, 8))
        for g in range(8):
            far = levels[np.abs(levels - a[p, g]) >= 10]
            a[p, g + 8] = far[np.random.randint(len(far))]
    return np.exp2(a.ravel()).repeat(32)


def f64(x):
    return np.asarray(x).astype(np.float64)


def striped(idx):
    return np.tile(idx.reshape(-1, 16).T, (8, 1)).astype(np.uint16)


def unstriped(offs):
    return offs[:16].T.reshape(-1).astype(np.int64)


def pack_weight(w):
    k, n = w.shape
    w = f64(np.asarray(w, np.float32).astype(ml_dtypes.bfloat16)).reshape(k // 32, 32, n)
    amax = np.abs(w).max(1)
    byte = np.clip(np.where(amax > 0, np.frexp(amax)[1] - 1 + 127 - 7, 1), 1, 254)
    scaled = (w * np.exp2(127.0 - byte)[:, None, :]).reshape(k, n).astype(np.float32)
    words = np.ascontiguousarray(scaled.reshape(k // 512, 128, 4, n).transpose(0, 1, 3, 2)).astype(ml_dtypes.float8_e4m3fn).view(np.uint8)
    return words, np.ascontiguousarray(byte.astype(np.uint8).reshape(k // 512, 16, n))


def unpack_weight(words, scales):
    g, p, n, _ = words.shape
    vals = np.ascontiguousarray(words).view(ml_dtypes.float8_e4m3fn).astype(np.float64) * np.repeat(np.exp2(scales.astype(np.float64) - 127.0), 8, axis=1)[..., None]
    return vals.transpose(0, 1, 3, 2).reshape(g * 512, n)


def silu(v):
    return v / (1.0 + np.exp(-np.maximum(v, -700.0)))


K, T, E, C, N = 1024, 512, 4, 128, 512
M = 512


def by_expert(wq, xq):
    return np.concatenate([wq[e].T @ xq[:, e * C:(e + 1) * C] for e in range(E)], axis=1)


def setup_inputs():
    n = np.random.standard_normal
    s = mx_kscale(K)[:, None]
    packed = [pack_weight(m) for m in n((E, K, N)) / np.sqrt(K) / s[None]]
    r = mx_kscale(M)[:, None]
    return {
        "uT": (n((M, T)) * r).astype(np.float32),
        "wu": (n((M, K)) / np.sqrt(M) / r * s.T).astype(np.float32),
        "w_words": np.stack([m[0] for m in packed]),
        "w_scales": np.stack([m[1] for m in packed]),
        "b": (0.3 * n((N, E))).astype(np.float32),
        "gate": np.tile(np.random.uniform(0.2, 1.0, E * C), (N, 1)).astype(np.float32),
        "offs": striped(np.random.permutation(T)[:E * C]),
    }


def reference(uT, wu, w_words, w_scales, b, gate, offs):
    idx = unstriped(offs)
    w = np.stack([unpack_weight(w_words[e], w_scales[e]) for e in range(E)])
    x = mxq(f64(wu), 0, "e4m3").T @ mxq(f64(uT), 0, "e4m3")
    xq = mxq(x[:, idx], 0, "e4m3")
    y = by_expert(w, xq)
    y = silu(y + np.repeat(f64(b), C, axis=1))
    out = np.zeros((N, T))
    out[:, idx] = f64(gate) * y
    return out

@@ -1,0 +1,210 @@
+from contextlib import ExitStack
+
+import concourse.mybir as mybir
+
+F, K, T, E, C, N = 512, 1024, 512, 4, 128, 512
+FLOPS = 2 * F * K * T + 2 * K * N * E * C
+
+F32 = mybir.dt.float32
+BF16 = mybir.dt.bfloat16
+I32 = mybir.dt.int32
+U32 = mybir.dt.uint32
+U16 = mybir.dt.uint16
+U8 = mybir.dt.uint8
+FP8X4 = mybir.dt.float8_e4m3fn_x4
+SILU = mybir.ActivationFunctionType.Silu
+MULT = mybir.AluOpType.mult
+
+P = 128
+PACK = 4
+K_PASS = P * PACK
+PASSES = K // K_PASS
+N_TILES = N // P
+HALF = T // 2
+COLS = 256
+
+
+def tile_moe_prv_lin_silu_kernel(tc, uT, wu, w_words, w_scales, b, gate, offs, out):
+    nc = tc.nc
+    with ExitStack() as ctx:
+        keep = ctx.enter_context(tc.tile_pool(name="keep", bufs=1))
+        ring = ctx.enter_context(tc.tile_pool(name="ring", bufs=4))
+        x_psum = ctx.enter_context(tc.psum_pool(name="x_psum", bufs=4))
+        y_psum = ctx.enter_context(tc.psum_pool(name="y_psum", bufs=4))
+
+        offsets = keep.tile([P, T // 16], U16, name="offsets")
+        u_raw = [keep.tile([P, 2, T], F32, name=f"u_raw{h}") for h in range(2)]
+        wu_raw = [[keep.tile([P, PACK, COLS], F32, name=f"wu_raw{a}{c}") for c in range(2)] for a in range(PASSES)]
+        bias = keep.tile([P, N_TILES, E], F32, name="bias")
+        w_codes = [keep.tile([P, PASSES, N], U32, name=f"w_codes{e}", align_bytes=64) for e in range(E)]
+        w_planes = [keep.tile([P, N], U8, name=f"w_planes{g}", align_bytes=64) for g in range(2)]
+        gates = [keep.tile([P, T], F32, name=f"gates{nt}") for nt in range(N_TILES)]
+
+        for g in range(2):
+            nc.vector.memset(w_planes[g][:].bitcast(I32), 0)
+
+        u_rows = uT.rearrange("(p j) t -> p j t", j=PACK)
+        wu_rows = wu.rearrange("(p j) k -> p j k", j=PACK)
+        scale_rows = w_scales.rearrange("e a q n -> (e a) q n")
+
+        def load_codes(e):
+            nc.sync.dma_start(
+                out=w_codes[e][:].bitcast(I32),
+                in_=w_words[e].rearrange("a p n r -> p a (n r)").bitcast(I32),
+            )
+
+        def load_planes(g):
+            for q in range(4):
+                nc.sync.dma_start(
+                    out=w_planes[g][32 * q : 32 * q + 16, :].bitcast(I32),
+                    in_=scale_rows[4 * g : 4 * g + 4, 4 * q : 4 * q + 4, :].bitcast(I32),
+                )
+
+        def load_gate(nt):
+            nc.sync.dma_start(out=gates[nt][:], in_=gate[nt * P : (nt + 1) * P, :])
+
+        nc.sync.dma_start(out=u_raw[0][:], in_=u_rows[:, 0:2, :])
+        nc.sync.dma_start(offsets[:], offs)
+        nc.sync.dma_start(out=u_raw[1][:], in_=u_rows[:, 2:4, :])
+        for a in range(PASSES):
+            for c in range(2):
+                k0 = a * K_PASS + c * COLS
+                nc.sync.dma_start(out=wu_raw[a][c][:], in_=wu_rows[:, :, k0 : k0 + COLS])
+        nc.sync.dma_start(out=bias[:], in_=b.rearrange("(nt p) e -> p nt e", p=P))
+        load_codes(0)
+        load_planes(0)
+        load_gate(0)
+        load_gate(1)
+        load_codes(1)
+        load_gate(2)
+        load_gate(3)
+        load_planes(1)
+        load_codes(2)
+        load_codes(3)
+
+        u_pairs = [keep.tile([P, T], U32, name=f"u_pairs{h}") for h in range(2)]
+        u_slots = [keep.tile([P, HALF, 2], U32, name=f"u_slots{s}", align_bytes=64) for s in range(2)]
+        u_codes = [keep.tile([P, HALF], U32, name=f"u_codes{s}", align_bytes=64) for s in range(2)]
+        u_scales = [keep.tile([P, HALF], U8, name=f"u_scales{s}", align_bytes=64) for s in range(2)]
+
+        def pair_view(h):
+            return u_pairs[h][:].bitcast(BF16).rearrange("p (t j) -> p t j", j=2)
+
+        nc.vector.tensor_copy(out=pair_view(0), in_=u_raw[0][:].rearrange("p j t -> p t j"))
+        nc.scalar.copy(out=pair_view(1), in_=u_raw[1][:].rearrange("p j t -> p t j"))
+        for h in range(2):
+            for s in range(2):
+                nc.vector.tensor_copy(
+                    out=u_slots[s][:, :, h],
+                    in_=u_pairs[h][:].indirect(offsets[:, s * (HALF // 16) : (s + 1) * (HALF // 16)]),
+                )
+        for s in range(2):
+            nc.vector.quantize_mx(
+                out=u_codes[s][:].bitcast(FP8X4),
+                scales=u_scales[s][:],
+                in_=u_slots[s][:].rearrange("p c w -> p (c w)").bitcast(BF16),
+            )
+
+        wu_bf = [keep.tile([P, PACK, P, PACK], BF16, name=f"wu_bf{a}", align_bytes=64) for a in range(PASSES)]
+        wu_codes = [keep.tile([P, PACK, P], U32, name=f"wu_codes{a}", align_bytes=64) for a in range(PASSES)]
+        wu_scales = [keep.tile([P, PACK, P], U8, name=f"wu_scales{a}", align_bytes=64) for a in range(PASSES)]
+        m_chunk = COLS // PACK
+
+        def round_wu(a, c):
+            dst = wu_bf[a][:, :, c * m_chunk : (c + 1) * m_chunk, :].rearrange("p r m j -> p m r j")
+            src = wu_raw[a][c][:].rearrange("p j (m r) -> p m r j", r=PACK)
+            if a == 0:
+                nc.scalar.copy(out=dst, in_=src)
+            else:
+                nc.vector.tensor_copy(out=dst, in_=src)
+
+        def quantise_wu(a, r0, r1):
+            nc.vector.quantize_mx(
+                out=wu_codes[a][:, r0:r1, :].rearrange("p r m -> p (r m)").bitcast(FP8X4),
+                scales=wu_scales[a][:, r0:r1, :].rearrange("p r m -> p (r m)"),
+                in_=wu_bf[a][:, r0:r1, :, :].rearrange("p r m j -> p (r m j)"),
+            )
+
+        x_bf = {}
+        x_codes = {}
+        x_scales = {}
+
+        def project(e, a):
+            s, c0 = divmod(e * C, HALF)
+            bank = x_psum.tile([P, PACK, C], F32, name="x_bank")
+            for r in range(PACK):
+                nc.tensor.matmul_mx(
+                    out=bank[:, r, :],
+                    lhsT=wu_codes[a][:, r, :].bitcast(FP8X4),
+                    lhsT_scale=wu_scales[a][:, r, :],
+                    rhs=u_codes[s][:, c0 : c0 + C].bitcast(FP8X4),
+                    rhs_scale=u_scales[s][:, c0 : c0 + C],
+                    start=True,
+                    stop=True,
+                )
+            x_bf[e, a] = keep.tile([P, C, PACK], BF16, name=f"x_bf{e}{a}", align_bytes=64)
+            nc.scalar.copy(out=x_bf[e, a][:], in_=bank[:].rearrange("p r c -> p c r"))
+
+        def quantise_x(e, a):
+            x_codes[e, a] = keep.tile([P, C], U32, name=f"x_codes{e}{a}", align_bytes=64)
+            x_scales[e, a] = keep.tile([P, C], U8, name=f"x_scales{e}{a}", align_bytes=64)
+            nc.vector.quantize_mx(
+                out=x_codes[e, a][:].bitcast(FP8X4),
+                scales=x_scales[e, a][:],
+                in_=x_bf[e, a][:].rearrange("p c r -> p (c r)"),
+            )
+
+        y = {}
+
+        def expert(e):
+            for nt in range(N_TILES):
+                cols = slice(nt * P, (nt + 1) * P)
+                bank = y_psum.tile([P, C], F32, name="y_bank")
+                for a in range(PASSES):
+                    g, j = divmod(e * PASSES + a, 4)
+                    nc.tensor.matmul_mx(
+                        out=bank[:],
+                        lhsT=w_codes[e][:, a, cols].bitcast(FP8X4),
+                        lhsT_scale=w_planes[g][4 * j : P, cols],
+                        rhs=x_codes[e, a][:].bitcast(FP8X4),
+                        rhs_scale=x_scales[e, a][:],
+                        start=(a == 0),
+                        stop=(a == PASSES - 1),
+                    )
+                y[e, nt] = ring.tile([P, C], F32, name=f"y{nt}", bufs=2)
+                nc.scalar.activation(out=y[e, nt][:], in_=bank[:], func=SILU, bias=bias[:, nt, e : e + 1])
+
+        results = [keep.tile([P, T], F32, name=f"results{nt}") for nt in range(N_TILES)]
+
+        def scatter(e, nt):
+            nc.vector.tensor_tensor(
+                results[nt][:].indirect(offsets[:, e * (C // 16) : (e + 1) * (C // 16)]),
+                y[e, nt][:],
+                gates[nt][:, e * C : (e + 1) * C],
+                MULT,
+            )
+
+        for c in range(2):
+            round_wu(0, c)
+        round_wu(1, 0)
+        quantise_wu(0, 0, PACK)
+        round_wu(1, 1)
+        project(0, 0)
+        for r in range(PACK):
+            quantise_wu(1, r, r + 1)
+        project(0, 1)
+        quantise_x(0, 0)
+        quantise_x(0, 1)
+        expert(0)
+        for e in range(E):
+            scatter(e, 0)
+            scatter(e, 1)
+            if e + 1 < E:
+                for a in range(PASSES):
+                    project(e + 1, a)
+                    quantise_x(e + 1, a)
+                expert(e + 1)
+            scatter(e, 2)
+            scatter(e, 3)
+        for nt in range(N_TILES):
+            nc.sync.dma_start(out=out[nt * P : (nt + 1) * P, :], in_=results[nt][:])

@@ -22,23 +22,30 @@ PASSES = K // K_PASS
 N_TILES = N // P
 HALF = T // 2
 COLS = 256
+M_CHUNK = COLS // PACK
+SPLIT = 36
+GROUPS = ((0,), (1,), (2, 3))
 
 
 def tile_moe_prv_lin_silu_kernel(tc, uT, wu, w_words, w_scales, b, gate, offs, out):
     nc = tc.nc
     with ExitStack() as ctx:
         keep = ctx.enter_context(tc.tile_pool(name="keep", bufs=1))
-        ring = ctx.enter_context(tc.tile_pool(name="ring", bufs=4))
         x_psum = ctx.enter_context(tc.psum_pool(name="x_psum", bufs=4))
         y_psum = ctx.enter_context(tc.psum_pool(name="y_psum", bufs=4))
 
         offsets = keep.tile([P, T // 16], U16, name="offsets")
         u_raw = [keep.tile([P, 2, T], F32, name=f"u_raw{h}") for h in range(2)]
-        wu_raw = [[keep.tile([P, PACK, COLS], F32, name=f"wu_raw{a}{c}") for c in range(2)] for a in range(PASSES)]
+        wu_raw = [[keep.tile([P, PACK, COLS], F32, name=f"wu_raw{a}{h}") for h in range(2)] for a in range(PASSES)]
         bias = keep.tile([P, N_TILES, E], F32, name="bias")
         w_codes = [keep.tile([P, PASSES, N], U32, name=f"w_codes{e}", align_bytes=64) for e in range(E)]
         w_planes = [keep.tile([P, N], U8, name=f"w_planes{g}", align_bytes=64) for g in range(2)]
         gates = [keep.tile([P, T], F32, name=f"gates{nt}") for nt in range(N_TILES)]
+
+        warm_in = keep.tile([P, 1], F32, name="warm_in")
+        warm_out = keep.tile([P, 1], F32, name="warm_out")
+        nc.vector.memset(warm_in[:], 0.0)
+        nc.scalar.activation(out=warm_out[:], in_=warm_in[:], func=SILU)
 
         for g in range(2):
             nc.vector.memset(w_planes[g][:].bitcast(I32), 0)
@@ -67,12 +74,12 @@ def tile_moe_prv_lin_silu_kernel(tc, uT, wu, w_words, w_scales, b, gate, offs, o
         nc.sync.dma_start(offsets[:], offs)
         nc.sync.dma_start(out=u_raw[1][:], in_=u_rows[:, 2:4, :])
         for a in range(PASSES):
-            for c in range(2):
-                k0 = a * K_PASS + c * COLS
-                nc.sync.dma_start(out=wu_raw[a][c][:], in_=wu_rows[:, :, k0 : k0 + COLS])
-        nc.sync.dma_start(out=bias[:], in_=b.rearrange("(nt p) e -> p nt e", p=P))
+            for h in range(2):
+                k0 = a * K_PASS + h * COLS
+                nc.sync.dma_start(out=wu_raw[a][h][:], in_=wu_rows[:, :, k0 : k0 + COLS])
         load_codes(0)
         load_planes(0)
+        nc.sync.dma_start(out=bias[:], in_=b.rearrange("(nt p) e -> p nt e", p=P))
         load_gate(0)
         load_gate(1)
         load_codes(1)
@@ -108,15 +115,11 @@ def tile_moe_prv_lin_silu_kernel(tc, uT, wu, w_words, w_scales, b, gate, offs, o
         wu_bf = [keep.tile([P, PACK, P, PACK], BF16, name=f"wu_bf{a}", align_bytes=64) for a in range(PASSES)]
         wu_codes = [keep.tile([P, PACK, P], U32, name=f"wu_codes{a}", align_bytes=64) for a in range(PASSES)]
         wu_scales = [keep.tile([P, PACK, P], U8, name=f"wu_scales{a}", align_bytes=64) for a in range(PASSES)]
-        m_chunk = COLS // PACK
 
-        def round_wu(a, c):
-            dst = wu_bf[a][:, :, c * m_chunk : (c + 1) * m_chunk, :].rearrange("p r m j -> p m r j")
-            src = wu_raw[a][c][:].rearrange("p j (m r) -> p m r j", r=PACK)
-            if a == 0:
-                nc.scalar.copy(out=dst, in_=src)
-            else:
-                nc.vector.tensor_copy(out=dst, in_=src)
+        def round_wu(a, h, m0, m1, copy):
+            dst = wu_bf[a][:, :, h * M_CHUNK + m0 : h * M_CHUNK + m1, :].rearrange("p r m j -> p m r j")
+            src = wu_raw[a][h][:].rearrange("p j (m r) -> p m r j", r=PACK)[:, m0:m1, :, :]
+            copy(out=dst, in_=src)
 
         def quantise_wu(a, r0, r1):
             nc.vector.quantize_mx(
@@ -125,9 +128,9 @@ def tile_moe_prv_lin_silu_kernel(tc, uT, wu, w_words, w_scales, b, gate, offs, o
                 in_=wu_bf[a][:, r0:r1, :, :].rearrange("p r m j -> p (r m j)"),
             )
 
-        x_bf = {}
-        x_codes = {}
-        x_scales = {}
+        x_bf = keep.tile([P, E, PASSES, C, PACK], BF16, name="x_bf", align_bytes=64)
+        x_codes = keep.tile([P, E, PASSES, C], U32, name="x_codes", align_bytes=64)
+        x_scales = keep.tile([P, E, PASSES, C], U8, name="x_scales", align_bytes=64)
 
         def project(e, a):
             s, c0 = divmod(e * C, HALF)
@@ -142,69 +145,73 @@ def tile_moe_prv_lin_silu_kernel(tc, uT, wu, w_words, w_scales, b, gate, offs, o
                     start=True,
                     stop=True,
                 )
-            x_bf[e, a] = keep.tile([P, C, PACK], BF16, name=f"x_bf{e}{a}", align_bytes=64)
-            nc.scalar.copy(out=x_bf[e, a][:], in_=bank[:].rearrange("p r c -> p c r"))
+            nc.scalar.copy(out=x_bf[:, e, a, :, :], in_=bank[:].rearrange("p r c -> p c r"))
 
-        def quantise_x(e, a):
-            x_codes[e, a] = keep.tile([P, C], U32, name=f"x_codes{e}{a}", align_bytes=64)
-            x_scales[e, a] = keep.tile([P, C], U8, name=f"x_scales{e}{a}", align_bytes=64)
+        def quantise_x(first, count):
+            words = slice(first * C, (first + count) * C)
+            values = slice(first * C * PACK, (first + count) * C * PACK)
             nc.vector.quantize_mx(
-                out=x_codes[e, a][:].bitcast(FP8X4),
-                scales=x_scales[e, a][:],
-                in_=x_bf[e, a][:].rearrange("p c r -> p (c r)"),
+                out=x_codes[:].rearrange("p e a c -> p (e a c)")[:, words].bitcast(FP8X4),
+                scales=x_scales[:].rearrange("p e a c -> p (e a c)")[:, words],
+                in_=x_bf[:].rearrange("p e a c r -> p (e a c r)")[:, values],
             )
 
-        y = {}
+        y = [keep.tile([P, E * C], F32, name=f"y{nt}") for nt in range(N_TILES)]
 
-        def expert(e):
+        def experts(group):
             for nt in range(N_TILES):
                 cols = slice(nt * P, (nt + 1) * P)
-                bank = y_psum.tile([P, C], F32, name="y_bank")
-                for a in range(PASSES):
-                    g, j = divmod(e * PASSES + a, 4)
-                    nc.tensor.matmul_mx(
-                        out=bank[:],
-                        lhsT=w_codes[e][:, a, cols].bitcast(FP8X4),
-                        lhsT_scale=w_planes[g][4 * j : P, cols],
-                        rhs=x_codes[e, a][:].bitcast(FP8X4),
-                        rhs_scale=x_scales[e, a][:],
-                        start=(a == 0),
-                        stop=(a == PASSES - 1),
+                for e in group:
+                    bank = y_psum.tile([P, C], F32, name="y_bank")
+                    for a in range(PASSES):
+                        g, j = divmod(e * PASSES + a, 4)
+                        nc.tensor.matmul_mx(
+                            out=bank[:],
+                            lhsT=w_codes[e][:, a, cols].bitcast(FP8X4),
+                            lhsT_scale=w_planes[g][4 * j : P, cols],
+                            rhs=x_codes[:, e, a, :].bitcast(FP8X4),
+                            rhs_scale=x_scales[:, e, a, :],
+                            start=(a == 0),
+                            stop=(a == PASSES - 1),
+                        )
+                    nc.scalar.activation(
+                        out=y[nt][:, e * C : (e + 1) * C], in_=bank[:], func=SILU, bias=bias[:, nt, e : e + 1]
                     )
-                y[e, nt] = ring.tile([P, C], F32, name=f"y{nt}", bufs=2)
-                nc.scalar.activation(out=y[e, nt][:], in_=bank[:], func=SILU, bias=bias[:, nt, e : e + 1])
 
         results = [keep.tile([P, T], F32, name=f"results{nt}") for nt in range(N_TILES)]
 
-        def scatter(e, nt):
+        def scatter(group, nt):
+            s0, s1 = group[0] * C, (group[-1] + 1) * C
             nc.vector.tensor_tensor(
-                results[nt][:].indirect(offsets[:, e * (C // 16) : (e + 1) * (C // 16)]),
-                y[e, nt][:],
-                gates[nt][:, e * C : (e + 1) * C],
+                results[nt][:].indirect(offsets[:, s0 // 16 : s1 // 16]),
+                y[nt][:, s0:s1],
+                gates[nt][:, s0:s1],
                 MULT,
             )
 
-        for c in range(2):
-            round_wu(0, c)
-        round_wu(1, 0)
+        for h in range(2):
+            round_wu(0, h, 0, M_CHUNK, nc.scalar.copy)
+        round_wu(1, 0, 0, M_CHUNK, nc.vector.tensor_copy)
         quantise_wu(0, 0, PACK)
-        round_wu(1, 1)
+        round_wu(1, 1, 0, SPLIT, nc.vector.tensor_copy)
+        round_wu(1, 1, SPLIT, M_CHUNK, nc.scalar.copy)
         project(0, 0)
         for r in range(PACK):
             quantise_wu(1, r, r + 1)
         project(0, 1)
-        quantise_x(0, 0)
         quantise_x(0, 1)
-        expert(0)
-        for e in range(E):
-            scatter(e, 0)
-            scatter(e, 1)
-            if e + 1 < E:
-                for a in range(PASSES):
-                    project(e + 1, a)
-                    quantise_x(e + 1, a)
-                expert(e + 1)
-            scatter(e, 2)
-            scatter(e, 3)
+        quantise_x(1, 1)
+        experts(GROUPS[0])
+        for i, group in enumerate(GROUPS):
+            scatter(group, 0)
+            if i + 1 < len(GROUPS):
+                ahead = GROUPS[i + 1]
+                for e in ahead:
+                    for a in range(PASSES):
+                        project(e, a)
+                quantise_x(ahead[0] * PASSES, len(ahead) * PASSES)
+                experts(ahead)
+            for nt in range(1, N_TILES):
+                scatter(group, nt)
         for nt in range(N_TILES):
             nc.sync.dma_start(out=out[nt * P : (nt + 1) * P, :], in_=results[nt][:])

@@ -21,9 +21,9 @@ K_PASS = P * PACK
 PASSES = K // K_PASS
 N_TILES = N // P
 HALF = T // 2
-COLS = 256
-M_CHUNK = COLS // PACK
-SPLIT = 36
+WU_CHUNKS = ((0, 0, 64, 0), (0, 64, 128, 0), (1, 0, 64, 40), (1, 64, 128, 40))
+X_BANK = ((0, 2), (1, 3), (4, 5), (6, 7))
+Y_BANK = ((4, 5, 6, 7), (0, 1, 2, 3), (4, 6, 0, 2), (5, 7, 1, 3))
 GROUPS = ((0,), (1,), (2, 3))
 
 
@@ -31,16 +31,16 @@ def tile_moe_prv_lin_silu_kernel(tc, uT, wu, w_words, w_scales, b, gate, offs, o
     nc = tc.nc
     with ExitStack() as ctx:
         keep = ctx.enter_context(tc.tile_pool(name="keep", bufs=1))
-        x_psum = ctx.enter_context(tc.psum_pool(name="x_psum", bufs=4))
-        y_psum = ctx.enter_context(tc.psum_pool(name="y_psum", bufs=4))
+        psum = ctx.enter_context(tc.psum_pool(name="psum", bufs=1))
 
         offsets = keep.tile([P, T // 16], U16, name="offsets")
         u_raw = [keep.tile([P, 2, T], F32, name=f"u_raw{h}") for h in range(2)]
-        wu_raw = [[keep.tile([P, PACK, COLS], F32, name=f"wu_raw{a}{h}") for h in range(2)] for a in range(PASSES)]
+        wu_raw = [keep.tile([P, PACK, PACK * (m1 - m0)], F32, name=f"wu_raw{a}_{m0}") for a, m0, m1, share in WU_CHUNKS]
         bias = keep.tile([P, N_TILES, E], F32, name="bias")
         w_codes = [keep.tile([P, PASSES, N], U32, name=f"w_codes{e}", align_bytes=64) for e in range(E)]
         w_planes = [keep.tile([P, N], U8, name=f"w_planes{g}", align_bytes=64) for g in range(2)]
-        gates = [keep.tile([P, T], F32, name=f"gates{nt}") for nt in range(N_TILES)]
+        gates_low = [keep.tile([P, 2, HALF], F32, name=f"gates_low{i}") for i in range(2)]
+        gates_high = keep.tile([P, N_TILES, HALF], F32, name="gates_high")
 
         warm_in = keep.tile([P, 1], F32, name="warm_in")
         warm_out = keep.tile([P, 1], F32, name="warm_out")
@@ -67,35 +67,32 @@ def tile_moe_prv_lin_silu_kernel(tc, uT, wu, w_words, w_scales, b, gate, offs, o
                     in_=scale_rows[4 * g : 4 * g + 4, 4 * q : 4 * q + 4, :].bitcast(I32),
                 )
 
-        def load_gate(nt):
-            nc.sync.dma_start(out=gates[nt][:], in_=gate[nt * P : (nt + 1) * P, :])
+        gate_rows = gate.rearrange("(nt p) s -> p nt s", p=P)
 
         nc.sync.dma_start(out=u_raw[0][:], in_=u_rows[:, 0:2, :])
         nc.sync.dma_start(offsets[:], offs)
         nc.sync.dma_start(out=u_raw[1][:], in_=u_rows[:, 2:4, :])
-        for a in range(PASSES):
-            for h in range(2):
-                k0 = a * K_PASS + h * COLS
-                nc.sync.dma_start(out=wu_raw[a][h][:], in_=wu_rows[:, :, k0 : k0 + COLS])
+        for raw, (a, m0, m1, share) in zip(wu_raw, WU_CHUNKS):
+            nc.sync.dma_start(out=raw[:], in_=wu_rows[:, :, a * K_PASS + PACK * m0 : a * K_PASS + PACK * m1])
         load_codes(0)
         load_planes(0)
         nc.sync.dma_start(out=bias[:], in_=b.rearrange("(nt p) e -> p nt e", p=P))
-        load_gate(0)
-        load_gate(1)
+        nc.sync.dma_start(out=gates_low[0][:], in_=gate_rows[:, 0:2, 0:HALF])
         load_codes(1)
-        load_gate(2)
-        load_gate(3)
+        nc.sync.dma_start(out=gates_low[1][:], in_=gate_rows[:, 2:4, 0:HALF])
         load_planes(1)
         load_codes(2)
         load_codes(3)
+        nc.sync.dma_start(out=gates_high[:], in_=gate_rows[:, :, HALF:T])
 
         u_pairs = [keep.tile([P, T], U32, name=f"u_pairs{h}") for h in range(2)]
-        u_slots = [keep.tile([P, HALF, 2], U32, name=f"u_slots{s}", align_bytes=64) for s in range(2)]
-        u_codes = [keep.tile([P, HALF], U32, name=f"u_codes{s}", align_bytes=64) for s in range(2)]
-        u_scales = [keep.tile([P, HALF], U8, name=f"u_scales{s}", align_bytes=64) for s in range(2)]
+        u_codes = keep.tile([P, T], U32, name="u_codes", align_bytes=64)
+        u_scales = keep.tile([P, T], U8, name="u_scales", align_bytes=64)
 
         def pair_view(h):
             return u_pairs[h][:].bitcast(BF16).rearrange("p (t j) -> p t j", j=2)
+
+        u_slots = [keep.tile([P, HALF, 2], U32, name=f"u_slots{s}", align_bytes=64) for s in range(2)]
 
         nc.vector.tensor_copy(out=pair_view(0), in_=u_raw[0][:].rearrange("p j t -> p t j"))
         nc.scalar.copy(out=pair_view(1), in_=u_raw[1][:].rearrange("p j t -> p t j"))
@@ -107,19 +104,21 @@ def tile_moe_prv_lin_silu_kernel(tc, uT, wu, w_words, w_scales, b, gate, offs, o
                 )
         for s in range(2):
             nc.vector.quantize_mx(
-                out=u_codes[s][:].bitcast(FP8X4),
-                scales=u_scales[s][:],
+                out=u_codes[:, s * HALF : (s + 1) * HALF].bitcast(FP8X4),
+                scales=u_scales[:, s * HALF : (s + 1) * HALF],
                 in_=u_slots[s][:].rearrange("p c w -> p (c w)").bitcast(BF16),
             )
 
-        wu_bf = [keep.tile([P, PACK, P, PACK], BF16, name=f"wu_bf{a}", align_bytes=64) for a in range(PASSES)]
+        wu_bf = [keep.tile([P, PACK, P, PACK], BF16, name=f"wu_bf{a}", tag=f"wu_bf{a}", align_bytes=64) for a in range(PASSES)]
         wu_codes = [keep.tile([P, PACK, P], U32, name=f"wu_codes{a}", align_bytes=64) for a in range(PASSES)]
         wu_scales = [keep.tile([P, PACK, P], U8, name=f"wu_scales{a}", align_bytes=64) for a in range(PASSES)]
 
-        def round_wu(a, h, m0, m1, copy):
-            dst = wu_bf[a][:, :, h * M_CHUNK + m0 : h * M_CHUNK + m1, :].rearrange("p r m j -> p m r j")
-            src = wu_raw[a][h][:].rearrange("p j (m r) -> p m r j", r=PACK)[:, m0:m1, :, :]
-            copy(out=dst, in_=src)
+        def round_wu(raw, a, m0, m1, share):
+            dst = wu_bf[a][:, :, m0:m1, :].rearrange("p r m j -> p m r j")
+            src = raw[:].rearrange("p j (m r) -> p m r j", r=PACK)
+            nc.scalar.copy(out=dst[:, share:, :, :], in_=src[:, share:, :, :])
+            if share:
+                nc.vector.tensor_copy(out=dst[:, :share, :, :], in_=src[:, :share, :, :])
 
         def quantise_wu(a, r0, r1):
             nc.vector.quantize_mx(
@@ -128,90 +127,101 @@ def tile_moe_prv_lin_silu_kernel(tc, uT, wu, w_words, w_scales, b, gate, offs, o
                 in_=wu_bf[a][:, r0:r1, :, :].rearrange("p r m j -> p (r m j)"),
             )
 
-        x_bf = keep.tile([P, E, PASSES, C, PACK], BF16, name="x_bf", align_bytes=64)
+        x_bf = {}
+        for group, tag in zip(GROUPS, ("x_first", "shared1", "shared2")):
+            tile = keep.tile([P, len(group), PASSES, C, PACK], BF16, name=f"x_bf{group[0]}", tag=tag, align_bytes=64)
+            x_bf[group] = tile
         x_codes = keep.tile([P, E, PASSES, C], U32, name="x_codes", align_bytes=64)
         x_scales = keep.tile([P, E, PASSES, C], U8, name="x_scales", align_bytes=64)
 
-        def project(e, a):
-            s, c0 = divmod(e * C, HALF)
-            bank = x_psum.tile([P, PACK, C], F32, name="x_bank")
+        def project(group, e, a):
+            bank = psum.tile([P, PACK, C], F32, name=f"bank{X_BANK[e][a]}")
             for r in range(PACK):
                 nc.tensor.matmul_mx(
                     out=bank[:, r, :],
                     lhsT=wu_codes[a][:, r, :].bitcast(FP8X4),
                     lhsT_scale=wu_scales[a][:, r, :],
-                    rhs=u_codes[s][:, c0 : c0 + C].bitcast(FP8X4),
-                    rhs_scale=u_scales[s][:, c0 : c0 + C],
+                    rhs=u_codes[:, e * C : (e + 1) * C].bitcast(FP8X4),
+                    rhs_scale=u_scales[:, e * C : (e + 1) * C],
                     start=True,
                     stop=True,
                 )
-            nc.scalar.copy(out=x_bf[:, e, a, :, :], in_=bank[:].rearrange("p r c -> p c r"))
+            nc.scalar.copy(out=x_bf[group][:, e - group[0], a, :, :], in_=bank[:].rearrange("p r c -> p c r"))
 
-        def quantise_x(first, count):
-            words = slice(first * C, (first + count) * C)
+        def quantise_x(group, first, count):
+            w0 = (group[0] * PASSES + first) * C
+            words = slice(w0, w0 + count * C)
             values = slice(first * C * PACK, (first + count) * C * PACK)
             nc.vector.quantize_mx(
                 out=x_codes[:].rearrange("p e a c -> p (e a c)")[:, words].bitcast(FP8X4),
                 scales=x_scales[:].rearrange("p e a c -> p (e a c)")[:, words],
-                in_=x_bf[:].rearrange("p e a c r -> p (e a c r)")[:, values],
+                in_=x_bf[group][:].rearrange("p e a c r -> p (e a c r)")[:, values],
             )
 
         y = [keep.tile([P, E * C], F32, name=f"y{nt}") for nt in range(N_TILES)]
 
-        def experts(group):
-            for nt in range(N_TILES):
-                cols = slice(nt * P, (nt + 1) * P)
-                for e in group:
-                    bank = y_psum.tile([P, C], F32, name="y_bank")
-                    for a in range(PASSES):
-                        g, j = divmod(e * PASSES + a, 4)
-                        nc.tensor.matmul_mx(
-                            out=bank[:],
-                            lhsT=w_codes[e][:, a, cols].bitcast(FP8X4),
-                            lhsT_scale=w_planes[g][4 * j : P, cols],
-                            rhs=x_codes[:, e, a, :].bitcast(FP8X4),
-                            rhs_scale=x_scales[:, e, a, :],
-                            start=(a == 0),
-                            stop=(a == PASSES - 1),
-                        )
-                    nc.scalar.activation(
-                        out=y[nt][:, e * C : (e + 1) * C], in_=bank[:], func=SILU, bias=bias[:, nt, e : e + 1]
-                    )
+        def expert(e, nt):
+            cols = slice(nt * P, (nt + 1) * P)
+            bank = psum.tile([P, C], F32, name=f"bank{Y_BANK[e][nt]}")
+            for a in range(PASSES):
+                g, j = divmod(e * PASSES + a, 4)
+                nc.tensor.matmul_mx(
+                    out=bank[:],
+                    lhsT=w_codes[e][:, a, cols].bitcast(FP8X4),
+                    lhsT_scale=w_planes[g][4 * j : P, cols],
+                    rhs=x_codes[:, e, a, :].bitcast(FP8X4),
+                    rhs_scale=x_scales[:, e, a, :],
+                    start=(a == 0),
+                    stop=(a == PASSES - 1),
+                )
+            nc.scalar.activation(
+                out=y[nt][:, e * C : (e + 1) * C], in_=bank[:], func=SILU, bias=bias[:, nt, e : e + 1]
+            )
 
-        results = [keep.tile([P, T], F32, name=f"results{nt}") for nt in range(N_TILES)]
+        results = {}
 
         def scatter(group, nt):
+            if nt not in results:
+                results[nt] = keep.tile([P, T], F32, name=f"results{nt}", tag=f"shared{nt}", align_bytes=64)
             s0, s1 = group[0] * C, (group[-1] + 1) * C
             nc.vector.tensor_tensor(
                 results[nt][:].indirect(offsets[:, s0 // 16 : s1 // 16]),
                 y[nt][:, s0:s1],
-                gates[nt][:, s0:s1],
+                gates_low[nt // 2][:, nt % 2, s0:s1] if s1 <= HALF else gates_high[:, nt, :],
                 MULT,
             )
 
-        for h in range(2):
-            round_wu(0, h, 0, M_CHUNK, nc.scalar.copy)
-        round_wu(1, 0, 0, M_CHUNK, nc.vector.tensor_copy)
-        quantise_wu(0, 0, PACK)
-        round_wu(1, 1, 0, SPLIT, nc.vector.tensor_copy)
-        round_wu(1, 1, SPLIT, M_CHUNK, nc.scalar.copy)
-        project(0, 0)
+        first, second, rest = GROUPS
+        for raw, (a, m0, m1, share) in zip(wu_raw, WU_CHUNKS):
+            round_wu(raw, a, m0, m1, share)
+            if (a, m0) == (1, 0):
+                for r in range(0, PACK, 2):
+                    quantise_wu(0, r, r + 2)
+        project(first, 0, 0)
+        project(second, 1, 0)
         for r in range(PACK):
             quantise_wu(1, r, r + 1)
-        project(0, 1)
-        quantise_x(0, 1)
-        quantise_x(1, 1)
-        experts(GROUPS[0])
-        for i, group in enumerate(GROUPS):
-            scatter(group, 0)
-            if i + 1 < len(GROUPS):
-                ahead = GROUPS[i + 1]
-                for e in ahead:
-                    for a in range(PASSES):
-                        project(e, a)
-                quantise_x(ahead[0] * PASSES, len(ahead) * PASSES)
-                experts(ahead)
-            for nt in range(1, N_TILES):
-                scatter(group, nt)
+        project(first, 0, 1)
+        project(second, 1, 1)
+        quantise_x(first, 0, 1)
+        quantise_x(first, 1, 1)
         for nt in range(N_TILES):
+            expert(0, nt)
+        scatter(first, 0)
+        quantise_x(second, 0, PASSES)
+        scatter(first, 1)
+        for nt in range(2):
+            expert(1, nt)
+            scatter(second, nt)
+        for e in rest:
+            for a in range(PASSES):
+                project(rest, e, a)
+        quantise_x(rest, 0, 2 * PASSES)
+        for nt in range(2, N_TILES):
+            expert(1, nt)
+            scatter(first + second, nt)
+        for nt in range(N_TILES):
+            for e in rest:
+                expert(e, nt)
+            scatter(rest, nt)
             nc.sync.dma_start(out=out[nt * P : (nt + 1) * P, :], in_=results[nt][:])

@@ -39,8 +39,7 @@ def tile_moe_prv_lin_silu_kernel(tc, uT, wu, w_words, w_scales, b, gate, offs, o
         bias = keep.tile([P, N_TILES, E], F32, name="bias")
         w_codes = [keep.tile([P, PASSES, N], U32, name=f"w_codes{e}", align_bytes=64) for e in range(E)]
         w_planes = [keep.tile([P, N], U8, name=f"w_planes{g}", align_bytes=64) for g in range(2)]
-        gates_low = [keep.tile([P, 2, HALF], F32, name=f"gates_low{i}") for i in range(2)]
-        gates_high = keep.tile([P, N_TILES, HALF], F32, name="gates_high")
+        gates = keep.tile([P, T], F32, name="gates")
 
         warm_in = keep.tile([P, 1], F32, name="warm_in")
         warm_out = keep.tile([P, 1], F32, name="warm_out")
@@ -67,8 +66,6 @@ def tile_moe_prv_lin_silu_kernel(tc, uT, wu, w_words, w_scales, b, gate, offs, o
                     in_=scale_rows[4 * g : 4 * g + 4, 4 * q : 4 * q + 4, :].bitcast(I32),
                 )
 
-        gate_rows = gate.rearrange("(nt p) s -> p nt s", p=P)
-
         nc.sync.dma_start(out=u_raw[0][:], in_=u_rows[:, 0:2, :])
         nc.sync.dma_start(offsets[:], offs)
         nc.sync.dma_start(out=u_raw[1][:], in_=u_rows[:, 2:4, :])
@@ -77,13 +74,11 @@ def tile_moe_prv_lin_silu_kernel(tc, uT, wu, w_words, w_scales, b, gate, offs, o
         load_codes(0)
         load_planes(0)
         nc.sync.dma_start(out=bias[:], in_=b.rearrange("(nt p) e -> p nt e", p=P))
-        nc.sync.dma_start(out=gates_low[0][:], in_=gate_rows[:, 0:2, 0:HALF])
+        nc.sync.dma_start(out=gates[:], in_=gate[0:P, :])
         load_codes(1)
-        nc.sync.dma_start(out=gates_low[1][:], in_=gate_rows[:, 2:4, 0:HALF])
         load_planes(1)
         load_codes(2)
         load_codes(3)
-        nc.sync.dma_start(out=gates_high[:], in_=gate_rows[:, :, HALF:T])
 
         u_pairs = [keep.tile([P, T], U32, name=f"u_pairs{h}") for h in range(2)]
         u_codes = keep.tile([P, T], U32, name="u_codes", align_bytes=64)
@@ -114,8 +109,8 @@ def tile_moe_prv_lin_silu_kernel(tc, uT, wu, w_words, w_scales, b, gate, offs, o
         wu_scales = [keep.tile([P, PACK, P], U8, name=f"wu_scales{a}", align_bytes=64) for a in range(PASSES)]
 
         def round_wu(raw, a, m0, m1, share):
-            dst = wu_bf[a][:, :, m0:m1, :].rearrange("p r m j -> p m r j")
-            src = raw[:].rearrange("p j (m r) -> p m r j", r=PACK)
+            dst = wu_bf[a][:, :, m0:m1, :].rearrange("p r m j -> p m j r")
+            src = raw[:].rearrange("p j (m r) -> p m j r", r=PACK)
             nc.scalar.copy(out=dst[:, share:, :, :], in_=src[:, share:, :, :])
             if share:
                 nc.vector.tensor_copy(out=dst[:, :share, :, :], in_=src[:, :share, :, :])
@@ -187,7 +182,7 @@ def tile_moe_prv_lin_silu_kernel(tc, uT, wu, w_words, w_scales, b, gate, offs, o
             nc.vector.tensor_tensor(
                 results[nt][:].indirect(offsets[:, s0 // 16 : s1 // 16]),
                 y[nt][:, s0:s1],
-                gates_low[nt // 2][:, nt % 2, s0:s1] if s1 <= HALF else gates_high[:, nt, :],
+                gates[:, s0:s1],
                 MULT,
             )
 

@@ -21,7 +21,9 @@ K_PASS = P * PACK
 PASSES = K // K_PASS
 N_TILES = N // P
 HALF = T // 2
-WU_CHUNKS = ((0, 0, 64, 0), (0, 64, 128, 0), (1, 0, 64, 40), (1, 64, 128, 40))
+WU_CHUNKS = ((0, 0, 64, 0), (0, 64, 128, 32), (1, 0, 64, 22), (1, 64, 128, 44))
+U_SHARE = (336, 160)
+EARLY = 384
 X_BANK = ((0, 2), (1, 3), (4, 5), (6, 7))
 Y_BANK = ((4, 5, 6, 7), (0, 1, 2, 3), (4, 6, 0, 2), (5, 7, 1, 3))
 GROUPS = ((0,), (1,), (2, 3))
@@ -35,7 +37,7 @@ def tile_moe_prv_lin_silu_kernel(tc, uT, wu, w_words, w_scales, b, gate, offs, o
 
         offsets = keep.tile([P, T // 16], U16, name="offsets")
         u_raw = [keep.tile([P, 2, T], F32, name=f"u_raw{h}") for h in range(2)]
-        wu_raw = [keep.tile([P, PACK, PACK * (m1 - m0)], F32, name=f"wu_raw{a}_{m0}") for a, m0, m1, share in WU_CHUNKS]
+        wu_raw = [keep.tile([P, PACK, PACK * (m1 - m0)], F32, name=f"wu_raw{a}_{m0}", tag=f"wu_raw{a}_{m0}", align_bytes=64) for a, m0, m1, share in WU_CHUNKS]
         bias = keep.tile([P, N_TILES, E], F32, name="bias")
         w_codes = [keep.tile([P, PASSES, N], U32, name=f"w_codes{e}", align_bytes=64) for e in range(E)]
         w_planes = [keep.tile([P, N], U8, name=f"w_planes{g}", align_bytes=64) for g in range(2)]
@@ -81,30 +83,43 @@ def tile_moe_prv_lin_silu_kernel(tc, uT, wu, w_words, w_scales, b, gate, offs, o
         load_codes(3)
 
         u_pairs = [keep.tile([P, T], U32, name=f"u_pairs{h}") for h in range(2)]
-        u_codes = keep.tile([P, T], U32, name="u_codes", align_bytes=64)
+        u_codes = keep.tile([P, HALF], U32, name="u_codes", align_bytes=64)
         u_scales = keep.tile([P, T], U8, name="u_scales", align_bytes=64)
 
         def pair_view(h):
             return u_pairs[h][:].bitcast(BF16).rearrange("p (t j) -> p t j", j=2)
 
-        u_slots = [keep.tile([P, HALF, 2], U32, name=f"u_slots{s}", align_bytes=64) for s in range(2)]
+        W = C * 2
+        stage = keep.tile([P, 2 * EARLY + 4 * W], U32, name="stage", align_bytes=64)
 
-        nc.vector.tensor_copy(out=pair_view(0), in_=u_raw[0][:].rearrange("p j t -> p t j"))
-        nc.scalar.copy(out=pair_view(1), in_=u_raw[1][:].rearrange("p j t -> p t j"))
-        for h in range(2):
-            for s in range(2):
-                nc.vector.tensor_copy(
-                    out=u_slots[s][:, :, h],
-                    in_=u_pairs[h][:].indirect(offsets[:, s * (HALF // 16) : (s + 1) * (HALF // 16)]),
-                )
-        for s in range(2):
-            nc.vector.quantize_mx(
-                out=u_codes[:, s * HALF : (s + 1) * HALF].bitcast(FP8X4),
-                scales=u_scales[:, s * HALF : (s + 1) * HALF],
-                in_=u_slots[s][:].rearrange("p c w -> p (c w)").bitcast(BF16),
+        def gather(dst, h, s0, s1):
+            nc.vector.tensor_copy(
+                out=dst.rearrange("p (c w) -> p c w", w=2)[:, :, h],
+                in_=u_pairs[h][:].indirect(offsets[:, s0 // 16 : s1 // 16]),
             )
 
-        wu_bf = [keep.tile([P, PACK, P, PACK], BF16, name=f"wu_bf{a}", tag=f"wu_bf{a}", align_bytes=64) for a in range(PASSES)]
+        slot_codes = {e: u_codes[:, e * C : (e + 1) * C] for e in range(2)}
+
+        def quantise_u(src, codes, s0, s1):
+            nc.vector.quantize_mx(
+                out=codes.bitcast(FP8X4),
+                scales=u_scales[:, s0:s1],
+                in_=src.bitcast(BF16),
+            )
+
+        for h in range(2):
+            src = u_raw[h][:].rearrange("p j t -> p t j")
+            if U_SHARE[h] < T:
+                nc.scalar.copy(out=pair_view(h)[:, U_SHARE[h] :, :], in_=src[:, U_SHARE[h] :, :])
+            nc.vector.tensor_copy(out=pair_view(h)[:, : U_SHARE[h], :], in_=src[:, : U_SHARE[h], :])
+            gather(stage[:, 0 : 2 * EARLY], h, 0, EARLY)
+        quantise_u(stage[:, 0:T], u_codes[:], 0, HALF)
+
+        wu_bf0 = keep.tile([P, 4 * W], U32, name="wu_bf0", align_bytes=64)
+        wu_bf = [
+            words.bitcast(BF16).rearrange("p (r m j) -> p r m j", r=PACK, j=PACK)
+            for words in (wu_bf0[:], stage[:, 2 * EARLY :])
+        ]
         wu_codes = [keep.tile([P, PACK, P], U32, name=f"wu_codes{a}", align_bytes=64) for a in range(PASSES)]
         wu_scales = [keep.tile([P, PACK, P], U8, name=f"wu_scales{a}", align_bytes=64) for a in range(PASSES)]
 
@@ -123,9 +138,11 @@ def tile_moe_prv_lin_silu_kernel(tc, uT, wu, w_words, w_scales, b, gate, offs, o
             )
 
         x_bf = {}
-        for group, tag in zip(GROUPS, ("x_first", "shared1", "shared2")):
-            tile = keep.tile([P, len(group), PASSES, C, PACK], BF16, name=f"x_bf{group[0]}", tag=tag, align_bytes=64)
-            x_bf[group] = tile
+        x_rest = keep.tile([P, 4 * C * PACK], BF16, name="x_rest", tag="shared3", align_bytes=64)
+        for e in (2, 3):
+            for a in range(PASSES):
+                i = (e - 2) * PASSES + a
+                x_bf[e, a] = x_rest[:, i * C * PACK : (i + 1) * C * PACK]
         x_codes = keep.tile([P, E, PASSES, C], U32, name="x_codes", align_bytes=64)
         x_scales = keep.tile([P, E, PASSES, C], U8, name="x_scales", align_bytes=64)
 
@@ -136,21 +153,20 @@ def tile_moe_prv_lin_silu_kernel(tc, uT, wu, w_words, w_scales, b, gate, offs, o
                     out=bank[:, r, :],
                     lhsT=wu_codes[a][:, r, :].bitcast(FP8X4),
                     lhsT_scale=wu_scales[a][:, r, :],
-                    rhs=u_codes[:, e * C : (e + 1) * C].bitcast(FP8X4),
+                    rhs=slot_codes[e].bitcast(FP8X4),
                     rhs_scale=u_scales[:, e * C : (e + 1) * C],
                     start=True,
                     stop=True,
                 )
-            nc.scalar.copy(out=x_bf[group][:, e - group[0], a, :, :], in_=bank[:].rearrange("p r c -> p c r"))
+            nc.scalar.copy(out=x_bf[e, a].rearrange("p (c r) -> p c r", r=PACK), in_=bank[:].rearrange("p r c -> p c r"))
 
-        def quantise_x(group, first, count):
-            w0 = (group[0] * PASSES + first) * C
+        def quantise_x(e, a, count, values):
+            w0 = (e * PASSES + a) * C
             words = slice(w0, w0 + count * C)
-            values = slice(first * C * PACK, (first + count) * C * PACK)
             nc.vector.quantize_mx(
                 out=x_codes[:].rearrange("p e a c -> p (e a c)")[:, words].bitcast(FP8X4),
                 scales=x_scales[:].rearrange("p e a c -> p (e a c)")[:, words],
-                in_=x_bf[group][:].rearrange("p e a c r -> p (e a c r)")[:, values],
+                in_=values,
             )
 
         y = [keep.tile([P, E * C], F32, name=f"y{nt}") for nt in range(N_TILES)]
@@ -177,7 +193,7 @@ def tile_moe_prv_lin_silu_kernel(tc, uT, wu, w_words, w_scales, b, gate, offs, o
 
         def scatter(group, nt):
             if nt not in results:
-                results[nt] = keep.tile([P, T], F32, name=f"results{nt}", tag=f"shared{nt}", align_bytes=64)
+                results[nt] = keep.tile([P, T], F32, name=f"results{nt}", tag=("shared0", "wu_raw1_64", "shared2", "shared3")[nt], align_bytes=64)
             s0, s1 = group[0] * C, (group[-1] + 1) * C
             nc.vector.tensor_tensor(
                 results[nt][:].indirect(offsets[:, s0 // 16 : s1 // 16]),
@@ -189,34 +205,52 @@ def tile_moe_prv_lin_silu_kernel(tc, uT, wu, w_words, w_scales, b, gate, offs, o
         first, second, rest = GROUPS
         for raw, (a, m0, m1, share) in zip(wu_raw, WU_CHUNKS):
             round_wu(raw, a, m0, m1, share)
-            if (a, m0) == (1, 0):
+            if (a, m0) == (0, 64):
                 for r in range(0, PACK, 2):
                     quantise_wu(0, r, r + 2)
+        late = keep.tile([P, 3 * W], U32, name="late", tag="wu_raw1_64", align_bytes=64)
+        x_last = keep.tile([P, W], U32, name="x_last", tag="x_last", align_bytes=64)
+        x_bf[0, 1] = x_last[:].bitcast(BF16)
+        x_bf[0, 0] = late[:, 0:W].bitcast(BF16)
+        x_bf[1, 0] = late[:, W : 2 * W].bitcast(BF16)
+        x_bf[1, 1] = late[:, 2 * W : 3 * W].bitcast(BF16)
         project(first, 0, 0)
-        project(second, 1, 0)
-        for r in range(PACK):
-            quantise_wu(1, r, r + 1)
+        for r0, r1 in ((0, 2), (2, 3), (3, 4)):
+            quantise_wu(1, r0, r1)
         project(first, 0, 1)
+        project(second, 1, 0)
         project(second, 1, 1)
-        quantise_x(first, 0, 1)
-        quantise_x(first, 1, 1)
+        quantise_x(0, 0, 1, x_bf[0, 0])
+        for h in range(2):
+            gather(stage[:, 2 * EARLY : 2 * T], h, EARLY, T)
+        quantise_x(0, 1, 1, x_bf[0, 1])
         for nt in range(N_TILES):
             expert(0, nt)
+        late_codes = keep.tile([P, HALF], U32, name="late_codes", tag="x_last", align_bytes=64)
+        for e in rest:
+            slot_codes[e] = late_codes[:, (e - 2) * C : (e - 1) * C]
+        quantise_u(stage[:, T : 2 * T], late_codes[:], HALF, T)
+        quantise_x(1, 0, PASSES, late[:, W : 3 * W].bitcast(BF16))
         scatter(first, 0)
-        quantise_x(second, 0, PASSES)
         scatter(first, 1)
+        scatter(first, 2)
         for nt in range(2):
             expert(1, nt)
             scatter(second, nt)
         for e in rest:
             for a in range(PASSES):
                 project(rest, e, a)
-        quantise_x(rest, 0, 2 * PASSES)
-        for nt in range(2, N_TILES):
-            expert(1, nt)
-            scatter(first + second, nt)
+        expert(1, 2)
+        scatter(second, 2)
+        quantise_x(2, 0, 2 * PASSES, x_rest[:])
+        expert(1, 3)
+        scatter(first + second, 3)
         for nt in range(N_TILES):
             for e in rest:
                 expert(e, nt)
             scatter(rest, nt)
-            nc.sync.dma_start(out=out[nt * P : (nt + 1) * P, :], in_=results[nt][:])
+            if nt < N_TILES - 1:
+                nc.sync.dma_start(out=out[nt * P : (nt + 1) * P, :], in_=results[nt][:])
+            else:
+                nc.sync.dma_start(out=out[nt * P : (nt + 1) * P, 0:HALF], in_=results[nt][:, 0:HALF])
+                nc.scalar.dma_start(out=out[nt * P : (nt + 1) * P, HALF:T], in_=results[nt][:, HALF:T])

@@ -138,7 +138,7 @@ def tile_moe_prv_lin_silu_kernel(tc, uT, wu, w_words, w_scales, b, gate, offs, o
             )
 
         x_bf = {}
-        x_rest = keep.tile([P, 4 * C * PACK], BF16, name="x_rest", tag="shared3", align_bytes=64)
+        x_rest = keep.tile([P, 4 * C * PACK], BF16, name="x_rest", align_bytes=64)
         for e in (2, 3):
             for a in range(PASSES):
                 i = (e - 2) * PASSES + a
@@ -234,17 +234,18 @@ def tile_moe_prv_lin_silu_kernel(tc, uT, wu, w_words, w_scales, b, gate, offs, o
         scatter(first, 0)
         scatter(first, 1)
         scatter(first, 2)
+        scatter(first, 3)
         for nt in range(2):
             expert(1, nt)
             scatter(second, nt)
         for e in rest:
             for a in range(PASSES):
                 project(rest, e, a)
+            quantise_x(e, 0, PASSES, x_rest[:, (e - 2) * PASSES * C * PACK : (e - 1) * PASSES * C * PACK])
         expert(1, 2)
         scatter(second, 2)
-        quantise_x(2, 0, 2 * PASSES, x_rest[:])
         expert(1, 3)
-        scatter(first + second, 3)
+        scatter(second, 3)
         for nt in range(N_TILES):
             for e in rest:
                 expert(e, nt)

@@ -21,7 +21,7 @@ K_PASS = P * PACK
 PASSES = K // K_PASS
 N_TILES = N // P
 HALF = T // 2
-WU_CHUNKS = ((0, 0, 64, 0), (0, 64, 128, 32), (1, 0, 64, 22), (1, 64, 128, 44))
+WU_CHUNKS = ((0, 0, 64, 0), (0, 64, 128, 32), (1, 0, 64, 22), (1, 64, 96, 20), (1, 96, 128, 22))
 U_SHARE = (336, 160)
 EARLY = 384
 X_BANK = ((0, 2), (1, 3), (4, 5), (6, 7))
@@ -193,7 +193,7 @@ def tile_moe_prv_lin_silu_kernel(tc, uT, wu, w_words, w_scales, b, gate, offs, o
 
         def scatter(group, nt):
             if nt not in results:
-                results[nt] = keep.tile([P, T], F32, name=f"results{nt}", tag=("shared0", "wu_raw1_64", "shared2", "shared3")[nt], align_bytes=64)
+                results[nt] = keep.tile([P, T], F32, name=f"results{nt}", tag=("shared0", "wu_raw1_96", "shared2", "shared3")[nt], align_bytes=64)
             s0, s1 = group[0] * C, (group[-1] + 1) * C
             nc.vector.tensor_tensor(
                 results[nt][:].indirect(offsets[:, s0 // 16 : s1 // 16]),
@@ -208,7 +208,7 @@ def tile_moe_prv_lin_silu_kernel(tc, uT, wu, w_words, w_scales, b, gate, offs, o
             if (a, m0) == (0, 64):
                 for r in range(0, PACK, 2):
                     quantise_wu(0, r, r + 2)
-        late = keep.tile([P, 3 * W], U32, name="late", tag="wu_raw1_64", align_bytes=64)
+        late = keep.tile([P, 3 * W], U32, name="late", tag="wu_raw1_96", align_bytes=64)
         x_last = keep.tile([P, W], U32, name="x_last", tag="x_last", align_bytes=64)
         x_bf[0, 1] = x_last[:].bitcast(BF16)
         x_bf[0, 0] = late[:, 0:W].bitcast(BF16)
@@ -250,8 +250,4 @@ def tile_moe_prv_lin_silu_kernel(tc, uT, wu, w_words, w_scales, b, gate, offs, o
             for e in rest:
                 expert(e, nt)
             scatter(rest, nt)
-            if nt < N_TILES - 1:
-                nc.sync.dma_start(out=out[nt * P : (nt + 1) * P, :], in_=results[nt][:])
-            else:
-                nc.sync.dma_start(out=out[nt * P : (nt + 1) * P, 0:HALF], in_=results[nt][:, 0:HALF])
-                nc.scalar.dma_start(out=out[nt * P : (nt + 1) * P, HALF:T], in_=results[nt][:, HALF:T])
+            nc.sync.dma_start(out=out[nt * P : (nt + 1) * P, :], in_=results[nt][:])

@@ -21,7 +21,7 @@ K_PASS = P * PACK
 PASSES = K // K_PASS
 N_TILES = N // P
 HALF = T // 2
-WU_CHUNKS = ((0, 0, 64, 0), (0, 64, 128, 32), (1, 0, 64, 22), (1, 64, 96, 20), (1, 96, 128, 22))
+WU_CHUNKS = ((0, 0, 64, 0), (0, 64, 128, 24), (1, 0, 64, 18), (1, 64, 96, 20), (1, 96, 128, 22))
 U_SHARE = (336, 160)
 EARLY = 384
 X_BANK = ((0, 2), (1, 3), (4, 5), (6, 7))
@@ -98,6 +98,7 @@ def tile_moe_prv_lin_silu_kernel(tc, uT, wu, w_words, w_scales, b, gate, offs, o
                 in_=u_pairs[h][:].indirect(offsets[:, s0 // 16 : s1 // 16]),
             )
 
+        early_pairs = keep.tile([P, 2 * EARLY], U32, name="early_pairs")
         slot_codes = {e: u_codes[:, e * C : (e + 1) * C] for e in range(2)}
 
         def quantise_u(src, codes, s0, s1):
@@ -112,7 +113,14 @@ def tile_moe_prv_lin_silu_kernel(tc, uT, wu, w_words, w_scales, b, gate, offs, o
             if U_SHARE[h] < T:
                 nc.scalar.copy(out=pair_view(h)[:, U_SHARE[h] :, :], in_=src[:, U_SHARE[h] :, :])
             nc.vector.tensor_copy(out=pair_view(h)[:, : U_SHARE[h], :], in_=src[:, : U_SHARE[h], :])
-            gather(stage[:, 0 : 2 * EARLY], h, 0, EARLY)
+            nc.vector.tensor_copy(
+                out=early_pairs[:, h * EARLY : (h + 1) * EARLY],
+                in_=u_pairs[h][:].indirect(offsets[:, 0 : EARLY // 16]),
+            )
+        nc.vector.tensor_copy(
+            out=stage[:, 0 : 2 * EARLY].bitcast(I32).rearrange("p (c w) -> p c w", w=2),
+            in_=early_pairs[:].bitcast(I32).rearrange("p (w c) -> p c w", w=2),
+        )
         quantise_u(stage[:, 0:T], u_codes[:], 0, HALF)
 
         wu_bf0 = keep.tile([P, 4 * W], U32, name="wu_bf0", align_bytes=64)

@@ -25,7 +25,9 @@ WU_CHUNKS = ((0, 0, 64, 0), (0, 64, 128, 24), (1, 0, 64, 18), (1, 64, 96, 20), (
 U_SHARE = (336, 160)
 EARLY = 384
 X_BANK = ((0, 2), (1, 3), (4, 5), (6, 7))
-Y_BANK = ((4, 5, 6, 7), (0, 1, 2, 3), (4, 6, 0, 2), (5, 7, 1, 3))
+Y_BANK = ((6, 5, 7, 0), (0, 1, 2, 3), (4, 6, 0, 2), (5, 7, 1, 3))
+LEAD = 64
+LEAD_BANK = 4
 GROUPS = ((0,), (1,), (2, 3))
 
 
@@ -50,6 +52,10 @@ def tile_moe_prv_lin_silu_kernel(tc, uT, wu, w_words, w_scales, b, gate, offs, o
 
         for g in range(2):
             nc.vector.memset(w_planes[g][:].bitcast(I32), 0)
+        x_codes = keep.tile([P, LEAD + E * PASSES * C], U32, name="x_codes", align_bytes=64)
+        x_scales = keep.tile([P, LEAD + E * PASSES * C], U8, name="x_scales", align_bytes=64)
+        nc.vector.memset(x_codes[:, 0:LEAD].bitcast(I32), 0)
+        nc.vector.memset(x_scales[:, 0:LEAD].bitcast(I32), 0)
 
         u_rows = uT.rearrange("(p j) t -> p j t", j=PACK)
         wu_rows = wu.rearrange("(p j) k -> p j k", j=PACK)
@@ -151,11 +157,14 @@ def tile_moe_prv_lin_silu_kernel(tc, uT, wu, w_words, w_scales, b, gate, offs, o
             for a in range(PASSES):
                 i = (e - 2) * PASSES + a
                 x_bf[e, a] = x_rest[:, i * C * PACK : (i + 1) * C * PACK]
-        x_codes = keep.tile([P, E, PASSES, C], U32, name="x_codes", align_bytes=64)
-        x_scales = keep.tile([P, E, PASSES, C], U8, name="x_scales", align_bytes=64)
+        banks = [psum.tile([P, PACK, C], F32, name=f"bank{i}") for i in range(8)]
 
-        def project(group, e, a):
-            bank = psum.tile([P, PACK, C], F32, name=f"bank{X_BANK[e][a]}")
+        def x_words(e, a, c0, count):
+            w0 = LEAD + (e * PASSES + a) * C + c0
+            return slice(w0, w0 + count)
+
+        def project(group, e, a, cuts=((0, C),)):
+            bank = banks[X_BANK[e][a]]
             for r in range(PACK):
                 nc.tensor.matmul_mx(
                     out=bank[:, r, :],
@@ -166,43 +175,45 @@ def tile_moe_prv_lin_silu_kernel(tc, uT, wu, w_words, w_scales, b, gate, offs, o
                     start=True,
                     stop=True,
                 )
-            nc.scalar.copy(out=x_bf[e, a].rearrange("p (c r) -> p c r", r=PACK), in_=bank[:].rearrange("p r c -> p c r"))
+            for c0, c1 in cuts:
+                nc.scalar.copy(
+                    out=x_bf[e, a].rearrange("p (c r) -> p c r", r=PACK)[:, c0:c1, :],
+                    in_=bank[:, :, c0:c1].rearrange("p r c -> p c r"),
+                )
 
-        def quantise_x(e, a, count, values):
-            w0 = (e * PASSES + a) * C
-            words = slice(w0, w0 + count * C)
-            nc.vector.quantize_mx(
-                out=x_codes[:].rearrange("p e a c -> p (e a c)")[:, words].bitcast(FP8X4),
-                scales=x_scales[:].rearrange("p e a c -> p (e a c)")[:, words],
-                in_=values,
-            )
+        def quantise_x(e, a, c0, count, values):
+            words = x_words(e, a, c0, count)
+            nc.vector.quantize_mx(out=x_codes[:, words].bitcast(FP8X4), scales=x_scales[:, words], in_=values)
 
         y = [keep.tile([P, E * C], F32, name=f"y{nt}") for nt in range(N_TILES)]
 
-        def expert(e, nt):
+        def expert(e, nt, c0=0, c1=C, shift=0, bank_number=None):
             cols = slice(nt * P, (nt + 1) * P)
-            bank = psum.tile([P, C], F32, name=f"bank{Y_BANK[e][nt]}")
+            bank = banks[Y_BANK[e][nt] if bank_number is None else bank_number][:, 0, :]
             for a in range(PASSES):
                 g, j = divmod(e * PASSES + a, 4)
                 nc.tensor.matmul_mx(
-                    out=bank[:],
+                    out=bank,
                     lhsT=w_codes[e][:, a, cols].bitcast(FP8X4),
                     lhsT_scale=w_planes[g][4 * j : P, cols],
-                    rhs=x_codes[:, e, a, :].bitcast(FP8X4),
-                    rhs_scale=x_scales[:, e, a, :],
+                    rhs=x_codes[:, x_words(e, a, -shift, C)].bitcast(FP8X4),
+                    rhs_scale=x_scales[:, x_words(e, a, -shift, C)],
                     start=(a == 0),
                     stop=(a == PASSES - 1),
                 )
             nc.scalar.activation(
-                out=y[nt][:, e * C : (e + 1) * C], in_=bank[:], func=SILU, bias=bias[:, nt, e : e + 1]
+                out=y[nt][:, e * C + c0 : e * C + c1],
+                in_=bank[:, shift + c0 : shift + c1],
+                func=SILU,
+                bias=bias[:, nt, e : e + 1],
             )
 
         results = {}
 
-        def scatter(group, nt):
+        def scatter(group, nt, part=None):
             if nt not in results:
                 results[nt] = keep.tile([P, T], F32, name=f"results{nt}", tag=("shared0", "wu_raw1_96", "shared2", "shared3")[nt], align_bytes=64)
-            s0, s1 = group[0] * C, (group[-1] + 1) * C
+            s0, s1 = (group[0] * C, (group[-1] + 1) * C) if part is None else part
             nc.vector.tensor_tensor(
                 results[nt][:].indirect(offsets[:, s0 // 16 : s1 // 16]),
                 y[nt][:, s0:s1],
@@ -225,22 +236,28 @@ def tile_moe_prv_lin_silu_kernel(tc, uT, wu, w_words, w_scales, b, gate, offs, o
         project(first, 0, 0)
         for r0, r1 in ((0, 2), (2, 3), (3, 4)):
             quantise_wu(1, r0, r1)
-        project(first, 0, 1)
+        project(first, 0, 1, ((0, LEAD), (LEAD, C)))
         project(second, 1, 0)
         project(second, 1, 1)
-        quantise_x(0, 0, 1, x_bf[0, 0])
+        quantise_x(0, 0, 0, C, x_bf[0, 0])
         for h in range(2):
             gather(stage[:, 2 * EARLY : 2 * T], h, EARLY, T)
-        quantise_x(0, 1, 1, x_bf[0, 1])
-        for nt in range(N_TILES):
-            expert(0, nt)
+        quantise_x(0, 1, 0, LEAD, x_bf[0, 1][:, 0 : LEAD * PACK])
+        expert(0, 0, 0, LEAD, C - LEAD, LEAD_BANK)
+        quantise_x(0, 1, LEAD, C - LEAD, x_bf[0, 1][:, LEAD * PACK :])
+        quantise_x(1, 0, 0, C, x_bf[1, 0])
+        expert(0, 1)
+        expert(0, 0, LEAD, C)
+        expert(0, 2)
+        expert(0, 3)
         late_codes = keep.tile([P, HALF], U32, name="late_codes", tag="x_last", align_bytes=64)
         for e in rest:
             slot_codes[e] = late_codes[:, (e - 2) * C : (e - 1) * C]
         quantise_u(stage[:, T : 2 * T], late_codes[:], HALF, T)
-        quantise_x(1, 0, PASSES, late[:, W : 3 * W].bitcast(BF16))
-        scatter(first, 0)
+        quantise_x(1, 1, 0, C, x_bf[1, 1])
+        scatter(first, 0, (0, LEAD))
         scatter(first, 1)
+        scatter(first, 0, (LEAD, C))
         scatter(first, 2)
         scatter(first, 3)
         for nt in range(2):
@@ -249,7 +266,7 @@ def tile_moe_prv_lin_silu_kernel(tc, uT, wu, w_words, w_scales, b, gate, offs, o
         for e in rest:
             for a in range(PASSES):
                 project(rest, e, a)
-            quantise_x(e, 0, PASSES, x_rest[:, (e - 2) * PASSES * C * PACK : (e - 1) * PASSES * C * PACK])
+            quantise_x(e, 0, 0, PASSES * C, x_rest[:, (e - 2) * PASSES * C * PACK : (e - 1) * PASSES * C * PACK])
         expert(1, 2)
         scatter(second, 2)
         expert(1, 3)

@@ -74,6 +74,7 @@ def tile_moe_prv_lin_silu_kernel(tc, uT, wu, w_words, w_scales, b, gate, offs, o
                     in_=scale_rows[4 * g : 4 * g + 4, 4 * q : 4 * q + 4, :].bitcast(I32),
                 )
 
+        nc.gpsimd.dma_start(out=bias[:], in_=b.rearrange("(nt p) e -> p nt e", p=P))
         nc.sync.dma_start(out=u_raw[0][:], in_=u_rows[:, 0:2, :])
         nc.sync.dma_start(offsets[:], offs)
         nc.sync.dma_start(out=u_raw[1][:], in_=u_rows[:, 2:4, :])
@@ -81,9 +82,9 @@ def tile_moe_prv_lin_silu_kernel(tc, uT, wu, w_words, w_scales, b, gate, offs, o
             nc.sync.dma_start(out=raw[:], in_=wu_rows[:, :, a * K_PASS + PACK * m0 : a * K_PASS + PACK * m1])
         load_codes(0)
         load_planes(0)
-        nc.sync.dma_start(out=bias[:], in_=b.rearrange("(nt p) e -> p nt e", p=P))
-        nc.sync.dma_start(out=gates[:], in_=gate[0:P, :])
+        nc.sync.dma_start(out=gates[:, 0:C], in_=gate[0:P, 0:C])
         load_codes(1)
+        nc.sync.dma_start(out=gates[:, C:T], in_=gate[0:P, C:T])
         load_planes(1)
         load_codes(2)
         load_codes(3)

@@ -74,7 +74,7 @@ def tile_moe_prv_lin_silu_kernel(tc, uT, wu, w_words, w_scales, b, gate, offs, o
                     in_=scale_rows[4 * g : 4 * g + 4, 4 * q : 4 * q + 4, :].bitcast(I32),
                 )
 
-        nc.gpsimd.dma_start(out=bias[:], in_=b.rearrange("(nt p) e -> p nt e", p=P))
+        nc.scalar.dma_start(out=bias[:], in_=b.rearrange("(nt p) e -> p nt e", p=P))
         nc.sync.dma_start(out=u_raw[0][:], in_=u_rows[:, 0:2, :])
         nc.sync.dma_start(offsets[:], offs)
         nc.sync.dma_start(out=u_raw[1][:], in_=u_rows[:, 2:4, :])

@@ -1,6 +1,7 @@
 from contextlib import ExitStack
 
 import concourse.mybir as mybir
+from concourse.masks import make_identity
 
 F, K, T, E, C, N = 512, 1024, 512, 4, 128, 512
 FLOPS = 2 * F * K * T + 2 * K * N * E * C
@@ -28,6 +29,7 @@ X_BANK = ((0, 2), (1, 3), (4, 5), (6, 7))
 Y_BANK = ((6, 5, 7, 0), (0, 1, 2, 3), (4, 6, 0, 2), (5, 7, 1, 3))
 LEAD = 64
 LEAD_BANK = 4
+BIAS_BANK = 7
 GROUPS = ((0,), (1,), (2, 3))
 
 
@@ -38,18 +40,23 @@ def tile_moe_prv_lin_silu_kernel(tc, uT, wu, w_words, w_scales, b, gate, offs, o
         psum = ctx.enter_context(tc.psum_pool(name="psum", bufs=1))
 
         offsets = keep.tile([P, T // 16], U16, name="offsets")
-        u_raw = [keep.tile([P, 2, T], F32, name=f"u_raw{h}") for h in range(2)]
+        u_raw = [keep.tile([P, 2, T], F32, name=f"u_raw{h}", tag=f"u_raw{h}") for h in range(2)]
         wu_raw = [keep.tile([P, PACK, PACK * (m1 - m0)], F32, name=f"wu_raw{a}_{m0}", tag=f"wu_raw{a}_{m0}", align_bytes=64) for a, m0, m1, share in WU_CHUNKS]
-        bias = keep.tile([P, N_TILES, E], F32, name="bias")
+        bias_rows = keep.tile([P, P * E], F32, name="bias_rows")
+        identity = keep.tile([P, P], F32, name="identity")
+        banks = [psum.tile([P, PACK, C], F32, name=f"bank{i}") for i in range(8)]
         w_codes = [keep.tile([P, PASSES, N], U32, name=f"w_codes{e}", align_bytes=64) for e in range(E)]
         w_planes = [keep.tile([P, N], U8, name=f"w_planes{g}", align_bytes=64) for g in range(2)]
         gates = keep.tile([P, T], F32, name="gates")
 
+        nc.scalar.dma_start(out=bias_rows[P - N_TILES : P, :], in_=b.rearrange("(nt p) e -> nt (p e)", p=P))
         warm_in = keep.tile([P, 1], F32, name="warm_in")
         warm_out = keep.tile([P, 1], F32, name="warm_out")
         nc.vector.memset(warm_in[:], 0.0)
         nc.scalar.activation(out=warm_out[:], in_=warm_in[:], func=SILU)
+        nc.vector.memset(bias_rows[0 : P - N_TILES, :].bitcast(I32), 0)
 
+        make_identity(nc, identity[:])
         for g in range(2):
             nc.vector.memset(w_planes[g][:].bitcast(I32), 0)
         x_codes = keep.tile([P, LEAD + E * PASSES * C], U32, name="x_codes", align_bytes=64)
@@ -74,7 +81,8 @@ def tile_moe_prv_lin_silu_kernel(tc, uT, wu, w_words, w_scales, b, gate, offs, o
                     in_=scale_rows[4 * g : 4 * g + 4, 4 * q : 4 * q + 4, :].bitcast(I32),
                 )
 
-        nc.scalar.dma_start(out=bias[:], in_=b.rearrange("(nt p) e -> p nt e", p=P))
+        for e in range(E):
+            nc.tensor.transpose(banks[BIAS_BANK][:, e, :], bias_rows[:].rearrange("q (p e) -> q e p", e=E)[:, e, :], identity[:])
         nc.sync.dma_start(out=u_raw[0][:], in_=u_rows[:, 0:2, :])
         nc.sync.dma_start(offsets[:], offs)
         nc.sync.dma_start(out=u_raw[1][:], in_=u_rows[:, 2:4, :])
@@ -120,14 +128,18 @@ def tile_moe_prv_lin_silu_kernel(tc, uT, wu, w_words, w_scales, b, gate, offs, o
             if U_SHARE[h] < T:
                 nc.scalar.copy(out=pair_view(h)[:, U_SHARE[h] :, :], in_=src[:, U_SHARE[h] :, :])
             nc.vector.tensor_copy(out=pair_view(h)[:, : U_SHARE[h], :], in_=src[:, : U_SHARE[h], :])
+            for s0, s1 in (((0, EARLY),), ((0, HALF), (HALF, EARLY)))[h]:
+                nc.vector.tensor_copy(
+                    out=early_pairs[:, h * EARLY + s0 : h * EARLY + s1],
+                    in_=u_pairs[h][:].indirect(offsets[:, s0 // 16 : s1 // 16]),
+                )
+        bias = keep.tile([P, E, N_TILES], F32, name="bias", tag="u_raw1")
+        nc.vector.tensor_copy(out=bias[:], in_=banks[BIAS_BANK][:, :, P - N_TILES : P])
+        for s0, s1 in ((0, HALF), (HALF, EARLY)):
             nc.vector.tensor_copy(
-                out=early_pairs[:, h * EARLY : (h + 1) * EARLY],
-                in_=u_pairs[h][:].indirect(offsets[:, 0 : EARLY // 16]),
+                out=stage[:, 2 * s0 : 2 * s1].bitcast(I32).rearrange("p (c w) -> p c w", w=2),
+                in_=early_pairs[:].bitcast(I32).rearrange("p (w c) -> p c w", w=2)[:, s0:s1, :],
             )
-        nc.vector.tensor_copy(
-            out=stage[:, 0 : 2 * EARLY].bitcast(I32).rearrange("p (c w) -> p c w", w=2),
-            in_=early_pairs[:].bitcast(I32).rearrange("p (w c) -> p c w", w=2),
-        )
         quantise_u(stage[:, 0:T], u_codes[:], 0, HALF)
 
         wu_bf0 = keep.tile([P, 4 * W], U32, name="wu_bf0", align_bytes=64)
@@ -145,6 +157,12 @@ def tile_moe_prv_lin_silu_kernel(tc, uT, wu, w_words, w_scales, b, gate, offs, o
             if share:
                 nc.vector.tensor_copy(out=dst[:, :share, :, :], in_=src[:, :share, :, :])
 
+        def round_last(raw, a, m0, m1):
+            dst = wu_bf[a][:, :, m0:m1, :].rearrange("p r m j -> p m j r")
+            src = raw[:].rearrange("p j (m r) -> p m j r", r=PACK)
+            nc.scalar.copy(out=dst[:, :, :, 0:1], in_=src[:, :, :, 0:1])
+            nc.vector.tensor_copy(out=dst[:, :, :, 1:PACK], in_=src[:, :, :, 1:PACK])
+
         def quantise_wu(a, r0, r1):
             nc.vector.quantize_mx(
                 out=wu_codes[a][:, r0:r1, :].rearrange("p r m -> p (r m)").bitcast(FP8X4),
@@ -158,7 +176,6 @@ def tile_moe_prv_lin_silu_kernel(tc, uT, wu, w_words, w_scales, b, gate, offs, o
             for a in range(PASSES):
                 i = (e - 2) * PASSES + a
                 x_bf[e, a] = x_rest[:, i * C * PACK : (i + 1) * C * PACK]
-        banks = [psum.tile([P, PACK, C], F32, name=f"bank{i}") for i in range(8)]
 
         def x_words(e, a, c0, count):
             w0 = LEAD + (e * PASSES + a) * C + c0
@@ -206,7 +223,7 @@ def tile_moe_prv_lin_silu_kernel(tc, uT, wu, w_words, w_scales, b, gate, offs, o
                 out=y[nt][:, e * C + c0 : e * C + c1],
                 in_=bank[:, shift + c0 : shift + c1],
                 func=SILU,
-                bias=bias[:, nt, e : e + 1],
+                bias=bias[:, e, nt : nt + 1],
             )
 
         results = {}
@@ -224,7 +241,10 @@ def tile_moe_prv_lin_silu_kernel(tc, uT, wu, w_words, w_scales, b, gate, offs, o
 
         first, second, rest = GROUPS
         for raw, (a, m0, m1, share) in zip(wu_raw, WU_CHUNKS):
-            round_wu(raw, a, m0, m1, share)
+            if m0 == 96:
+                round_last(raw, a, m0, m1)
+            else:
+                round_wu(raw, a, m0, m1, share)
             if (a, m0) == (0, 64):
                 for r in range(0, PACK, 2):
                     quantise_wu(0, r, r + 2)
@@ -235,7 +255,7 @@ def tile_moe_prv_lin_silu_kernel(tc, uT, wu, w_words, w_scales, b, gate, offs, o
         x_bf[1, 0] = late[:, W : 2 * W].bitcast(BF16)
         x_bf[1, 1] = late[:, 2 * W : 3 * W].bitcast(BF16)
         project(first, 0, 0)
-        for r0, r1 in ((0, 2), (2, 3), (3, 4)):
+        for r0, r1 in ((0, 1), (1, 3), (3, 4)):
             quantise_wu(1, r0, r1)
         project(first, 0, 1, ((0, LEAD), (LEAD, C)))
         project(second, 1, 0)

@@ -163,11 +163,11 @@ def tile_moe_prv_lin_silu_kernel(tc, uT, wu, w_words, w_scales, b, gate, offs, o
             nc.scalar.copy(out=dst[:, :, :, 0:1], in_=src[:, :, :, 0:1])
             nc.vector.tensor_copy(out=dst[:, :, :, 1:PACK], in_=src[:, :, :, 1:PACK])
 
-        def quantise_wu(a, r0, r1):
+        def quantise_wu(a, r0, r1, m0=0, m1=P):
             nc.vector.quantize_mx(
-                out=wu_codes[a][:, r0:r1, :].rearrange("p r m -> p (r m)").bitcast(FP8X4),
-                scales=wu_scales[a][:, r0:r1, :].rearrange("p r m -> p (r m)"),
-                in_=wu_bf[a][:, r0:r1, :, :].rearrange("p r m j -> p (r m j)"),
+                out=wu_codes[a][:, r0:r1, m0:m1].rearrange("p r m -> p (r m)").bitcast(FP8X4),
+                scales=wu_scales[a][:, r0:r1, m0:m1].rearrange("p r m -> p (r m)"),
+                in_=wu_bf[a][:, r0:r1, m0:m1, :].rearrange("p r m j -> p (r m j)"),
             )
 
         x_bf = {}
@@ -248,6 +248,9 @@ def tile_moe_prv_lin_silu_kernel(tc, uT, wu, w_words, w_scales, b, gate, offs, o
             if (a, m0) == (0, 64):
                 for r in range(0, PACK, 2):
                     quantise_wu(0, r, r + 2)
+            if (a, m0) == (1, 0):
+                for r in range(PACK):
+                    quantise_wu(1, r, r + 1, 0, 64)
         late = keep.tile([P, 3 * W], U32, name="late", tag="wu_raw1_96", align_bytes=64)
         x_last = keep.tile([P, W], U32, name="x_last", tag="x_last", align_bytes=64)
         x_bf[0, 1] = x_last[:].bitcast(BF16)
@@ -255,10 +258,10 @@ def tile_moe_prv_lin_silu_kernel(tc, uT, wu, w_words, w_scales, b, gate, offs, o
         x_bf[1, 0] = late[:, W : 2 * W].bitcast(BF16)
         x_bf[1, 1] = late[:, 2 * W : 3 * W].bitcast(BF16)
         project(first, 0, 0)
-        for r0, r1 in ((0, 1), (1, 3), (3, 4)):
-            quantise_wu(1, r0, r1)
-        project(first, 0, 1, ((0, LEAD), (LEAD, C)))
         project(second, 1, 0)
+        for r in range(PACK):
+            quantise_wu(1, r, r + 1, 64, P)
+        project(first, 0, 1, ((0, LEAD), (LEAD, C)))
         project(second, 1, 1)
         quantise_x(0, 0, 0, C, x_bf[0, 0])
         for h in range(2):

@@ -21,16 +21,24 @@ PACK = 4
 K_PASS = P * PACK
 PASSES = K // K_PASS
 N_TILES = N // P
-HALF = T // 2
-WU_CHUNKS = ((0, 0, 64, 0), (0, 64, 128, 24), (1, 0, 64, 18), (1, 64, 96, 20), (1, 96, 128, 22))
-U_SHARE = (336, 160)
-EARLY = 384
-X_BANK = ((0, 2), (1, 3), (4, 5), (6, 7))
-Y_BANK = ((6, 5, 7, 0), (0, 1, 2, 3), (4, 6, 0, 2), (5, 7, 1, 3))
+BANKS = 8
+PER_COLUMN = 16
+PLANES_A_TILE = 4
+PAIR_SLOTS = 2 * C
+EARLY = 3 * C
 LEAD = 64
-LEAD_BANK = 4
-BIAS_BANK = 7
-GROUPS = ((0,), (1,), (2, 3))
+X_WORDS = C * PACK // 2
+
+U_SHARE = (336, 160)
+WU_SHARE = 24
+
+WU_LOADS = ((0, 0, P // 2), (0, P // 2, P), (1, 0, P // 2), (1, P // 2, 3 * P // 4), (1, 3 * P // 4, P))
+
+BIAS_BANK = BANKS - 1
+
+
+def x_bank(e, a):
+    return 2 * a + e if e < 2 else 2 * e + a
 
 
 def tile_moe_prv_lin_silu_kernel(tc, uT, wu, w_words, w_scales, b, gate, offs, out):
@@ -39,23 +47,27 @@ def tile_moe_prv_lin_silu_kernel(tc, uT, wu, w_words, w_scales, b, gate, offs, o
         keep = ctx.enter_context(tc.tile_pool(name="keep", bufs=1))
         psum = ctx.enter_context(tc.psum_pool(name="psum", bufs=1))
 
-        offsets = keep.tile([P, T // 16], U16, name="offsets")
+        offsets = keep.tile([P, T // PER_COLUMN], U16, name="offsets")
         u_raw = [keep.tile([P, 2, T], F32, name=f"u_raw{h}", tag=f"u_raw{h}") for h in range(2)]
-        wu_raw = [keep.tile([P, PACK, PACK * (m1 - m0)], F32, name=f"wu_raw{a}_{m0}", tag=f"wu_raw{a}_{m0}", align_bytes=64) for a, m0, m1, share in WU_CHUNKS]
+        wu_raw = [
+            keep.tile([P, PACK, PACK * (m1 - m0)], F32, name=f"wu_raw{i}", tag=f"wu_raw{i}", align_bytes=64)
+            for i, (a, m0, m1) in enumerate(WU_LOADS)
+        ]
         bias_rows = keep.tile([P, P * E], F32, name="bias_rows")
         identity = keep.tile([P, P], F32, name="identity")
-        banks = [psum.tile([P, PACK, C], F32, name=f"bank{i}") for i in range(8)]
+        banks = [psum.tile([P, PACK, C], F32, name=f"bank{i}") for i in range(BANKS)]
         w_codes = [keep.tile([P, PASSES, N], U32, name=f"w_codes{e}", align_bytes=64) for e in range(E)]
         w_planes = [keep.tile([P, N], U8, name=f"w_planes{g}", align_bytes=64) for g in range(2)]
         gates = keep.tile([P, T], F32, name="gates")
 
         nc.scalar.dma_start(out=bias_rows[P - N_TILES : P, :], in_=b.rearrange("(nt p) e -> nt (p e)", p=P))
+
         warm_in = keep.tile([P, 1], F32, name="warm_in")
         warm_out = keep.tile([P, 1], F32, name="warm_out")
         nc.vector.memset(warm_in[:], 0.0)
         nc.scalar.activation(out=warm_out[:], in_=warm_in[:], func=SILU)
-        nc.vector.memset(bias_rows[0 : P - N_TILES, :].bitcast(I32), 0)
 
+        nc.vector.memset(bias_rows[0 : P - N_TILES, :].bitcast(I32), 0)
         make_identity(nc, identity[:])
         for g in range(2):
             nc.vector.memset(w_planes[g][:].bitcast(I32), 0)
@@ -75,18 +87,19 @@ def tile_moe_prv_lin_silu_kernel(tc, uT, wu, w_words, w_scales, b, gate, offs, o
             )
 
         def load_planes(g):
-            for q in range(4):
+            for quadrant in range(4):
                 nc.sync.dma_start(
-                    out=w_planes[g][32 * q : 32 * q + 16, :].bitcast(I32),
-                    in_=scale_rows[4 * g : 4 * g + 4, 4 * q : 4 * q + 4, :].bitcast(I32),
+                    out=w_planes[g][32 * quadrant : 32 * quadrant + 4 * PLANES_A_TILE, :].bitcast(I32),
+                    in_=scale_rows[PLANES_A_TILE * g : PLANES_A_TILE * (g + 1), 4 * quadrant : 4 * quadrant + 4, :].bitcast(I32),
                 )
 
         for e in range(E):
             nc.tensor.transpose(banks[BIAS_BANK][:, e, :], bias_rows[:].rearrange("q (p e) -> q e p", e=E)[:, e, :], identity[:])
+
         nc.sync.dma_start(out=u_raw[0][:], in_=u_rows[:, 0:2, :])
         nc.sync.dma_start(offsets[:], offs)
         nc.sync.dma_start(out=u_raw[1][:], in_=u_rows[:, 2:4, :])
-        for raw, (a, m0, m1, share) in zip(wu_raw, WU_CHUNKS):
+        for raw, (a, m0, m1) in zip(wu_raw, WU_LOADS):
             nc.sync.dma_start(out=raw[:], in_=wu_rows[:, :, a * K_PASS + PACK * m0 : a * K_PASS + PACK * m1])
         load_codes(0)
         load_planes(0)
@@ -98,51 +111,36 @@ def tile_moe_prv_lin_silu_kernel(tc, uT, wu, w_words, w_scales, b, gate, offs, o
         load_codes(3)
 
         u_pairs = [keep.tile([P, T], U32, name=f"u_pairs{h}") for h in range(2)]
-        u_codes = keep.tile([P, HALF], U32, name="u_codes", align_bytes=64)
+        u_codes = keep.tile([P, PAIR_SLOTS], U32, name="u_codes", align_bytes=64)
         u_scales = keep.tile([P, T], U8, name="u_scales", align_bytes=64)
-
-        def pair_view(h):
-            return u_pairs[h][:].bitcast(BF16).rearrange("p (t j) -> p t j", j=2)
-
-        W = C * 2
-        stage = keep.tile([P, 2 * EARLY + 4 * W], U32, name="stage", align_bytes=64)
-
-        def gather(dst, h, s0, s1):
-            nc.vector.tensor_copy(
-                out=dst.rearrange("p (c w) -> p c w", w=2)[:, :, h],
-                in_=u_pairs[h][:].indirect(offsets[:, s0 // 16 : s1 // 16]),
-            )
-
+        stage = keep.tile([P, 2 * EARLY + PACK * X_WORDS], U32, name="stage", align_bytes=64)
         early_pairs = keep.tile([P, 2 * EARLY], U32, name="early_pairs")
         slot_codes = {e: u_codes[:, e * C : (e + 1) * C] for e in range(2)}
 
-        def quantise_u(src, codes, s0, s1):
-            nc.vector.quantize_mx(
-                out=codes.bitcast(FP8X4),
-                scales=u_scales[:, s0:s1],
-                in_=src.bitcast(BF16),
-            )
+        def listed(window, s0, s1):
+            return window[:].indirect(offsets[:, s0 // PER_COLUMN : s1 // PER_COLUMN])
 
-        for h in range(2):
+        def quantise_u(words, codes, s0, s1):
+            nc.vector.quantize_mx(out=codes.bitcast(FP8X4), scales=u_scales[:, s0:s1], in_=words.bitcast(BF16))
+
+        parts = ((0, PAIR_SLOTS), (PAIR_SLOTS, EARLY))
+        for h, gathers in enumerate((((0, EARLY),), parts)):
             src = u_raw[h][:].rearrange("p j t -> p t j")
-            if U_SHARE[h] < T:
-                nc.scalar.copy(out=pair_view(h)[:, U_SHARE[h] :, :], in_=src[:, U_SHARE[h] :, :])
-            nc.vector.tensor_copy(out=pair_view(h)[:, : U_SHARE[h], :], in_=src[:, : U_SHARE[h], :])
-            for s0, s1 in (((0, EARLY),), ((0, HALF), (HALF, EARLY)))[h]:
-                nc.vector.tensor_copy(
-                    out=early_pairs[:, h * EARLY + s0 : h * EARLY + s1],
-                    in_=u_pairs[h][:].indirect(offsets[:, s0 // 16 : s1 // 16]),
-                )
+            dst = u_pairs[h][:].bitcast(BF16).rearrange("p (t j) -> p t j", j=2)
+            nc.scalar.copy(out=dst[:, U_SHARE[h] :, :], in_=src[:, U_SHARE[h] :, :])
+            nc.vector.tensor_copy(out=dst[:, : U_SHARE[h], :], in_=src[:, : U_SHARE[h], :])
+            for s0, s1 in gathers:
+                nc.vector.tensor_copy(out=early_pairs[:, h * EARLY + s0 : h * EARLY + s1], in_=listed(u_pairs[h], s0, s1))
         bias = keep.tile([P, E, N_TILES], F32, name="bias", tag="u_raw1")
         nc.vector.tensor_copy(out=bias[:], in_=banks[BIAS_BANK][:, :, P - N_TILES : P])
-        for s0, s1 in ((0, HALF), (HALF, EARLY)):
+        for s0, s1 in parts:
             nc.vector.tensor_copy(
-                out=stage[:, 2 * s0 : 2 * s1].bitcast(I32).rearrange("p (c w) -> p c w", w=2),
-                in_=early_pairs[:].bitcast(I32).rearrange("p (w c) -> p c w", w=2)[:, s0:s1, :],
+                out=stage[:, 2 * s0 : 2 * s1].bitcast(I32).rearrange("p (c h) -> p c h", h=2),
+                in_=early_pairs[:].bitcast(I32).rearrange("p (h c) -> p c h", h=2)[:, s0:s1, :],
             )
-        quantise_u(stage[:, 0:T], u_codes[:], 0, HALF)
+        quantise_u(stage[:, 0 : 2 * PAIR_SLOTS], u_codes[:], 0, PAIR_SLOTS)
 
-        wu_bf0 = keep.tile([P, 4 * W], U32, name="wu_bf0", align_bytes=64)
+        wu_bf0 = keep.tile([P, PACK * X_WORDS], U32, name="wu_bf0", align_bytes=64)
         wu_bf = [
             words.bitcast(BF16).rearrange("p (r m j) -> p r m j", r=PACK, j=PACK)
             for words in (wu_bf0[:], stage[:, 2 * EARLY :])
@@ -150,20 +148,26 @@ def tile_moe_prv_lin_silu_kernel(tc, uT, wu, w_words, w_scales, b, gate, offs, o
         wu_codes = [keep.tile([P, PACK, P], U32, name=f"wu_codes{a}", align_bytes=64) for a in range(PASSES)]
         wu_scales = [keep.tile([P, PACK, P], U8, name=f"wu_scales{a}", align_bytes=64) for a in range(PASSES)]
 
-        def round_wu(raw, a, m0, m1, share):
+        def wu_views(i):
+            a, m0, m1 = WU_LOADS[i]
             dst = wu_bf[a][:, :, m0:m1, :].rearrange("p r m j -> p m j r")
-            src = raw[:].rearrange("p j (m r) -> p m j r", r=PACK)
-            nc.scalar.copy(out=dst[:, share:, :, :], in_=src[:, share:, :, :])
-            if share:
-                nc.vector.tensor_copy(out=dst[:, :share, :, :], in_=src[:, :share, :, :])
+            return dst, wu_raw[i][:].rearrange("p j (m r) -> p m j r", r=PACK)
 
-        def round_last(raw, a, m0, m1):
-            dst = wu_bf[a][:, :, m0:m1, :].rearrange("p r m j -> p m j r")
-            src = raw[:].rearrange("p j (m r) -> p m j r", r=PACK)
-            nc.scalar.copy(out=dst[:, :, :, 0:1], in_=src[:, :, :, 0:1])
-            nc.vector.tensor_copy(out=dst[:, :, :, 1:PACK], in_=src[:, :, :, 1:PACK])
+        def round_on_scalar(i):
+            dst, src = wu_views(i)
+            nc.scalar.copy(out=dst, in_=src)
 
-        def quantise_wu(a, r0, r1, m0=0, m1=P):
+        def round_on_both(i):
+            dst, src = wu_views(i)
+            nc.scalar.copy(out=dst[:, WU_SHARE:, :, :], in_=src[:, WU_SHARE:, :, :])
+            nc.vector.tensor_copy(out=dst[:, :WU_SHARE, :, :], in_=src[:, :WU_SHARE, :, :])
+
+        def round_on_vector(i):
+            dst, src = wu_views(i)
+            for r in range(0, PACK, 2):
+                nc.vector.tensor_copy(out=dst[:, :, :, r : r + 2], in_=src[:, :, :, r : r + 2])
+
+        def quantise_wu(a, r0, r1, m0, m1):
             nc.vector.quantize_mx(
                 out=wu_codes[a][:, r0:r1, m0:m1].rearrange("p r m -> p (r m)").bitcast(FP8X4),
                 scales=wu_scales[a][:, r0:r1, m0:m1].rearrange("p r m -> p (r m)"),
@@ -171,18 +175,18 @@ def tile_moe_prv_lin_silu_kernel(tc, uT, wu, w_words, w_scales, b, gate, offs, o
             )
 
         x_bf = {}
-        x_rest = keep.tile([P, 4 * C * PACK], BF16, name="x_rest", align_bytes=64)
+        x_bf23 = keep.tile([P, 2 * PASSES * C * PACK], BF16, name="x_bf23", align_bytes=64)
         for e in (2, 3):
             for a in range(PASSES):
                 i = (e - 2) * PASSES + a
-                x_bf[e, a] = x_rest[:, i * C * PACK : (i + 1) * C * PACK]
+                x_bf[e, a] = x_bf23[:, i * C * PACK : (i + 1) * C * PACK]
 
-        def x_words(e, a, c0, count):
-            w0 = LEAD + (e * PASSES + a) * C + c0
-            return slice(w0, w0 + count)
+        def x_columns(e, a, c0, count):
+            first = LEAD + (e * PASSES + a) * C + c0
+            return slice(first, first + count)
 
-        def project(group, e, a, cuts=((0, C),)):
-            bank = banks[X_BANK[e][a]]
+        def project(e, a, cuts=((0, C),)):
+            bank = banks[x_bank(e, a)]
             for r in range(PACK):
                 nc.tensor.matmul_mx(
                     out=bank[:, r, :],
@@ -200,103 +204,95 @@ def tile_moe_prv_lin_silu_kernel(tc, uT, wu, w_words, w_scales, b, gate, offs, o
                 )
 
         def quantise_x(e, a, c0, count, values):
-            words = x_words(e, a, c0, count)
-            nc.vector.quantize_mx(out=x_codes[:, words].bitcast(FP8X4), scales=x_scales[:, words], in_=values)
+            columns = x_columns(e, a, c0, count)
+            nc.vector.quantize_mx(out=x_codes[:, columns].bitcast(FP8X4), scales=x_scales[:, columns], in_=values)
 
         y = [keep.tile([P, E * C], F32, name=f"y{nt}") for nt in range(N_TILES)]
 
-        def expert(e, nt, c0=0, c1=C, shift=0, bank_number=None):
+        def expert(e, nt, bank_number, c0=0, c1=C, shift=0):
             cols = slice(nt * P, (nt + 1) * P)
-            bank = banks[Y_BANK[e][nt] if bank_number is None else bank_number][:, 0, :]
+            sums = banks[bank_number][:, 0, :]
             for a in range(PASSES):
-                g, j = divmod(e * PASSES + a, 4)
+                g, i = divmod(e * PASSES + a, PLANES_A_TILE)
                 nc.tensor.matmul_mx(
-                    out=bank,
+                    out=sums,
                     lhsT=w_codes[e][:, a, cols].bitcast(FP8X4),
-                    lhsT_scale=w_planes[g][4 * j : P, cols],
-                    rhs=x_codes[:, x_words(e, a, -shift, C)].bitcast(FP8X4),
-                    rhs_scale=x_scales[:, x_words(e, a, -shift, C)],
+                    lhsT_scale=w_planes[g][4 * i : P, cols],
+                    rhs=x_codes[:, x_columns(e, a, -shift, C)].bitcast(FP8X4),
+                    rhs_scale=x_scales[:, x_columns(e, a, -shift, C)],
                     start=(a == 0),
                     stop=(a == PASSES - 1),
                 )
             nc.scalar.activation(
                 out=y[nt][:, e * C + c0 : e * C + c1],
-                in_=bank[:, shift + c0 : shift + c1],
+                in_=sums[:, shift + c0 : shift + c1],
                 func=SILU,
                 bias=bias[:, e, nt : nt + 1],
             )
 
         results = {}
 
-        def scatter(group, nt, part=None):
-            if nt not in results:
-                results[nt] = keep.tile([P, T], F32, name=f"results{nt}", tag=("shared0", "wu_raw1_96", "shared2", "shared3")[nt], align_bytes=64)
-            s0, s1 = (group[0] * C, (group[-1] + 1) * C) if part is None else part
-            nc.vector.tensor_tensor(
-                results[nt][:].indirect(offsets[:, s0 // 16 : s1 // 16]),
-                y[nt][:, s0:s1],
-                gates[:, s0:s1],
-                MULT,
-            )
+        def scatter(nt, s0, s1):
+            nc.vector.tensor_tensor(listed(results[nt], s0, s1), y[nt][:, s0:s1], gates[:, s0:s1], MULT)
 
-        first, second, rest = GROUPS
-        for raw, (a, m0, m1, share) in zip(wu_raw, WU_CHUNKS):
-            if m0 == 96:
-                round_last(raw, a, m0, m1)
-            else:
-                round_wu(raw, a, m0, m1, share)
-            if (a, m0) == (0, 64):
-                for r in range(0, PACK, 2):
-                    quantise_wu(0, r, r + 2)
-            if (a, m0) == (1, 0):
-                for r in range(PACK):
-                    quantise_wu(1, r, r + 1, 0, 64)
-        late = keep.tile([P, 3 * W], U32, name="late", tag="wu_raw1_96", align_bytes=64)
-        x_last = keep.tile([P, W], U32, name="x_last", tag="x_last", align_bytes=64)
-        x_bf[0, 1] = x_last[:].bitcast(BF16)
-        x_bf[0, 0] = late[:, 0:W].bitcast(BF16)
-        x_bf[1, 0] = late[:, W : 2 * W].bitcast(BF16)
-        x_bf[1, 1] = late[:, 2 * W : 3 * W].bitcast(BF16)
-        project(first, 0, 0)
-        project(second, 1, 0)
+        round_on_scalar(0)
+        round_on_both(1)
+        for r in range(0, PACK, 2):
+            quantise_wu(0, r, r + 2, 0, P)
+        round_on_both(2)
         for r in range(PACK):
-            quantise_wu(1, r, r + 1, 64, P)
-        project(first, 0, 1, ((0, LEAD), (LEAD, C)))
-        project(second, 1, 1)
+            quantise_wu(1, r, r + 1, 0, P // 2)
+        round_on_scalar(3)
+        round_on_vector(4)
+
+        x_held = keep.tile([P, 3 * X_WORDS], U32, name="x_held", tag="wu_raw3", align_bytes=64)
+        x_last = keep.tile([P, X_WORDS], U32, name="x_last", tag="x_last", align_bytes=64)
+        x_bf[0, 1] = x_last[:].bitcast(BF16)
+        for i, (e, a) in enumerate(((0, 0), (1, 0), (1, 1))):
+            x_bf[e, a] = x_held[:, i * X_WORDS : (i + 1) * X_WORDS].bitcast(BF16)
+        project(0, 0)
+        project(1, 0)
+        for r in range(PACK):
+            quantise_wu(1, r, r + 1, P // 2, P)
+        project(0, 1, ((0, LEAD), (LEAD, C)))
+        project(1, 1)
+
         quantise_x(0, 0, 0, C, x_bf[0, 0])
+        last_pairs = stage[:, 2 * EARLY : 2 * T].rearrange("p (c h) -> p c h", h=2)
         for h in range(2):
-            gather(stage[:, 2 * EARLY : 2 * T], h, EARLY, T)
+            nc.vector.tensor_copy(out=last_pairs[:, :, h], in_=listed(u_pairs[h], EARLY, T))
         quantise_x(0, 1, 0, LEAD, x_bf[0, 1][:, 0 : LEAD * PACK])
-        expert(0, 0, 0, LEAD, C - LEAD, LEAD_BANK)
+        pieces = ((0, 0, LEAD), (1, 0, C), (0, LEAD, C), (2, 0, C), (3, 0, C))
+        expert(0, 0, BANKS // 2, 0, LEAD, C - LEAD)
         quantise_x(0, 1, LEAD, C - LEAD, x_bf[0, 1][:, LEAD * PACK :])
         quantise_x(1, 0, 0, C, x_bf[1, 0])
-        expert(0, 1)
-        expert(0, 0, LEAD, C)
-        expert(0, 2)
-        expert(0, 3)
-        late_codes = keep.tile([P, HALF], U32, name="late_codes", tag="x_last", align_bytes=64)
-        for e in rest:
+        for i, (nt, c0, c1) in enumerate(pieces[1:], 1):
+            expert(0, nt, (BANKS // 2 + i) % BANKS, c0, c1)
+        late_codes = keep.tile([P, PAIR_SLOTS], U32, name="late_codes", tag="x_last", align_bytes=64)
+        for e in (2, 3):
             slot_codes[e] = late_codes[:, (e - 2) * C : (e - 1) * C]
-        quantise_u(stage[:, T : 2 * T], late_codes[:], HALF, T)
+        quantise_u(stage[:, 2 * PAIR_SLOTS : 2 * T], late_codes[:], PAIR_SLOTS, T)
         quantise_x(1, 1, 0, C, x_bf[1, 1])
-        scatter(first, 0, (0, LEAD))
-        scatter(first, 1)
-        scatter(first, 0, (LEAD, C))
-        scatter(first, 2)
-        scatter(first, 3)
-        for nt in range(2):
-            expert(1, nt)
-            scatter(second, nt)
-        for e in rest:
-            for a in range(PASSES):
-                project(rest, e, a)
-            quantise_x(e, 0, 0, PASSES * C, x_rest[:, (e - 2) * PASSES * C * PACK : (e - 1) * PASSES * C * PACK])
-        expert(1, 2)
-        scatter(second, 2)
-        expert(1, 3)
-        scatter(second, 3)
+
         for nt in range(N_TILES):
-            for e in rest:
-                expert(e, nt)
-            scatter(rest, nt)
+            tag = "wu_raw3" if nt == 1 else f"results{nt}"
+            results[nt] = keep.tile([P, T], F32, name=f"results{nt}", tag=tag, align_bytes=64)
+        for nt, c0, c1 in pieces:
+            scatter(nt, c0, c1)
+
+        for nt in range(N_TILES // 2):
+            expert(1, nt, nt)
+            scatter(nt, C, 2 * C)
+        for e in (2, 3):
+            for a in range(PASSES):
+                project(e, a)
+            quantise_x(e, 0, 0, PASSES * C, x_bf23[:, (e - 2) * PASSES * C * PACK : (e - 1) * PASSES * C * PACK])
+        for nt in range(N_TILES // 2, N_TILES):
+            expert(1, nt, nt)
+            scatter(nt, C, 2 * C)
+
+        for nt in range(N_TILES):
+            for e in (2, 3):
+                expert(e, nt, (BANKS // 2 + 2 * nt + e - 2) % BANKS)
+            scatter(nt, 2 * C, T)
             nc.sync.dma_start(out=out[nt * P : (nt + 1) * P, :], in_=results[nt][:])

@@ -15,6 +15,7 @@ U8 = mybir.dt.uint8
 FP8X4 = mybir.dt.float8_e4m3fn_x4
 SILU = mybir.ActivationFunctionType.Silu
 MULT = mybir.AluOpType.mult
+ADD = mybir.AluOpType.add
 
 P = 128
 PACK = 4
@@ -25,20 +26,26 @@ BANKS = 8
 PER_COLUMN = 16
 PLANES_A_TILE = 4
 PAIR_SLOTS = 2 * C
-EARLY = 3 * C
+OVERLAP = 16
 LEAD = 64
 X_WORDS = C * PACK // 2
 
-U_SHARE = (336, 160)
-WU_SHARE = 24
+U_VECTOR = 336
+U_GPSIMD = 224
+WU_VECTOR = {1: 32, 2: 16}
+HALVED = 2
 
 WU_LOADS = ((0, 0, P // 2), (0, P // 2, P), (1, 0, P // 2), (1, P // 2, 3 * P // 4), (1, 3 * P // 4, P))
 
+LATE_X = ((2, 1), (3, 0), (3, 1))
+X_ORDER = ((1, 0), (0, 0), (0, 1), (1, 1), (2, 0)) + LATE_X
 BIAS_BANK = BANKS - 1
 
 
 def x_bank(e, a):
-    return 2 * a + e if e < 2 else 2 * e + a
+    if (e, a) in LATE_X:
+        return BANKS // 2 + LATE_X.index((e, a))
+    return 2 * a + e if e < 2 else BIAS_BANK - 1
 
 
 def tile_moe_prv_lin_silu_kernel(tc, uT, wu, w_words, w_scales, b, gate, offs, out):
@@ -71,10 +78,6 @@ def tile_moe_prv_lin_silu_kernel(tc, uT, wu, w_words, w_scales, b, gate, offs, o
         make_identity(nc, identity[:])
         for g in range(2):
             nc.vector.memset(w_planes[g][:].bitcast(I32), 0)
-        x_codes = keep.tile([P, LEAD + E * PASSES * C], U32, name="x_codes", align_bytes=64)
-        x_scales = keep.tile([P, LEAD + E * PASSES * C], U8, name="x_scales", align_bytes=64)
-        nc.vector.memset(x_codes[:, 0:LEAD].bitcast(I32), 0)
-        nc.vector.memset(x_scales[:, 0:LEAD].bitcast(I32), 0)
 
         u_rows = uT.rearrange("(p j) t -> p j t", j=PACK)
         wu_rows = wu.rearrange("(p j) k -> p j k", j=PACK)
@@ -110,41 +113,53 @@ def tile_moe_prv_lin_silu_kernel(tc, uT, wu, w_words, w_scales, b, gate, offs, o
         load_codes(2)
         load_codes(3)
 
-        u_pairs = [keep.tile([P, T], U32, name=f"u_pairs{h}") for h in range(2)]
+        first_pairs = keep.tile([P, T], U32, name="first_pairs")
+        shared = keep.tile([P, PACK * X_WORDS - OVERLAP + T], U32, name="shared", tag="shared", align_bytes=64)
+        u_pairs = [first_pairs[:], shared[:, PACK * X_WORDS - OVERLAP :]]
         u_codes = keep.tile([P, PAIR_SLOTS], U32, name="u_codes", align_bytes=64)
         u_scales = keep.tile([P, T], U8, name="u_scales", align_bytes=64)
-        stage = keep.tile([P, 2 * EARLY + PACK * X_WORDS], U32, name="stage", align_bytes=64)
-        early_pairs = keep.tile([P, 2 * EARLY], U32, name="early_pairs")
+        pair_words = keep.tile([P, 2 * PAIR_SLOTS], U32, name="pair_words", align_bytes=64)
+        gathered = keep.tile([P, 2 * T], U32, name="gathered")
+
+        def weave(words, s0, s1):
+            nc.vector.tensor_copy(
+                out=words.bitcast(I32).rearrange("p (c h) -> p c h", h=2),
+                in_=gathered[:].bitcast(I32).rearrange("p (h c) -> p c h", h=2)[:, s0:s1, :],
+            )
+
         slot_codes = {e: u_codes[:, e * C : (e + 1) * C] for e in range(2)}
 
         def listed(window, s0, s1):
-            return window[:].indirect(offsets[:, s0 // PER_COLUMN : s1 // PER_COLUMN])
+            return window.indirect(offsets[:, s0 // PER_COLUMN : s1 // PER_COLUMN])
 
         def quantise_u(words, codes, s0, s1):
             nc.vector.quantize_mx(out=codes.bitcast(FP8X4), scales=u_scales[:, s0:s1], in_=words.bitcast(BF16))
 
-        parts = ((0, PAIR_SLOTS), (PAIR_SLOTS, EARLY))
-        for h, gathers in enumerate((((0, EARLY),), parts)):
-            src = u_raw[h][:].rearrange("p j t -> p t j")
-            dst = u_pairs[h][:].bitcast(BF16).rearrange("p (t j) -> p t j", j=2)
-            nc.scalar.copy(out=dst[:, U_SHARE[h] :, :], in_=src[:, U_SHARE[h] :, :])
-            nc.vector.tensor_copy(out=dst[:, : U_SHARE[h], :], in_=src[:, : U_SHARE[h], :])
-            for s0, s1 in gathers:
-                nc.vector.tensor_copy(out=early_pairs[:, h * EARLY + s0 : h * EARLY + s1], in_=listed(u_pairs[h], s0, s1))
+        def u_views(h):
+            dst = u_pairs[h].bitcast(BF16).rearrange("p (t j) -> p t j", j=2)
+            return dst, u_raw[h][:].rearrange("p j t -> p t j")
+
+        def gather(h):
+            for s0 in range(0, T, PAIR_SLOTS):
+                s1 = s0 + PAIR_SLOTS
+                nc.vector.tensor_copy(out=gathered[:, h * T + s0 : h * T + s1], in_=listed(u_pairs[h], s0, s1))
+
+        dst, src = u_views(0)
+        nc.scalar.copy(out=dst[:, U_VECTOR:, :], in_=src[:, U_VECTOR:, :])
+        nc.vector.tensor_copy(out=dst[:, :U_VECTOR, :], in_=src[:, :U_VECTOR, :])
+        gather(0)
+        dst, src = u_views(1)
+        nc.scalar.copy(out=dst[:, U_GPSIMD:, :], in_=src[:, U_GPSIMD:, :])
+        nc.gpsimd.tensor_scalar(dst[:, :U_GPSIMD, :], src[:, :U_GPSIMD, :], 1.0, 0.0, MULT, ADD)
+        gather(1)
         bias = keep.tile([P, E, N_TILES], F32, name="bias", tag="u_raw1")
         nc.vector.tensor_copy(out=bias[:], in_=banks[BIAS_BANK][:, :, P - N_TILES : P])
-        for s0, s1 in parts:
-            nc.vector.tensor_copy(
-                out=stage[:, 2 * s0 : 2 * s1].bitcast(I32).rearrange("p (c h) -> p c h", h=2),
-                in_=early_pairs[:].bitcast(I32).rearrange("p (h c) -> p c h", h=2)[:, s0:s1, :],
-            )
-        quantise_u(stage[:, 0 : 2 * PAIR_SLOTS], u_codes[:], 0, PAIR_SLOTS)
+        weave(pair_words[:], 0, PAIR_SLOTS)
 
-        wu_bf0 = keep.tile([P, PACK * X_WORDS], U32, name="wu_bf0", align_bytes=64)
-        wu_bf = [
-            words.bitcast(BF16).rearrange("p (r m j) -> p r m j", r=PACK, j=PACK)
-            for words in (wu_bf0[:], stage[:, 2 * EARLY :])
-        ]
+        def planes(words):
+            return words.bitcast(BF16).rearrange("p (r m j) -> p r m j", r=PACK, j=PACK)
+
+        wu_bf = {0: planes(shared[:, 0 : PACK * X_WORDS])}
         wu_codes = [keep.tile([P, PACK, P], U32, name=f"wu_codes{a}", align_bytes=64) for a in range(PASSES)]
         wu_scales = [keep.tile([P, PACK, P], U8, name=f"wu_scales{a}", align_bytes=64) for a in range(PASSES)]
 
@@ -153,16 +168,17 @@ def tile_moe_prv_lin_silu_kernel(tc, uT, wu, w_words, w_scales, b, gate, offs, o
             dst = wu_bf[a][:, :, m0:m1, :].rearrange("p r m j -> p m j r")
             return dst, wu_raw[i][:].rearrange("p j (m r) -> p m j r", r=PACK)
 
-        def round_on_scalar(i):
+        def round_whole(copy, i):
             dst, src = wu_views(i)
-            nc.scalar.copy(out=dst, in_=src)
+            copy(out=dst, in_=src)
 
         def round_on_both(i):
             dst, src = wu_views(i)
-            nc.scalar.copy(out=dst[:, WU_SHARE:, :, :], in_=src[:, WU_SHARE:, :, :])
-            nc.vector.tensor_copy(out=dst[:, :WU_SHARE, :, :], in_=src[:, :WU_SHARE, :, :])
+            cut = P // 2 - WU_VECTOR[i]
+            nc.scalar.copy(out=dst[:, :cut, :, :], in_=src[:, :cut, :, :])
+            nc.vector.tensor_copy(out=dst[:, cut:, :, :], in_=src[:, cut:, :, :])
 
-        def round_on_vector(i):
+        def round_by_planes(i):
             dst, src = wu_views(i)
             for r in range(0, PACK, 2):
                 nc.vector.tensor_copy(out=dst[:, :, :, r : r + 2], in_=src[:, :, :, r : r + 2])
@@ -175,19 +191,17 @@ def tile_moe_prv_lin_silu_kernel(tc, uT, wu, w_words, w_scales, b, gate, offs, o
             )
 
         x_bf = {}
-        x_bf23 = keep.tile([P, 2 * PASSES * C * PACK], BF16, name="x_bf23", align_bytes=64)
-        for e in (2, 3):
-            for a in range(PASSES):
-                i = (e - 2) * PASSES + a
-                x_bf[e, a] = x_bf23[:, i * C * PACK : (i + 1) * C * PACK]
+        x_late = keep.tile([P, len(LATE_X) * C * PACK], BF16, name="x_late", align_bytes=64)
+        for i, (e, a) in enumerate(LATE_X):
+            x_bf[e, a] = x_late[:, i * C * PACK : (i + 1) * C * PACK]
 
         def x_columns(e, a, c0, count):
-            first = LEAD + (e * PASSES + a) * C + c0
+            first = X_ORDER.index((e, a)) * C + c0
             return slice(first, first + count)
 
-        def project(e, a, cuts=((0, C),)):
+        def project(e, a, cuts=((0, C),), order=range(PACK)):
             bank = banks[x_bank(e, a)]
-            for r in range(PACK):
+            for r in order:
                 nc.tensor.matmul_mx(
                     out=bank[:, r, :],
                     lhsT=wu_codes[a][:, r, :].bitcast(FP8X4),
@@ -233,49 +247,59 @@ def tile_moe_prv_lin_silu_kernel(tc, uT, wu, w_words, w_scales, b, gate, offs, o
         results = {}
 
         def scatter(nt, s0, s1):
-            nc.vector.tensor_tensor(listed(results[nt], s0, s1), y[nt][:, s0:s1], gates[:, s0:s1], MULT)
+            nc.vector.tensor_tensor(listed(results[nt][:], s0, s1), y[nt][:, s0:s1], gates[:, s0:s1], MULT)
 
-        round_on_scalar(0)
+        round_whole(nc.scalar.copy, 0)
         round_on_both(1)
-        for r in range(0, PACK, 2):
-            quantise_wu(0, r, r + 2, 0, P)
+        quantise_u(pair_words[:], u_codes[:], 0, PAIR_SLOTS)
+        for r0, r1 in ((0, 2), (2, 3), (3, 4)):
+            quantise_wu(0, r0, r1, 0, P)
+        wu_bf1 = keep.tile([P, PACK * X_WORDS], U32, name="wu_bf1", tag="wu_raw1", align_bytes=64)
+        wu_bf[1] = planes(wu_bf1[:])
         round_on_both(2)
-        for r in range(PACK):
+        third_words = keep.tile([P, X_WORDS], U32, name="third_words", tag="shared", align_bytes=64)
+        weave(third_words[:], 2 * C, 3 * C)
+        round_whole(nc.vector.tensor_copy, 3)
+        third_codes = keep.tile([P, C], U32, name="third_codes", align_bytes=64)
+        slot_codes[2] = third_codes[:]
+        quantise_u(third_words[:], slot_codes[2], 2 * C, 3 * C)
+        for r in range(HALVED):
             quantise_wu(1, r, r + 1, 0, P // 2)
-        round_on_scalar(3)
-        round_on_vector(4)
+        round_by_planes(4)
+        x_codes = keep.tile([P, E * PASSES * C], U32, name="x_codes", tag="wu_raw4", align_bytes=64)
+        x_scales = keep.tile([P, E * PASSES * C], U8, name="x_scales", align_bytes=64)
 
-        x_held = keep.tile([P, 3 * X_WORDS], U32, name="x_held", tag="wu_raw3", align_bytes=64)
+        x_held = keep.tile([P, 4 * X_WORDS], U32, name="x_held", tag="wu_raw2", align_bytes=64)
         x_last = keep.tile([P, X_WORDS], U32, name="x_last", tag="x_last", align_bytes=64)
         x_bf[0, 1] = x_last[:].bitcast(BF16)
-        for i, (e, a) in enumerate(((0, 0), (1, 0), (1, 1))):
+        for i, (e, a) in enumerate(((0, 0), (1, 0), (2, 0), (1, 1))):
             x_bf[e, a] = x_held[:, i * X_WORDS : (i + 1) * X_WORDS].bitcast(BF16)
         project(0, 0)
-        project(1, 0)
+        project(1, 0, order=range(PACK - 1, -1, -1))
+        project(2, 0)
         for r in range(PACK):
-            quantise_wu(1, r, r + 1, P // 2, P)
+            quantise_wu(1, r, r + 1, P // 2 if r < HALVED else 0, P)
         project(0, 1, ((0, LEAD), (LEAD, C)))
         project(1, 1)
 
         quantise_x(0, 0, 0, C, x_bf[0, 0])
-        last_pairs = stage[:, 2 * EARLY : 2 * T].rearrange("p (c h) -> p c h", h=2)
-        for h in range(2):
-            nc.vector.tensor_copy(out=last_pairs[:, :, h], in_=listed(u_pairs[h], EARLY, T))
+        quantise_x(1, 0, 0, C, x_bf[1, 0])
+        late_words = wu_bf1[:, (PACK - 1) * X_WORDS :]
+        weave(late_words, 3 * C, T)
         quantise_x(0, 1, 0, LEAD, x_bf[0, 1][:, 0 : LEAD * PACK])
         pieces = ((0, 0, LEAD), (1, 0, C), (0, LEAD, C), (2, 0, C), (3, 0, C))
         expert(0, 0, BANKS // 2, 0, LEAD, C - LEAD)
         quantise_x(0, 1, LEAD, C - LEAD, x_bf[0, 1][:, LEAD * PACK :])
-        quantise_x(1, 0, 0, C, x_bf[1, 0])
+        quantise_x(2, 0, 0, C, x_bf[2, 0])
         for i, (nt, c0, c1) in enumerate(pieces[1:], 1):
             expert(0, nt, (BANKS // 2 + i) % BANKS, c0, c1)
-        late_codes = keep.tile([P, PAIR_SLOTS], U32, name="late_codes", tag="x_last", align_bytes=64)
-        for e in (2, 3):
-            slot_codes[e] = late_codes[:, (e - 2) * C : (e - 1) * C]
-        quantise_u(stage[:, 2 * PAIR_SLOTS : 2 * T], late_codes[:], PAIR_SLOTS, T)
+        late_codes = keep.tile([P, C], U32, name="late_codes", tag="x_last", align_bytes=64)
+        slot_codes[3] = late_codes[:]
+        quantise_u(late_words, late_codes[:], 3 * C, T)
         quantise_x(1, 1, 0, C, x_bf[1, 1])
 
         for nt in range(N_TILES):
-            tag = "wu_raw3" if nt == 1 else f"results{nt}"
+            tag = "wu_raw2" if nt == 1 else f"results{nt}"
             results[nt] = keep.tile([P, T], F32, name=f"results{nt}", tag=tag, align_bytes=64)
         for nt, c0, c1 in pieces:
             scatter(nt, c0, c1)
@@ -283,10 +307,10 @@ def tile_moe_prv_lin_silu_kernel(tc, uT, wu, w_words, w_scales, b, gate, offs, o
         for nt in range(N_TILES // 2):
             expert(1, nt, nt)
             scatter(nt, C, 2 * C)
-        for e in (2, 3):
-            for a in range(PASSES):
-                project(e, a)
-            quantise_x(e, 0, 0, PASSES * C, x_bf23[:, (e - 2) * PASSES * C * PACK : (e - 1) * PASSES * C * PACK])
+        for e, a in LATE_X:
+            project(e, a)
+        quantise_x(2, 1, 0, C, x_late[:, 0 : C * PACK])
+        quantise_x(3, 0, 0, PASSES * C, x_late[:, C * PACK :])
         for nt in range(N_TILES // 2, N_TILES):
             expert(1, nt, nt)
             scatter(nt, C, 2 * C)

@@ -14,6 +14,7 @@ U16 = mybir.dt.uint16
 U8 = mybir.dt.uint8
 FP8X4 = mybir.dt.float8_e4m3fn_x4
 SILU = mybir.ActivationFunctionType.Silu
+COPY = mybir.ActivationFunctionType.Copy
 MULT = mybir.AluOpType.mult
 ADD = mybir.AluOpType.add
 
@@ -27,7 +28,6 @@ PER_COLUMN = 16
 PLANES_A_TILE = 4
 PAIR_SLOTS = 2 * C
 OVERLAP = 16
-LEAD = 64
 X_WORDS = C * PACK // 2
 
 U_VECTOR = 336
@@ -37,15 +37,9 @@ HALVED = 2
 
 WU_LOADS = ((0, 0, P // 2), (0, P // 2, P), (1, 0, P // 2), (1, P // 2, 3 * P // 4), (1, 3 * P // 4, P))
 
-LATE_X = ((2, 1), (3, 0), (3, 1))
-X_ORDER = ((1, 0), (0, 0), (0, 1), (1, 1), (2, 0)) + LATE_X
+X_ORDER = ((0, 0), (1, 0), (2, 0), (0, 1), (1, 1), (2, 1), (3, 0), (3, 1))
 BIAS_BANK = BANKS - 1
-
-
-def x_bank(e, a):
-    if (e, a) in LATE_X:
-        return BANKS // 2 + LATE_X.index((e, a))
-    return 2 * a + e if e < 2 else BIAS_BANK - 1
+TILE_ORDER = ((0, 2, 1, 3), (0, 2, 1, 3), (2, 0, 1, 3), (3, 0, 2, 1))
 
 
 def tile_moe_prv_lin_silu_kernel(tc, uT, wu, w_words, w_scales, b, gate, offs, out):
@@ -191,16 +185,13 @@ def tile_moe_prv_lin_silu_kernel(tc, uT, wu, w_words, w_scales, b, gate, offs, o
             )
 
         x_bf = {}
-        x_late = keep.tile([P, len(LATE_X) * C * PACK], BF16, name="x_late", align_bytes=64)
-        for i, (e, a) in enumerate(LATE_X):
-            x_bf[e, a] = x_late[:, i * C * PACK : (i + 1) * C * PACK]
 
-        def x_columns(e, a, c0, count):
-            first = X_ORDER.index((e, a)) * C + c0
-            return slice(first, first + count)
+        def x_columns(e, a, passes=1):
+            first = X_ORDER.index((e, a)) * C
+            return slice(first, first + passes * C)
 
-        def project(e, a, cuts=((0, C),), order=range(PACK)):
-            bank = banks[x_bank(e, a)]
+        def project(e, a, copy, order=range(PACK)):
+            bank = banks[X_ORDER.index((e, a))]
             for r in order:
                 nc.tensor.matmul_mx(
                     out=bank[:, r, :],
@@ -211,43 +202,47 @@ def tile_moe_prv_lin_silu_kernel(tc, uT, wu, w_words, w_scales, b, gate, offs, o
                     start=True,
                     stop=True,
                 )
-            for c0, c1 in cuts:
-                nc.scalar.copy(
-                    out=x_bf[e, a].rearrange("p (c r) -> p c r", r=PACK)[:, c0:c1, :],
-                    in_=bank[:, :, c0:c1].rearrange("p r c -> p c r"),
-                )
+            copy(
+                out=x_bf[e, a].rearrange("p (c r) -> p c r", r=PACK),
+                in_=bank[:].rearrange("p r c -> p c r"),
+            )
 
-        def quantise_x(e, a, c0, count, values):
-            columns = x_columns(e, a, c0, count)
+        def quantise_x(e, a, passes, values):
+            columns = x_columns(e, a, passes)
             nc.vector.quantize_mx(out=x_codes[:, columns].bitcast(FP8X4), scales=x_scales[:, columns], in_=values)
 
         y = [keep.tile([P, E * C], F32, name=f"y{nt}") for nt in range(N_TILES)]
 
-        def expert(e, nt, bank_number, c0=0, c1=C, shift=0):
-            cols = slice(nt * P, (nt + 1) * P)
-            sums = banks[bank_number][:, 0, :]
-            for a in range(PASSES):
-                g, i = divmod(e * PASSES + a, PLANES_A_TILE)
-                nc.tensor.matmul_mx(
-                    out=sums,
-                    lhsT=w_codes[e][:, a, cols].bitcast(FP8X4),
-                    lhsT_scale=w_planes[g][4 * i : P, cols],
-                    rhs=x_codes[:, x_columns(e, a, -shift, C)].bitcast(FP8X4),
-                    rhs_scale=x_scales[:, x_columns(e, a, -shift, C)],
-                    start=(a == 0),
-                    stop=(a == PASSES - 1),
-                )
-            nc.scalar.activation(
-                out=y[nt][:, e * C + c0 : e * C + c1],
-                in_=sums[:, shift + c0 : shift + c1],
-                func=SILU,
-                bias=bias[:, e, nt : nt + 1],
-            )
+        def expert(e):
+            for place, nt in enumerate(TILE_ORDER[e]):
+                cols = slice(nt * P, (nt + 1) * P)
+                sums = banks[(e * N_TILES + place) % BANKS][:, 0, :]
+                for a in range(PASSES):
+                    g, i = divmod(e * PASSES + a, PLANES_A_TILE)
+                    nc.tensor.matmul_mx(
+                        out=sums,
+                        lhsT=w_codes[e][:, a, cols].bitcast(FP8X4),
+                        lhsT_scale=w_planes[g][4 * i : P, cols],
+                        rhs=x_codes[:, x_columns(e, a)].bitcast(FP8X4),
+                        rhs_scale=x_scales[:, x_columns(e, a)],
+                        start=(a == 0),
+                        stop=(a == PASSES - 1),
+                    )
+                nc.scalar.activation(out=y[nt][:, e * C : (e + 1) * C], in_=sums, func=SILU, bias=bias[:, e, nt : nt + 1])
 
         results = {}
 
-        def scatter(nt, s0, s1):
+        def scatter_vector(nt, s0, s1):
             nc.vector.tensor_tensor(listed(results[nt][:], s0, s1), y[nt][:, s0:s1], gates[:, s0:s1], MULT)
+
+        def times_gate(gated, nt, s0, s1):
+            nc.vector.tensor_tensor(gated[:, s0:s1], y[nt][:, s0:s1], gates[:, s0:s1], MULT)
+
+        def scatter_scalar(gated, nt, s0, s1):
+            nc.scalar.activation(listed(results[nt][:], s0, s1), gated[:, s0:s1], COPY)
+
+        def store(nt):
+            nc.sync.dma_start(out=out[nt * P : (nt + 1) * P, :], in_=results[nt][:])
 
         round_whole(nc.scalar.copy, 0)
         round_on_both(1)
@@ -269,54 +264,54 @@ def tile_moe_prv_lin_silu_kernel(tc, uT, wu, w_words, w_scales, b, gate, offs, o
         x_codes = keep.tile([P, E * PASSES * C], U32, name="x_codes", tag="wu_raw4", align_bytes=64)
         x_scales = keep.tile([P, E * PASSES * C], U8, name="x_scales", align_bytes=64)
 
-        x_held = keep.tile([P, 4 * X_WORDS], U32, name="x_held", tag="wu_raw2", align_bytes=64)
-        x_last = keep.tile([P, X_WORDS], U32, name="x_last", tag="x_last", align_bytes=64)
-        x_bf[0, 1] = x_last[:].bitcast(BF16)
-        for i, (e, a) in enumerate(((0, 0), (1, 0), (2, 0), (1, 1))):
-            x_bf[e, a] = x_held[:, i * X_WORDS : (i + 1) * X_WORDS].bitcast(BF16)
-        project(0, 0)
-        project(1, 0, order=range(PACK - 1, -1, -1))
-        project(2, 0)
+        x_early = keep.tile([P, 3 * X_WORDS], U32, name="x_early", tag="wu_raw2", align_bytes=64)
+        x_middle = keep.tile([P, 2 * X_WORDS], U32, name="x_middle", align_bytes=64)
+        x_late = keep.tile([P, 3 * X_WORDS], U32, name="x_late", tag="x_late", align_bytes=64)
+        for tile, first, end in ((x_early, 0, 3), (x_middle, 3, 5), (x_late, 5, 8)):
+            for i, (e, a) in enumerate(X_ORDER[first:end]):
+                x_bf[e, a] = tile[:, i * X_WORDS : (i + 1) * X_WORDS].bitcast(BF16)
+        project(0, 0, nc.scalar.copy)
+        project(1, 0, nc.scalar.copy, order=range(PACK - 1, -1, -1))
+        project(2, 0, nc.scalar.copy)
         for r in range(PACK):
             quantise_wu(1, r, r + 1, P // 2 if r < HALVED else 0, P)
-        project(0, 1, ((0, LEAD), (LEAD, C)))
-        project(1, 1)
-
-        quantise_x(0, 0, 0, C, x_bf[0, 0])
-        quantise_x(1, 0, 0, C, x_bf[1, 0])
         late_words = wu_bf1[:, (PACK - 1) * X_WORDS :]
         weave(late_words, 3 * C, T)
-        quantise_x(0, 1, 0, LEAD, x_bf[0, 1][:, 0 : LEAD * PACK])
-        pieces = ((0, 0, LEAD), (1, 0, C), (0, LEAD, C), (2, 0, C), (3, 0, C))
-        expert(0, 0, BANKS // 2, 0, LEAD, C - LEAD)
-        quantise_x(0, 1, LEAD, C - LEAD, x_bf[0, 1][:, LEAD * PACK :])
-        quantise_x(2, 0, 0, C, x_bf[2, 0])
-        for i, (nt, c0, c1) in enumerate(pieces[1:], 1):
-            expert(0, nt, (BANKS // 2 + i) % BANKS, c0, c1)
-        late_codes = keep.tile([P, C], U32, name="late_codes", tag="x_last", align_bytes=64)
+        quantise_x(0, 0, 3, x_early[:].bitcast(BF16))
+        late_codes = keep.tile([P, C], U32, name="late_codes", align_bytes=64)
         slot_codes[3] = late_codes[:]
         quantise_u(late_words, late_codes[:], 3 * C, T)
-        quantise_x(1, 1, 0, C, x_bf[1, 1])
+        project(0, 1, nc.scalar.copy)
+        project(1, 1, nc.vector.tensor_copy)
+        quantise_x(0, 1, 1, x_bf[0, 1])
+        quantise_x(1, 1, 1, x_bf[1, 1])
+        project(2, 1, nc.scalar.copy)
+        project(3, 0, nc.scalar.copy)
+        project(3, 1, nc.vector.tensor_copy)
+        expert(0)
+        quantise_x(2, 1, 3, x_late[:].bitcast(BF16))
+        for e in range(1, E):
+            expert(e)
 
-        for nt in range(N_TILES):
-            tag = "wu_raw2" if nt == 1 else f"results{nt}"
-            results[nt] = keep.tile([P, T], F32, name=f"results{nt}", tag=tag, align_bytes=64)
-        for nt, c0, c1 in pieces:
-            scatter(nt, c0, c1)
-
-        for nt in range(N_TILES // 2):
-            expert(1, nt, nt)
-            scatter(nt, C, 2 * C)
-        for e, a in LATE_X:
-            project(e, a)
-        quantise_x(2, 1, 0, C, x_late[:, 0 : C * PACK])
-        quantise_x(3, 0, 0, PASSES * C, x_late[:, C * PACK :])
-        for nt in range(N_TILES // 2, N_TILES):
-            expert(1, nt, nt)
-            scatter(nt, C, 2 * C)
-
-        for nt in range(N_TILES):
-            for e in (2, 3):
-                expert(e, nt, (BANKS // 2 + 2 * nt + e - 2) % BANKS)
-            scatter(nt, 2 * C, T)
-            nc.sync.dma_start(out=out[nt * P : (nt + 1) * P, :], in_=results[nt][:])
+        results[0] = keep.tile([P, T], F32, name="results0", tag="x_late", align_bytes=64)
+        results[1] = keep.tile([P, T], F32, name="results1")
+        results[2] = keep.tile([P, T], F32, name="results2", tag="u_raw1")
+        gated2 = keep.tile([P, T], F32, name="gated2", tag="gated2")
+        gated3 = keep.tile([P, T], F32, name="gated3")
+        scatter_vector(0, 0, C)
+        scatter_vector(0, C, 2 * C)
+        times_gate(gated2, 2, 0, 3 * C)
+        scatter_vector(0, 2 * C, 3 * C)
+        times_gate(gated3, 3, 0, T)
+        scatter_vector(0, 3 * C, T)
+        store(0)
+        scatter_scalar(gated2, 2, 0, 3 * C)
+        results[3] = keep.tile([P, T], F32, name="results3", tag="gated2")
+        scatter_vector(1, 2 * C, T)
+        scatter_vector(2, 3 * C, T)
+        store(2)
+        scatter_scalar(gated3, 3, 0, 2 * C)
+        scatter_scalar(gated3, 3, 2 * C, T)
+        store(3)
+        scatter_vector(1, 0, 2 * C)
+        store(1)

@@ -30,16 +30,16 @@ PAIR_SLOTS = 2 * C
 OVERLAP = 16
 X_WORDS = C * PACK // 2
 
-U_VECTOR = 336
-U_GPSIMD = 224
-WU_VECTOR = {1: 32, 2: 16}
+U_VECTOR = 176
+U_GPSIMD = 128
+WU_VECTOR = {0: 12, 1: 40, 2: 8}
 HALVED = 2
 
 WU_LOADS = ((0, 0, P // 2), (0, P // 2, P), (1, 0, P // 2), (1, P // 2, 3 * P // 4), (1, 3 * P // 4, P))
 
-X_ORDER = ((0, 0), (1, 0), (2, 0), (0, 1), (1, 1), (2, 1), (3, 0), (3, 1))
+X_ORDER = tuple((e, a) for a in range(PASSES) for e in range(E))
 BIAS_BANK = BANKS - 1
-TILE_ORDER = ((0, 2, 1, 3), (0, 2, 1, 3), (2, 0, 1, 3), (3, 0, 2, 1))
+TILE_ORDER = ((2, 0, 3, 1), (3, 1, 0, 2), (0, 1, 2, 3), (2, 3, 0, 1))
 
 
 def tile_moe_prv_lin_silu_kernel(tc, uT, wu, w_words, w_scales, b, gate, offs, out):
@@ -49,7 +49,7 @@ def tile_moe_prv_lin_silu_kernel(tc, uT, wu, w_words, w_scales, b, gate, offs, o
         psum = ctx.enter_context(tc.psum_pool(name="psum", bufs=1))
 
         offsets = keep.tile([P, T // PER_COLUMN], U16, name="offsets")
-        u_raw = [keep.tile([P, 2, T], F32, name=f"u_raw{h}", tag=f"u_raw{h}") for h in range(2)]
+        u_raw = [keep.tile([P, 2, T // 2], F32, name=f"u_raw{i}", tag=f"u_raw{i}") for i in range(4)]
         wu_raw = [
             keep.tile([P, PACK, PACK * (m1 - m0)], F32, name=f"wu_raw{i}", tag=f"wu_raw{i}", align_bytes=64)
             for i, (a, m0, m1) in enumerate(WU_LOADS)
@@ -93,35 +93,37 @@ def tile_moe_prv_lin_silu_kernel(tc, uT, wu, w_words, w_scales, b, gate, offs, o
         for e in range(E):
             nc.tensor.transpose(banks[BIAS_BANK][:, e, :], bias_rows[:].rearrange("q (p e) -> q e p", e=E)[:, e, :], identity[:])
 
-        nc.sync.dma_start(out=u_raw[0][:], in_=u_rows[:, 0:2, :])
-        nc.sync.dma_start(offsets[:], offs)
-        nc.sync.dma_start(out=u_raw[1][:], in_=u_rows[:, 2:4, :])
+        for i in range(4):
+            h, half = divmod(i, 2)
+            nc.sync.dma_start(out=u_raw[i][:], in_=u_rows[:, 2 * h : 2 * h + 2, half * T // 2 : (half + 1) * T // 2])
+            if i == 1:
+                nc.sync.dma_start(offsets[:], offs)
         for raw, (a, m0, m1) in zip(wu_raw, WU_LOADS):
             nc.sync.dma_start(out=raw[:], in_=wu_rows[:, :, a * K_PASS + PACK * m0 : a * K_PASS + PACK * m1])
         load_codes(0)
         load_planes(0)
-        nc.sync.dma_start(out=gates[:, 0:C], in_=gate[0:P, 0:C])
+        nc.sync.dma_start(out=gates[:, 0 : 2 * C], in_=gate[0:P, 0 : 2 * C])
         load_codes(1)
-        nc.sync.dma_start(out=gates[:, C:T], in_=gate[0:P, C:T])
         load_planes(1)
         load_codes(2)
         load_codes(3)
+        nc.sync.dma_start(out=gates[:, 2 * C : T], in_=gate[0:P, 2 * C : T])
 
         first_pairs = keep.tile([P, T], U32, name="first_pairs")
         shared = keep.tile([P, PACK * X_WORDS - OVERLAP + T], U32, name="shared", tag="shared", align_bytes=64)
         u_pairs = [first_pairs[:], shared[:, PACK * X_WORDS - OVERLAP :]]
-        u_codes = keep.tile([P, PAIR_SLOTS], U32, name="u_codes", align_bytes=64)
+        u_codes = keep.tile([P, T], U32, name="u_codes", align_bytes=64)
         u_scales = keep.tile([P, T], U8, name="u_scales", align_bytes=64)
         pair_words = keep.tile([P, 2 * PAIR_SLOTS], U32, name="pair_words", align_bytes=64)
         gathered = keep.tile([P, 2 * T], U32, name="gathered")
 
-        def weave(words, s0, s1):
-            nc.vector.tensor_copy(
+        def weave(copy, words, s0, s1):
+            copy(
                 out=words.bitcast(I32).rearrange("p (c h) -> p c h", h=2),
                 in_=gathered[:].bitcast(I32).rearrange("p (h c) -> p c h", h=2)[:, s0:s1, :],
             )
 
-        slot_codes = {e: u_codes[:, e * C : (e + 1) * C] for e in range(2)}
+        slot_codes = {e: u_codes[:, e * C : (e + 1) * C] for e in range(E)}
 
         def listed(window, s0, s1):
             return window.indirect(offsets[:, s0 // PER_COLUMN : s1 // PER_COLUMN])
@@ -129,9 +131,10 @@ def tile_moe_prv_lin_silu_kernel(tc, uT, wu, w_words, w_scales, b, gate, offs, o
         def quantise_u(words, codes, s0, s1):
             nc.vector.quantize_mx(out=codes.bitcast(FP8X4), scales=u_scales[:, s0:s1], in_=words.bitcast(BF16))
 
-        def u_views(h):
-            dst = u_pairs[h].bitcast(BF16).rearrange("p (t j) -> p t j", j=2)
-            return dst, u_raw[h][:].rearrange("p j t -> p t j")
+        def u_views(i):
+            h, half = divmod(i, 2)
+            words = u_pairs[h][:, half * T // 2 : (half + 1) * T // 2]
+            return words.bitcast(BF16).rearrange("p (t j) -> p t j", j=2), u_raw[i][:].rearrange("p j t -> p t j")
 
         def gather(h):
             for s0 in range(0, T, PAIR_SLOTS):
@@ -139,16 +142,21 @@ def tile_moe_prv_lin_silu_kernel(tc, uT, wu, w_words, w_scales, b, gate, offs, o
                 nc.vector.tensor_copy(out=gathered[:, h * T + s0 : h * T + s1], in_=listed(u_pairs[h], s0, s1))
 
         dst, src = u_views(0)
+        nc.scalar.copy(out=dst, in_=src)
+        dst, src = u_views(1)
         nc.scalar.copy(out=dst[:, U_VECTOR:, :], in_=src[:, U_VECTOR:, :])
         nc.vector.tensor_copy(out=dst[:, :U_VECTOR, :], in_=src[:, :U_VECTOR, :])
         gather(0)
-        dst, src = u_views(1)
+        dst, src = u_views(2)
+        nc.scalar.copy(out=dst, in_=src)
+        dst, src = u_views(3)
         nc.scalar.copy(out=dst[:, U_GPSIMD:, :], in_=src[:, U_GPSIMD:, :])
         nc.gpsimd.tensor_scalar(dst[:, :U_GPSIMD, :], src[:, :U_GPSIMD, :], 1.0, 0.0, MULT, ADD)
         gather(1)
-        bias = keep.tile([P, E, N_TILES], F32, name="bias", tag="u_raw1")
-        nc.vector.tensor_copy(out=bias[:], in_=banks[BIAS_BANK][:, :, P - N_TILES : P])
-        weave(pair_words[:], 0, PAIR_SLOTS)
+        bias_all = keep.tile([P, E, N_TILES], F32, name="bias_all", tag="u_raw3")
+        nc.scalar.copy(out=bias_all[:], in_=banks[BIAS_BANK][:, :, P - N_TILES : P])
+        bias = [bias_all[:, e, :] for e in range(E)]
+        weave(nc.vector.tensor_copy, pair_words[:], 0, PAIR_SLOTS)
 
         def planes(words):
             return words.bitcast(BF16).rearrange("p (r m j) -> p r m j", r=PACK, j=PACK)
@@ -211,7 +219,7 @@ def tile_moe_prv_lin_silu_kernel(tc, uT, wu, w_words, w_scales, b, gate, offs, o
             columns = x_columns(e, a, passes)
             nc.vector.quantize_mx(out=x_codes[:, columns].bitcast(FP8X4), scales=x_scales[:, columns], in_=values)
 
-        y = [keep.tile([P, E * C], F32, name=f"y{nt}") for nt in range(N_TILES)]
+        y = keep.tile([P, N_TILES, T], F32, name="y")
 
         def expert(e):
             for place, nt in enumerate(TILE_ORDER[e]):
@@ -228,90 +236,86 @@ def tile_moe_prv_lin_silu_kernel(tc, uT, wu, w_words, w_scales, b, gate, offs, o
                         start=(a == 0),
                         stop=(a == PASSES - 1),
                     )
-                nc.scalar.activation(out=y[nt][:, e * C : (e + 1) * C], in_=sums, func=SILU, bias=bias[:, e, nt : nt + 1])
+                nc.scalar.activation(out=y[:, nt, e * C : (e + 1) * C], in_=sums, func=SILU, bias=bias[e][:, nt : nt + 1])
 
         results = {}
 
         def scatter_vector(nt, s0, s1):
-            nc.vector.tensor_tensor(listed(results[nt][:], s0, s1), y[nt][:, s0:s1], gates[:, s0:s1], MULT)
+            nc.vector.tensor_tensor(listed(results[nt][:], s0, s1), y[:, nt, s0:s1], gates[:, s0:s1], MULT)
 
-        def times_gate(gated, nt, s0, s1):
-            nc.vector.tensor_tensor(gated[:, s0:s1], y[nt][:, s0:s1], gates[:, s0:s1], MULT)
+        gated = keep.tile([P, 2, T], F32, name="gated")
 
-        def scatter_scalar(gated, nt, s0, s1):
-            nc.scalar.activation(listed(results[nt][:], s0, s1), gated[:, s0:s1], COPY)
+        def times_gate(nt, s0, s1):
+            nc.vector.tensor_tensor(gated[:, nt - 2, s0:s1], y[:, nt, s0:s1], gates[:, s0:s1], MULT)
+
+        def scatter_scalar(nt, s0, s1):
+            nc.scalar.activation(listed(results[nt][:], s0, s1), gated[:, nt - 2, s0:s1], COPY)
 
         def store(nt):
             nc.sync.dma_start(out=out[nt * P : (nt + 1) * P, :], in_=results[nt][:])
 
-        round_whole(nc.scalar.copy, 0)
+        round_on_both(0)
+        quantise_u(pair_words[:], u_codes[:, 0:PAIR_SLOTS], 0, PAIR_SLOTS)
         round_on_both(1)
-        quantise_u(pair_words[:], u_codes[:], 0, PAIR_SLOTS)
         for r0, r1 in ((0, 2), (2, 3), (3, 4)):
             quantise_wu(0, r0, r1, 0, P)
         wu_bf1 = keep.tile([P, PACK * X_WORDS], U32, name="wu_bf1", tag="wu_raw1", align_bytes=64)
         wu_bf[1] = planes(wu_bf1[:])
         round_on_both(2)
-        third_words = keep.tile([P, X_WORDS], U32, name="third_words", tag="shared", align_bytes=64)
-        weave(third_words[:], 2 * C, 3 * C)
+        late_words = keep.tile([P, 2 * PAIR_SLOTS], U32, name="late_words", tag="shared", align_bytes=64)
+        weave(nc.vector.tensor_copy, late_words[:], PAIR_SLOTS, T)
         round_whole(nc.vector.tensor_copy, 3)
-        third_codes = keep.tile([P, C], U32, name="third_codes", align_bytes=64)
-        slot_codes[2] = third_codes[:]
-        quantise_u(third_words[:], slot_codes[2], 2 * C, 3 * C)
+        quantise_u(late_words[:], u_codes[:, PAIR_SLOTS:T], PAIR_SLOTS, T)
         for r in range(HALVED):
             quantise_wu(1, r, r + 1, 0, P // 2)
         round_by_planes(4)
         x_codes = keep.tile([P, E * PASSES * C], U32, name="x_codes", tag="wu_raw4", align_bytes=64)
         x_scales = keep.tile([P, E * PASSES * C], U8, name="x_scales", align_bytes=64)
 
-        x_early = keep.tile([P, 3 * X_WORDS], U32, name="x_early", tag="wu_raw2", align_bytes=64)
-        x_middle = keep.tile([P, 2 * X_WORDS], U32, name="x_middle", align_bytes=64)
-        x_late = keep.tile([P, 3 * X_WORDS], U32, name="x_late", tag="x_late", align_bytes=64)
-        for tile, first, end in ((x_early, 0, 3), (x_middle, 3, 5), (x_late, 5, 8)):
+        x_early = keep.tile([P, E * X_WORDS], U32, name="x_early", tag="wu_raw2", align_bytes=64)
+        x_middle = keep.tile([P, 3 * X_WORDS], U32, name="x_middle", tag="x_middle", align_bytes=64)
+        x_late = keep.tile([P, X_WORDS], U32, name="x_late", tag="x_late", align_bytes=64)
+        for tile, first, end in ((x_early, 0, 4), (x_middle, 4, 7), (x_late, 7, 8)):
             for i, (e, a) in enumerate(X_ORDER[first:end]):
                 x_bf[e, a] = tile[:, i * X_WORDS : (i + 1) * X_WORDS].bitcast(BF16)
+        backwards = range(PACK - 1, -1, -1)
         project(0, 0, nc.scalar.copy)
-        project(1, 0, nc.scalar.copy, order=range(PACK - 1, -1, -1))
+        project(1, 0, nc.scalar.copy, order=backwards)
         project(2, 0, nc.scalar.copy)
+        project(3, 0, nc.scalar.copy)
         for r in range(PACK):
             quantise_wu(1, r, r + 1, P // 2 if r < HALVED else 0, P)
-        late_words = wu_bf1[:, (PACK - 1) * X_WORDS :]
-        weave(late_words, 3 * C, T)
-        quantise_x(0, 0, 3, x_early[:].bitcast(BF16))
-        late_codes = keep.tile([P, C], U32, name="late_codes", align_bytes=64)
-        slot_codes[3] = late_codes[:]
-        quantise_u(late_words, late_codes[:], 3 * C, T)
+        quantise_x(0, 0, 2, x_early[:, 0 : 2 * X_WORDS].bitcast(BF16))
         project(0, 1, nc.scalar.copy)
-        project(1, 1, nc.vector.tensor_copy)
+        project(1, 1, nc.vector.tensor_copy, order=backwards)
         quantise_x(0, 1, 1, x_bf[0, 1])
+        quantise_x(2, 0, 2, x_early[:, 2 * X_WORDS :].bitcast(BF16))
         quantise_x(1, 1, 1, x_bf[1, 1])
-        project(2, 1, nc.scalar.copy)
-        project(3, 0, nc.scalar.copy)
-        project(3, 1, nc.vector.tensor_copy)
+        project(2, 1, nc.scalar.copy, order=backwards)
+        project(3, 1, nc.vector.tensor_copy, order=backwards)
+        quantise_x(2, 1, 1, x_bf[2, 1])
         expert(0)
-        quantise_x(2, 1, 3, x_late[:].bitcast(BF16))
-        for e in range(1, E):
-            expert(e)
-
-        results[0] = keep.tile([P, T], F32, name="results0", tag="x_late", align_bytes=64)
         results[1] = keep.tile([P, T], F32, name="results1")
-        results[2] = keep.tile([P, T], F32, name="results2", tag="u_raw1")
-        gated2 = keep.tile([P, T], F32, name="gated2", tag="gated2")
-        gated3 = keep.tile([P, T], F32, name="gated3")
+        results[2] = keep.tile([P, T], F32, name="results2", tag="x_middle", align_bytes=64)
+        scatter_vector(2, 0, C)
+        quantise_x(3, 1, 1, x_bf[3, 1])
+        results[0] = keep.tile([P, T], F32, name="results0", tag="x_late", align_bytes=64)
         scatter_vector(0, 0, C)
-        scatter_vector(0, C, 2 * C)
-        times_gate(gated2, 2, 0, 3 * C)
-        scatter_vector(0, 2 * C, 3 * C)
-        times_gate(gated3, 3, 0, T)
-        scatter_vector(0, 3 * C, T)
-        store(0)
-        scatter_scalar(gated2, 2, 0, 3 * C)
-        results[3] = keep.tile([P, T], F32, name="results3", tag="gated2")
-        scatter_vector(1, 2 * C, T)
-        scatter_vector(2, 3 * C, T)
-        store(2)
-        scatter_scalar(gated3, 3, 0, 2 * C)
-        scatter_scalar(gated3, 3, 2 * C, T)
-        store(3)
+        expert(1)
+        times_gate(3, 0, 2 * C)
         scatter_vector(1, 0, 2 * C)
+        expert(2)
+        expert(3)
+        results[3] = keep.tile([P, T], F32, name="results3", tag="u_raw3")
+        scatter_scalar(3, 0, 2 * C)
+        times_gate(2, C, T)
+        times_gate(3, 2 * C, T)
+        scatter_vector(0, 3 * C, T)
+        scatter_scalar(2, C, T)
+        store(2)
+        scatter_vector(1, 2 * C, T)
         store(1)
+        scatter_vector(0, C, 3 * C)
+        store(0)
+        scatter_scalar(3, 2 * C, T)
+        store(3)

@@ -30,15 +30,19 @@ PAIR_SLOTS = 2 * C
 OVERLAP = 16
 X_WORDS = C * PACK // 2
 
-U_VECTOR = 176
-U_GPSIMD = 128
-WU_VECTOR = {0: 12, 1: 40, 2: 8}
-HALVED = 2
+WU_WORDS = PACK * X_WORDS
+PAIRS_FROM = WU_WORDS - OVERLAP
 
-WU_LOADS = ((0, 0, P // 2), (0, P // 2, P), (1, 0, P // 2), (1, P // 2, 3 * P // 4), (1, 3 * P // 4, P))
+U_VECTOR = 336
+U_GPSIMD = 224
+WU_SCALAR = 24
+
+WU_LOADS = tuple((a, m0, m0 + P // 2) for a in range(PASSES) for m0 in (0, P // 2))
 
 X_ORDER = tuple((e, a) for a in range(PASSES) for e in range(E))
+X_PLACE = {(e, a): (e // 2, 2 * a + e % 2) for e, a in X_ORDER}
 BIAS_BANK = BANKS - 1
+SHARE = 64
 TILE_ORDER = ((2, 0, 3, 1), (3, 1, 0, 2), (0, 1, 2, 3), (2, 3, 0, 1))
 
 
@@ -49,7 +53,7 @@ def tile_moe_prv_lin_silu_kernel(tc, uT, wu, w_words, w_scales, b, gate, offs, o
         psum = ctx.enter_context(tc.psum_pool(name="psum", bufs=1))
 
         offsets = keep.tile([P, T // PER_COLUMN], U16, name="offsets")
-        u_raw = [keep.tile([P, 2, T // 2], F32, name=f"u_raw{i}", tag=f"u_raw{i}") for i in range(4)]
+        u_raw = [keep.tile([P, 2, T], F32, name=f"u_raw{h}", tag=f"u_raw{h}") for h in range(2)]
         wu_raw = [
             keep.tile([P, PACK, PACK * (m1 - m0)], F32, name=f"wu_raw{i}", tag=f"wu_raw{i}", align_bytes=64)
             for i, (a, m0, m1) in enumerate(WU_LOADS)
@@ -57,7 +61,7 @@ def tile_moe_prv_lin_silu_kernel(tc, uT, wu, w_words, w_scales, b, gate, offs, o
         bias_rows = keep.tile([P, P * E], F32, name="bias_rows")
         identity = keep.tile([P, P], F32, name="identity")
         banks = [psum.tile([P, PACK, C], F32, name=f"bank{i}") for i in range(BANKS)]
-        w_codes = [keep.tile([P, PASSES, N], U32, name=f"w_codes{e}", align_bytes=64) for e in range(E)]
+        w_codes = [keep.tile([P, PASSES, N], U32, name=f"w_codes{e}", tag=f"w_codes{e}", align_bytes=64) for e in range(E)]
         w_planes = [keep.tile([P, N], U8, name=f"w_planes{g}", align_bytes=64) for g in range(2)]
         gates = keep.tile([P, T], F32, name="gates")
 
@@ -93,11 +97,9 @@ def tile_moe_prv_lin_silu_kernel(tc, uT, wu, w_words, w_scales, b, gate, offs, o
         for e in range(E):
             nc.tensor.transpose(banks[BIAS_BANK][:, e, :], bias_rows[:].rearrange("q (p e) -> q e p", e=E)[:, e, :], identity[:])
 
-        for i in range(4):
-            h, half = divmod(i, 2)
-            nc.sync.dma_start(out=u_raw[i][:], in_=u_rows[:, 2 * h : 2 * h + 2, half * T // 2 : (half + 1) * T // 2])
-            if i == 1:
-                nc.sync.dma_start(offsets[:], offs)
+        nc.sync.dma_start(out=u_raw[0][:], in_=u_rows[:, 0:2, :])
+        nc.sync.dma_start(offsets[:], offs)
+        nc.sync.dma_start(out=u_raw[1][:], in_=u_rows[:, 2:4, :])
         for raw, (a, m0, m1) in zip(wu_raw, WU_LOADS):
             nc.sync.dma_start(out=raw[:], in_=wu_rows[:, :, a * K_PASS + PACK * m0 : a * K_PASS + PACK * m1])
         load_codes(0)
@@ -110,20 +112,20 @@ def tile_moe_prv_lin_silu_kernel(tc, uT, wu, w_words, w_scales, b, gate, offs, o
         nc.sync.dma_start(out=gates[:, 2 * C : T], in_=gate[0:P, 2 * C : T])
 
         first_pairs = keep.tile([P, T], U32, name="first_pairs")
-        shared = keep.tile([P, PACK * X_WORDS - OVERLAP + T], U32, name="shared", tag="shared", align_bytes=64)
-        u_pairs = [first_pairs[:], shared[:, PACK * X_WORDS - OVERLAP :]]
-        u_codes = keep.tile([P, T], U32, name="u_codes", align_bytes=64)
+        shared = keep.tile([P, PAIRS_FROM + T], U32, name="shared", tag="shared", align_bytes=64)
+        u_pairs = [first_pairs[:], shared[:, PAIRS_FROM:]]
+        u_codes = keep.tile([P, PAIR_SLOTS], U32, name="u_codes", align_bytes=64)
         u_scales = keep.tile([P, T], U8, name="u_scales", align_bytes=64)
-        pair_words = keep.tile([P, 2 * PAIR_SLOTS], U32, name="pair_words", align_bytes=64)
-        gathered = keep.tile([P, 2 * T], U32, name="gathered")
+        early_words = keep.tile([P, T], U32, name="early_words", align_bytes=64)
+        gathered = [keep.tile([P, T], U32, name=f"gathered{g}") for g in range(2)]
 
-        def weave(copy, words, s0, s1):
+        def weave(copy, dtype, words, s0, s1):
             copy(
-                out=words.bitcast(I32).rearrange("p (c h) -> p c h", h=2),
-                in_=gathered[:].bitcast(I32).rearrange("p (h c) -> p c h", h=2)[:, s0:s1, :],
+                out=words.bitcast(dtype).rearrange("p (c h) -> p c h", h=2),
+                in_=gathered[s0 // PAIR_SLOTS][:].bitcast(dtype).rearrange("p (h c) -> p c h", h=2),
             )
 
-        slot_codes = {e: u_codes[:, e * C : (e + 1) * C] for e in range(E)}
+        slot_codes = {e: u_codes[:, e * C : (e + 1) * C] for e in range(2)}
 
         def listed(window, s0, s1):
             return window.indirect(offsets[:, s0 // PER_COLUMN : s1 // PER_COLUMN])
@@ -131,37 +133,32 @@ def tile_moe_prv_lin_silu_kernel(tc, uT, wu, w_words, w_scales, b, gate, offs, o
         def quantise_u(words, codes, s0, s1):
             nc.vector.quantize_mx(out=codes.bitcast(FP8X4), scales=u_scales[:, s0:s1], in_=words.bitcast(BF16))
 
-        def u_views(i):
-            h, half = divmod(i, 2)
-            words = u_pairs[h][:, half * T // 2 : (half + 1) * T // 2]
-            return words.bitcast(BF16).rearrange("p (t j) -> p t j", j=2), u_raw[i][:].rearrange("p j t -> p t j")
+        def u_views(h):
+            return u_pairs[h].bitcast(BF16).rearrange("p (t j) -> p t j", j=2), u_raw[h][:].rearrange("p j t -> p t j")
 
         def gather(h):
             for s0 in range(0, T, PAIR_SLOTS):
                 s1 = s0 + PAIR_SLOTS
-                nc.vector.tensor_copy(out=gathered[:, h * T + s0 : h * T + s1], in_=listed(u_pairs[h], s0, s1))
+                nc.vector.tensor_copy(out=gathered[s0 // PAIR_SLOTS][:, h * PAIR_SLOTS : (h + 1) * PAIR_SLOTS], in_=listed(u_pairs[h], s0, s1))
 
         dst, src = u_views(0)
-        nc.scalar.copy(out=dst, in_=src)
-        dst, src = u_views(1)
         nc.scalar.copy(out=dst[:, U_VECTOR:, :], in_=src[:, U_VECTOR:, :])
         nc.vector.tensor_copy(out=dst[:, :U_VECTOR, :], in_=src[:, :U_VECTOR, :])
         gather(0)
-        dst, src = u_views(2)
-        nc.scalar.copy(out=dst, in_=src)
-        dst, src = u_views(3)
+        dst, src = u_views(1)
         nc.scalar.copy(out=dst[:, U_GPSIMD:, :], in_=src[:, U_GPSIMD:, :])
         nc.gpsimd.tensor_scalar(dst[:, :U_GPSIMD, :], src[:, :U_GPSIMD, :], 1.0, 0.0, MULT, ADD)
         gather(1)
-        bias_all = keep.tile([P, E, N_TILES], F32, name="bias_all", tag="u_raw3")
+        bias_all = keep.tile([P, E, N_TILES], F32, name="bias_all", tag="u_raw1")
         nc.scalar.copy(out=bias_all[:], in_=banks[BIAS_BANK][:, :, P - N_TILES : P])
         bias = [bias_all[:, e, :] for e in range(E)]
-        weave(nc.vector.tensor_copy, pair_words[:], 0, PAIR_SLOTS)
+        weave(nc.vector.tensor_copy, I32, early_words[:], 0, PAIR_SLOTS)
+        quantise_u(early_words[:], u_codes[:], 0, PAIR_SLOTS)
 
         def planes(words):
             return words.bitcast(BF16).rearrange("p (r m j) -> p r m j", r=PACK, j=PACK)
 
-        wu_bf = {0: planes(shared[:, 0 : PACK * X_WORDS])}
+        wu_bf = {0: planes(shared[:, 0:WU_WORDS])}
         wu_codes = [keep.tile([P, PACK, P], U32, name=f"wu_codes{a}", align_bytes=64) for a in range(PASSES)]
         wu_scales = [keep.tile([P, PACK, P], U8, name=f"wu_scales{a}", align_bytes=64) for a in range(PASSES)]
 
@@ -174,9 +171,8 @@ def tile_moe_prv_lin_silu_kernel(tc, uT, wu, w_words, w_scales, b, gate, offs, o
             dst, src = wu_views(i)
             copy(out=dst, in_=src)
 
-        def round_on_both(i):
+        def round_on_both(i, cut):
             dst, src = wu_views(i)
-            cut = P // 2 - WU_VECTOR[i]
             nc.scalar.copy(out=dst[:, :cut, :, :], in_=src[:, :cut, :, :])
             nc.vector.tensor_copy(out=dst[:, cut:, :, :], in_=src[:, cut:, :, :])
 
@@ -194,9 +190,9 @@ def tile_moe_prv_lin_silu_kernel(tc, uT, wu, w_words, w_scales, b, gate, offs, o
 
         x_bf = {}
 
-        def x_columns(e, a, passes=1):
-            first = X_ORDER.index((e, a)) * C
-            return slice(first, first + passes * C)
+        def x_operand(tiles, e, a, passes=1):
+            pair, place = X_PLACE[e, a]
+            return tiles[pair][:, place * C : (place + passes) * C]
 
         def project(e, a, copy, order=range(PACK)):
             bank = banks[X_ORDER.index((e, a))]
@@ -216,8 +212,9 @@ def tile_moe_prv_lin_silu_kernel(tc, uT, wu, w_words, w_scales, b, gate, offs, o
             )
 
         def quantise_x(e, a, passes, values):
-            columns = x_columns(e, a, passes)
-            nc.vector.quantize_mx(out=x_codes[:, columns].bitcast(FP8X4), scales=x_scales[:, columns], in_=values)
+            nc.vector.quantize_mx(
+                out=x_operand(x_codes, e, a, passes).bitcast(FP8X4), scales=x_operand(x_scales, e, a, passes), in_=values
+            )
 
         y = keep.tile([P, N_TILES, T], F32, name="y")
 
@@ -231,8 +228,8 @@ def tile_moe_prv_lin_silu_kernel(tc, uT, wu, w_words, w_scales, b, gate, offs, o
                         out=sums,
                         lhsT=w_codes[e][:, a, cols].bitcast(FP8X4),
                         lhsT_scale=w_planes[g][4 * i : P, cols],
-                        rhs=x_codes[:, x_columns(e, a)].bitcast(FP8X4),
-                        rhs_scale=x_scales[:, x_columns(e, a)],
+                        rhs=x_operand(x_codes, e, a).bitcast(FP8X4),
+                        rhs_scale=x_operand(x_scales, e, a),
                         start=(a == 0),
                         stop=(a == PASSES - 1),
                     )
@@ -254,68 +251,71 @@ def tile_moe_prv_lin_silu_kernel(tc, uT, wu, w_words, w_scales, b, gate, offs, o
         def store(nt):
             nc.sync.dma_start(out=out[nt * P : (nt + 1) * P, :], in_=results[nt][:])
 
-        round_on_both(0)
-        quantise_u(pair_words[:], u_codes[:, 0:PAIR_SLOTS], 0, PAIR_SLOTS)
-        round_on_both(1)
-        for r0, r1 in ((0, 2), (2, 3), (3, 4)):
-            quantise_wu(0, r0, r1, 0, P)
-        wu_bf1 = keep.tile([P, PACK * X_WORDS], U32, name="wu_bf1", tag="wu_raw1", align_bytes=64)
+        round_whole(nc.scalar.copy, 0)
+        round_on_both(1, WU_SCALAR)
+        late_words = keep.tile([P, T], U32, name="late_words", tag="wu_raw1", align_bytes=64)
+        weave(nc.scalar.copy, U32, late_words[:], PAIR_SLOTS, T)
+        for r in range(0, PACK, 2):
+            quantise_wu(0, r, r + 2, 0, P)
+        late_codes = keep.tile([P, PAIR_SLOTS], U32, name="late_codes", tag="shared", align_bytes=64)
+        for e in range(2, E):
+            slot_codes[e] = late_codes[:, (e - 2) * C : (e - 1) * C]
+        quantise_u(late_words[:], late_codes[:], PAIR_SLOTS, T)
+        wu_bf1 = keep.tile([P, WU_WORDS], U32, name="wu_bf1", tag="wu_raw1", align_bytes=64)
         wu_bf[1] = planes(wu_bf1[:])
-        round_on_both(2)
-        late_words = keep.tile([P, 2 * PAIR_SLOTS], U32, name="late_words", tag="shared", align_bytes=64)
-        weave(nc.vector.tensor_copy, late_words[:], PAIR_SLOTS, T)
-        round_whole(nc.vector.tensor_copy, 3)
-        quantise_u(late_words[:], u_codes[:, PAIR_SLOTS:T], PAIR_SLOTS, T)
-        for r in range(HALVED):
-            quantise_wu(1, r, r + 1, 0, P // 2)
-        round_by_planes(4)
-        x_codes = keep.tile([P, E * PASSES * C], U32, name="x_codes", tag="wu_raw4", align_bytes=64)
-        x_scales = keep.tile([P, E * PASSES * C], U8, name="x_scales", align_bytes=64)
+        round_whole(nc.vector.tensor_copy, 2)
+        round_by_planes(3)
+        x_codes = {0: keep.tile([P, 2 * PASSES * C], U32, name="x_codes0", tag="wu_raw1", align_bytes=64)}
+        x_scales = [keep.tile([P, 2 * PASSES * C], U8, name=f"x_scales{g}", align_bytes=64) for g in range(2)]
 
-        x_early = keep.tile([P, E * X_WORDS], U32, name="x_early", tag="wu_raw2", align_bytes=64)
-        x_middle = keep.tile([P, 3 * X_WORDS], U32, name="x_middle", tag="x_middle", align_bytes=64)
-        x_late = keep.tile([P, X_WORDS], U32, name="x_late", tag="x_late", align_bytes=64)
-        for tile, first, end in ((x_early, 0, 4), (x_middle, 4, 7), (x_late, 7, 8)):
-            for i, (e, a) in enumerate(X_ORDER[first:end]):
-                x_bf[e, a] = tile[:, i * X_WORDS : (i + 1) * X_WORDS].bitcast(BF16)
+        x_early = keep.tile([P, 2 * X_WORDS], U32, name="x_early", align_bytes=64)
+        x_chain = keep.tile([P, X_WORDS], U32, name="x_chain", tag="x_chain", align_bytes=64)
+        x_middle = keep.tile([P, X_WORDS], U32, name="x_middle", align_bytes=64)
+        x_late = keep.tile([P, 2 * PASSES * X_WORDS], U32, name="x_late", tag="x_late", align_bytes=64)
+        for e, a in X_ORDER:
+            pair, place = X_PLACE[e, a]
+            if pair == 1 or a == 0:
+                x_bf[e, a] = (x_early, x_late)[pair][:, place * X_WORDS : (place + 1) * X_WORDS].bitcast(BF16)
+        x_bf[0, 1] = x_chain[:].bitcast(BF16)
+        x_bf[1, 1] = x_middle[:].bitcast(BF16)
         backwards = range(PACK - 1, -1, -1)
         project(0, 0, nc.scalar.copy)
         project(1, 0, nc.scalar.copy, order=backwards)
         project(2, 0, nc.scalar.copy)
         project(3, 0, nc.scalar.copy)
-        for r in range(PACK):
-            quantise_wu(1, r, r + 1, P // 2 if r < HALVED else 0, P)
-        quantise_x(0, 0, 2, x_early[:, 0 : 2 * X_WORDS].bitcast(BF16))
-        project(0, 1, nc.scalar.copy)
-        project(1, 1, nc.vector.tensor_copy, order=backwards)
+        for r in range(0, PACK, 2):
+            quantise_wu(1, r, r + 2, 0, P)
+        quantise_x(0, 0, 2, x_early[:].bitcast(BF16))
+        project(0, 1, nc.vector.tensor_copy)
         quantise_x(0, 1, 1, x_bf[0, 1])
-        quantise_x(2, 0, 2, x_early[:, 2 * X_WORDS :].bitcast(BF16))
+        project(1, 1, nc.scalar.copy, order=backwards)
+        project(2, 1, nc.vector.tensor_copy, order=backwards)
+        project(3, 1, nc.scalar.copy, order=backwards)
         quantise_x(1, 1, 1, x_bf[1, 1])
-        project(2, 1, nc.scalar.copy, order=backwards)
-        project(3, 1, nc.vector.tensor_copy, order=backwards)
-        quantise_x(2, 1, 1, x_bf[2, 1])
+        x_codes[1] = keep.tile([P, 2 * PASSES * C], U32, name="x_codes1", align_bytes=64)
+        quantise_x(2, 0, 2 * PASSES, x_late[:].bitcast(BF16))
         expert(0)
+        results[0] = keep.tile([P, T], F32, name="results0")
         results[1] = keep.tile([P, T], F32, name="results1")
-        results[2] = keep.tile([P, T], F32, name="results2", tag="x_middle", align_bytes=64)
-        scatter_vector(2, 0, C)
-        quantise_x(3, 1, 1, x_bf[3, 1])
-        results[0] = keep.tile([P, T], F32, name="results0", tag="x_late", align_bytes=64)
+        results[2] = keep.tile([P, T], F32, name="results2", tag="x_late", align_bytes=64)
+        scatter_vector(2, 0, SHARE)
         scatter_vector(0, 0, C)
         expert(1)
         times_gate(3, 0, 2 * C)
         scatter_vector(1, 0, 2 * C)
         expert(2)
         expert(3)
-        results[3] = keep.tile([P, T], F32, name="results3", tag="u_raw3")
+        results[3] = keep.tile([P, T], F32, name="results3", tag="w_codes3", align_bytes=64)
         scatter_scalar(3, 0, 2 * C)
-        times_gate(2, C, T)
+        times_gate(2, SHARE, T)
         times_gate(3, 2 * C, T)
+        scatter_scalar(2, SHARE, 2 * C)
         scatter_vector(0, 3 * C, T)
-        scatter_scalar(2, C, T)
-        store(2)
         scatter_vector(1, 2 * C, T)
         store(1)
-        scatter_vector(0, C, 3 * C)
-        store(0)
         scatter_scalar(3, 2 * C, T)
         store(3)
+        scatter_vector(0, C, 3 * C)
+        store(0)
+        scatter_scalar(2, 2 * C, T)
+        store(2)

@@ -27,37 +27,26 @@ BANKS = 8
 PER_COLUMN = 16
 PLANES_A_TILE = 4
 PAIR_SLOTS = 2 * C
-OVERLAP = 16
 X_WORDS = C * PACK // 2
-
-WU_WORDS = PACK * X_WORDS
-PAIRS_FROM = WU_WORDS - OVERLAP
-
 U_VECTOR = 336
 U_GPSIMD = 224
-WU_SCALAR = 24
-
-WU_LOADS = tuple((a, m0, m0 + P // 2) for a in range(PASSES) for m0 in (0, P // 2))
-
-X_ORDER = tuple((e, a) for a in range(PASSES) for e in range(E))
-X_PLACE = {(e, a): (e // 2, 2 * a + e % 2) for e, a in X_ORDER}
-BIAS_BANK = BANKS - 1
 SHARE = 64
+BIAS_BANK = BANKS - 1
 TILE_ORDER = ((2, 0, 3, 1), (3, 1, 0, 2), (0, 1, 2, 3), (2, 3, 0, 1))
+WU_LOADS = ((0, 0, P), (1, 0, P // 2), (1, P // 2, P))
+HALF = 2048
 
 
 def tile_moe_prv_lin_silu_kernel(tc, uT, wu, w_words, w_scales, b, gate, offs, out):
     nc = tc.nc
     with ExitStack() as ctx:
         keep = ctx.enter_context(tc.tile_pool(name="keep", bufs=1))
+        placed = ctx.enter_context(tc.tile_pool(name="placed", bufs=1))
         psum = ctx.enter_context(tc.psum_pool(name="psum", bufs=1))
 
         offsets = keep.tile([P, T // PER_COLUMN], U16, name="offsets")
         u_raw = [keep.tile([P, 2, T], F32, name=f"u_raw{h}", tag=f"u_raw{h}") for h in range(2)]
-        wu_raw = [
-            keep.tile([P, PACK, PACK * (m1 - m0)], F32, name=f"wu_raw{i}", tag=f"wu_raw{i}", align_bytes=64)
-            for i, (a, m0, m1) in enumerate(WU_LOADS)
-        ]
+        wu_raw = [keep.tile([P, PACK, PACK * (m1 - m0)], F32, name=f"wu_raw{i}", align_bytes=64) for i, (a, m0, m1) in enumerate(WU_LOADS)]
         bias_rows = keep.tile([P, P * E], F32, name="bias_rows")
         identity = keep.tile([P, P], F32, name="identity")
         banks = [psum.tile([P, PACK, C], F32, name=f"bank{i}") for i in range(BANKS)]
@@ -66,12 +55,10 @@ def tile_moe_prv_lin_silu_kernel(tc, uT, wu, w_words, w_scales, b, gate, offs, o
         gates = keep.tile([P, T], F32, name="gates")
 
         nc.scalar.dma_start(out=bias_rows[P - N_TILES : P, :], in_=b.rearrange("(nt p) e -> nt (p e)", p=P))
-
         warm_in = keep.tile([P, 1], F32, name="warm_in")
         warm_out = keep.tile([P, 1], F32, name="warm_out")
         nc.vector.memset(warm_in[:], 0.0)
         nc.scalar.activation(out=warm_out[:], in_=warm_in[:], func=SILU)
-
         nc.vector.memset(bias_rows[0 : P - N_TILES, :].bitcast(I32), 0)
         make_identity(nc, identity[:])
         for g in range(2):
@@ -82,10 +69,7 @@ def tile_moe_prv_lin_silu_kernel(tc, uT, wu, w_words, w_scales, b, gate, offs, o
         scale_rows = w_scales.rearrange("e a q n -> (e a) q n")
 
         def load_codes(e):
-            nc.sync.dma_start(
-                out=w_codes[e][:].bitcast(I32),
-                in_=w_words[e].rearrange("a p n r -> p a (n r)").bitcast(I32),
-            )
+            nc.sync.dma_start(out=w_codes[e][:].bitcast(I32), in_=w_words[e].rearrange("a p n r -> p a (n r)").bitcast(I32))
 
         def load_planes(g):
             for quadrant in range(4):
@@ -104,143 +88,157 @@ def tile_moe_prv_lin_silu_kernel(tc, uT, wu, w_words, w_scales, b, gate, offs, o
             nc.sync.dma_start(out=raw[:], in_=wu_rows[:, :, a * K_PASS + PACK * m0 : a * K_PASS + PACK * m1])
         load_codes(0)
         load_planes(0)
-        nc.sync.dma_start(out=gates[:, 0 : 2 * C], in_=gate[0:P, 0 : 2 * C])
         load_codes(1)
-        load_planes(1)
+        nc.sync.dma_start(out=gates[:, 0 : 2 * C], in_=gate[0:P, 0 : 2 * C])
         load_codes(2)
+        load_planes(1)
         load_codes(3)
         nc.sync.dma_start(out=gates[:, 2 * C : T], in_=gate[0:P, 2 * C : T])
 
-        first_pairs = keep.tile([P, T], U32, name="first_pairs")
-        shared = keep.tile([P, PAIRS_FROM + T], U32, name="shared", tag="shared", align_bytes=64)
-        u_pairs = [first_pairs[:], shared[:, PAIRS_FROM:]]
-        u_codes = keep.tile([P, PAIR_SLOTS], U32, name="u_codes", align_bytes=64)
-        u_scales = keep.tile([P, T], U8, name="u_scales", align_bytes=64)
-        early_words = keep.tile([P, T], U32, name="early_words", align_bytes=64)
-        gathered = [keep.tile([P, T], U32, name=f"gathered{g}") for g in range(2)]
+        def place(name, words, offset):
+            return placed.tile([P, words], U32, name=name, offset=offset, align_bytes=64)
 
-        def weave(copy, dtype, words, s0, s1):
-            copy(
-                out=words.bitcast(dtype).rearrange("p (c h) -> p c h", h=2),
-                in_=gathered[s0 // PAIR_SLOTS][:].bitcast(dtype).rearrange("p (h c) -> p c h", h=2),
-            )
-
-        slot_codes = {e: u_codes[:, e * C : (e + 1) * C] for e in range(2)}
+        u_pairs = [keep.tile([P, T], U32, name="u_pairs0"), place("u_pairs1", T, HALF + HALF // 2)]
+        gathered = [keep.tile([P, 2 * slots], U32, name=f"gathered{g}") for g, slots in enumerate((PAIR_SLOTS, C))]
+        u_words = [keep.tile([P, T], U32, name=f"u_words{g}", align_bytes=64) for g in range(2)]
+        u_codes = [keep.tile([P, PAIR_SLOTS], U32, name=f"u_codes{g}", align_bytes=64) for g in range(2)]
+        u_scales = [keep.tile([P, PAIR_SLOTS], U8, name=f"u_scales{g}", align_bytes=64) for g in range(2)]
 
         def listed(window, s0, s1):
             return window.indirect(offsets[:, s0 // PER_COLUMN : s1 // PER_COLUMN])
 
-        def quantise_u(words, codes, s0, s1):
-            nc.vector.quantize_mx(out=codes.bitcast(FP8X4), scales=u_scales[:, s0:s1], in_=words.bitcast(BF16))
-
         def u_views(h):
-            return u_pairs[h].bitcast(BF16).rearrange("p (t j) -> p t j", j=2), u_raw[h][:].rearrange("p j t -> p t j")
+            return u_pairs[h][:].bitcast(BF16).rearrange("p (t j) -> p t j", j=2), u_raw[h][:].rearrange("p j t -> p t j")
+
+        last_rows = keep.tile([P, PACK, C], F32, name="last_rows")
 
         def gather(h):
-            for s0 in range(0, T, PAIR_SLOTS):
-                s1 = s0 + PAIR_SLOTS
-                nc.vector.tensor_copy(out=gathered[s0 // PAIR_SLOTS][:, h * PAIR_SLOTS : (h + 1) * PAIR_SLOTS], in_=listed(u_pairs[h], s0, s1))
+            for g, slots in enumerate((PAIR_SLOTS, C)):
+                s0 = g * PAIR_SLOTS
+                nc.vector.tensor_copy(out=gathered[g][:, h * slots : (h + 1) * slots], in_=listed(u_pairs[h][:], s0, s0 + slots))
+
+        def gather_last(h):
+            for j in range(2):
+                nc.scalar.activation(last_rows[:, 2 * h + j, :], listed(u_raw[h][:, j, :], T - C, T), COPY)
+
+        def weave(g):
+            words = gathered[g].shape[1]
+            nc.vector.tensor_copy(
+                out=u_words[g][:, 0:words].bitcast(I32).rearrange("p (c h) -> p c h", h=2),
+                in_=gathered[g][:].bitcast(I32).rearrange("p (h c) -> p c h", h=2),
+            )
+
+        def quantise_u(g):
+            nc.vector.quantize_mx(out=u_codes[g][:].bitcast(FP8X4), scales=u_scales[g][:], in_=u_words[g][:].bitcast(BF16))
 
         dst, src = u_views(0)
         nc.scalar.copy(out=dst[:, U_VECTOR:, :], in_=src[:, U_VECTOR:, :])
         nc.vector.tensor_copy(out=dst[:, :U_VECTOR, :], in_=src[:, :U_VECTOR, :])
+        gather_last(0)
         gather(0)
         dst, src = u_views(1)
         nc.scalar.copy(out=dst[:, U_GPSIMD:, :], in_=src[:, U_GPSIMD:, :])
         nc.gpsimd.tensor_scalar(dst[:, :U_GPSIMD, :], src[:, :U_GPSIMD, :], 1.0, 0.0, MULT, ADD)
+        gather_last(1)
+        nc.scalar.copy(
+            out=u_words[1][:, X_WORDS:].bitcast(BF16).rearrange("p (c i j) -> p c j i", i=PACK, j=PACK),
+            in_=last_rows[:].rearrange("p j (c i) -> p c j i", i=PACK),
+        )
         gather(1)
         bias_all = keep.tile([P, E, N_TILES], F32, name="bias_all", tag="u_raw1")
         nc.scalar.copy(out=bias_all[:], in_=banks[BIAS_BANK][:, :, P - N_TILES : P])
-        bias = [bias_all[:, e, :] for e in range(E)]
-        weave(nc.vector.tensor_copy, I32, early_words[:], 0, PAIR_SLOTS)
-        quantise_u(early_words[:], u_codes[:], 0, PAIR_SLOTS)
+        weave(0)
+        weave(1)
 
-        def planes(words):
-            return words.bitcast(BF16).rearrange("p (r m j) -> p r m j", r=PACK, j=PACK)
-
-        wu_bf = {0: planes(shared[:, 0:WU_WORDS])}
-        wu_codes = [keep.tile([P, PACK, P], U32, name=f"wu_codes{a}", align_bytes=64) for a in range(PASSES)]
+        wu_bf = {
+            (0, 0): place("wu_bf00", T, HALF),
+            (0, 1): keep.tile([P, T], U32, name="wu_bf01", align_bytes=64),
+        }
+        wu_codes = [
+            place("wu_codes0", T, 2 * HALF + 64)[:].rearrange("p (r m) -> p r m", r=PACK),
+            keep.tile([P, PACK, P], U32, name="wu_codes1", align_bytes=64),
+        ]
         wu_scales = [keep.tile([P, PACK, P], U8, name=f"wu_scales{a}", align_bytes=64) for a in range(PASSES)]
 
-        def wu_views(i):
+        def round_wu(copy, i, half, c0, c1):
             a, m0, m1 = WU_LOADS[i]
-            dst = wu_bf[a][:, :, m0:m1, :].rearrange("p r m j -> p m j r")
-            return dst, wu_raw[i][:].rearrange("p j (m r) -> p m j r", r=PACK)
+            dst = wu_bf[a, half][:].bitcast(BF16).rearrange("p (r m j) -> p m j r", r=2, j=PACK)[:, m0 + c0 : m0 + c1]
+            copy(out=dst, in_=wu_raw[i][:].rearrange("p j (m r) -> p m j r", r=PACK)[:, c0:c1, :, 2 * half : 2 * half + 2])
 
-        def round_whole(copy, i):
-            dst, src = wu_views(i)
-            copy(out=dst, in_=src)
-
-        def round_on_both(i, cut):
-            dst, src = wu_views(i)
-            nc.scalar.copy(out=dst[:, :cut, :, :], in_=src[:, :cut, :, :])
-            nc.vector.tensor_copy(out=dst[:, cut:, :, :], in_=src[:, cut:, :, :])
-
-        def round_by_planes(i):
-            dst, src = wu_views(i)
-            for r in range(0, PACK, 2):
-                nc.vector.tensor_copy(out=dst[:, :, :, r : r + 2], in_=src[:, :, :, r : r + 2])
-
-        def quantise_wu(a, r0, r1, m0, m1):
+        def quantise_wu(a, half):
             nc.vector.quantize_mx(
-                out=wu_codes[a][:, r0:r1, m0:m1].rearrange("p r m -> p (r m)").bitcast(FP8X4),
-                scales=wu_scales[a][:, r0:r1, m0:m1].rearrange("p r m -> p (r m)"),
-                in_=wu_bf[a][:, r0:r1, m0:m1, :].rearrange("p r m j -> p (r m j)"),
+                out=wu_codes[a][:, 2 * half : 2 * half + 2, :].rearrange("p r m -> p (r m)").bitcast(FP8X4),
+                scales=wu_scales[a][:, 2 * half : 2 * half + 2, :].rearrange("p r m -> p (r m)"),
+                in_=wu_bf[a, half][:].bitcast(BF16),
             )
 
-        x_bf = {}
+        round_wu(nc.scalar.copy, 0, 1, 0, P)
+        round_wu(nc.vector.tensor_copy, 0, 0, 0, P)
+        quantise_u(0)
+        quantise_wu(0, 0)
+        quantise_wu(0, 1)
+        wu_bf[1, 0] = place("wu_bf10", T, 64)
+        wu_bf[1, 1] = keep.tile([P, T], U32, name="wu_bf11", align_bytes=64)
+        round_wu(nc.vector.tensor_copy, 1, 0, 0, P // 2)
+        quantise_u(1)
+        round_wu(nc.scalar.copy, 1, 1, 0, P // 2)
+        for half in range(2):
+            round_wu(nc.vector.tensor_copy, 2, half, 0, P // 2)
 
-        def x_operand(tiles, e, a, passes=1):
-            pair, place = X_PLACE[e, a]
-            return tiles[pair][:, place * C : (place + passes) * C]
+        groups = (((0, 0), (1, 0)), ((2, 0), (3, 0)), ((0, 1),), ((1, 1),), ((2, 1), (3, 1)))
+        x_bf = [keep.tile([P, len(gr) * X_WORDS], U32, name=f"x_bf{i}", tag=f"x_bf{i}", align_bytes=64) for i, gr in enumerate(groups)]
+        x_scales = [keep.tile([P, len(gr) * C], U8, name=f"x_scales{i}", align_bytes=64) for i, gr in enumerate(groups)]
+        x_codes = {}
+        where = {ea: (i, n) for i, gr in enumerate(groups) for n, ea in enumerate(gr)}
 
-        def project(e, a, copy, order=range(PACK)):
-            bank = banks[X_ORDER.index((e, a))]
+        def project(e, a, copy, order):
+            bank = banks[a * E + e]
             for r in order:
                 nc.tensor.matmul_mx(
                     out=bank[:, r, :],
                     lhsT=wu_codes[a][:, r, :].bitcast(FP8X4),
                     lhsT_scale=wu_scales[a][:, r, :],
-                    rhs=slot_codes[e].bitcast(FP8X4),
-                    rhs_scale=u_scales[:, e * C : (e + 1) * C],
+                    rhs=u_codes[e // 2][:, (e % 2) * C : (e % 2 + 1) * C].bitcast(FP8X4),
+                    rhs_scale=u_scales[e // 2][:, (e % 2) * C : (e % 2 + 1) * C],
                     start=True,
                     stop=True,
                 )
+            i, n = where[e, a]
             copy(
-                out=x_bf[e, a].rearrange("p (c r) -> p c r", r=PACK),
+                out=x_bf[i][:, n * X_WORDS : (n + 1) * X_WORDS].bitcast(BF16).rearrange("p (c r) -> p c r", r=PACK),
                 in_=bank[:].rearrange("p r c -> p c r"),
             )
 
-        def quantise_x(e, a, passes, values):
-            nc.vector.quantize_mx(
-                out=x_operand(x_codes, e, a, passes).bitcast(FP8X4), scales=x_operand(x_scales, e, a, passes), in_=values
-            )
+        def quantise_x(i):
+            if i not in x_codes:
+                x_codes[i] = keep.tile([P, len(groups[i]) * C], U32, name=f"x_codes{i}", align_bytes=64)
+            nc.vector.quantize_mx(out=x_codes[i][:].bitcast(FP8X4), scales=x_scales[i][:], in_=x_bf[i][:].bitcast(BF16))
 
         y = keep.tile([P, N_TILES, T], F32, name="y")
 
         def expert(e):
-            for place, nt in enumerate(TILE_ORDER[e]):
+            for spot, nt in enumerate(TILE_ORDER[e]):
                 cols = slice(nt * P, (nt + 1) * P)
-                sums = banks[(e * N_TILES + place) % BANKS][:, 0, :]
+                sums = banks[(e * N_TILES + spot) % BANKS][:, 0, :]
                 for a in range(PASSES):
                     g, i = divmod(e * PASSES + a, PLANES_A_TILE)
+                    xi, n = where[e, a]
                     nc.tensor.matmul_mx(
                         out=sums,
                         lhsT=w_codes[e][:, a, cols].bitcast(FP8X4),
                         lhsT_scale=w_planes[g][4 * i : P, cols],
-                        rhs=x_operand(x_codes, e, a).bitcast(FP8X4),
-                        rhs_scale=x_operand(x_scales, e, a),
+                        rhs=x_codes[xi][:, n * C : (n + 1) * C].bitcast(FP8X4),
+                        rhs_scale=x_scales[xi][:, n * C : (n + 1) * C],
                         start=(a == 0),
                         stop=(a == PASSES - 1),
                     )
-                nc.scalar.activation(out=y[:, nt, e * C : (e + 1) * C], in_=sums, func=SILU, bias=bias[e][:, nt : nt + 1])
+                nc.scalar.activation(out=y[:, nt, e * C : (e + 1) * C], in_=sums, func=SILU, bias=bias_all[:, e, nt : nt + 1])
 
         results = {}
+        gated = keep.tile([P, 2, T], F32, name="gated")
 
         def scatter_vector(nt, s0, s1):
             nc.vector.tensor_tensor(listed(results[nt][:], s0, s1), y[:, nt, s0:s1], gates[:, s0:s1], MULT)
-
-        gated = keep.tile([P, 2, T], F32, name="gated")
 
         def times_gate(nt, s0, s1):
             nc.vector.tensor_tensor(gated[:, nt - 2, s0:s1], y[:, nt, s0:s1], gates[:, s0:s1], MULT)
@@ -251,53 +249,28 @@ def tile_moe_prv_lin_silu_kernel(tc, uT, wu, w_words, w_scales, b, gate, offs, o
         def store(nt):
             nc.sync.dma_start(out=out[nt * P : (nt + 1) * P, :], in_=results[nt][:])
 
-        round_whole(nc.scalar.copy, 0)
-        round_on_both(1, WU_SCALAR)
-        late_words = keep.tile([P, T], U32, name="late_words", tag="wu_raw1", align_bytes=64)
-        weave(nc.scalar.copy, U32, late_words[:], PAIR_SLOTS, T)
-        for r in range(0, PACK, 2):
-            quantise_wu(0, r, r + 2, 0, P)
-        late_codes = keep.tile([P, PAIR_SLOTS], U32, name="late_codes", tag="shared", align_bytes=64)
-        for e in range(2, E):
-            slot_codes[e] = late_codes[:, (e - 2) * C : (e - 1) * C]
-        quantise_u(late_words[:], late_codes[:], PAIR_SLOTS, T)
-        wu_bf1 = keep.tile([P, WU_WORDS], U32, name="wu_bf1", tag="wu_raw1", align_bytes=64)
-        wu_bf[1] = planes(wu_bf1[:])
-        round_whole(nc.vector.tensor_copy, 2)
-        round_by_planes(3)
-        x_codes = {0: keep.tile([P, 2 * PASSES * C], U32, name="x_codes0", tag="wu_raw1", align_bytes=64)}
-        x_scales = [keep.tile([P, 2 * PASSES * C], U8, name=f"x_scales{g}", align_bytes=64) for g in range(2)]
-
-        x_early = keep.tile([P, 2 * X_WORDS], U32, name="x_early", align_bytes=64)
-        x_chain = keep.tile([P, X_WORDS], U32, name="x_chain", tag="x_chain", align_bytes=64)
-        x_middle = keep.tile([P, X_WORDS], U32, name="x_middle", align_bytes=64)
-        x_late = keep.tile([P, 2 * PASSES * X_WORDS], U32, name="x_late", tag="x_late", align_bytes=64)
-        for e, a in X_ORDER:
-            pair, place = X_PLACE[e, a]
-            if pair == 1 or a == 0:
-                x_bf[e, a] = (x_early, x_late)[pair][:, place * X_WORDS : (place + 1) * X_WORDS].bitcast(BF16)
-        x_bf[0, 1] = x_chain[:].bitcast(BF16)
-        x_bf[1, 1] = x_middle[:].bitcast(BF16)
+        forwards = range(PACK)
         backwards = range(PACK - 1, -1, -1)
-        project(0, 0, nc.scalar.copy)
-        project(1, 0, nc.scalar.copy, order=backwards)
-        project(2, 0, nc.scalar.copy)
-        project(3, 0, nc.scalar.copy)
-        for r in range(0, PACK, 2):
-            quantise_wu(1, r, r + 2, 0, P)
-        quantise_x(0, 0, 2, x_early[:].bitcast(BF16))
-        project(0, 1, nc.vector.tensor_copy)
-        quantise_x(0, 1, 1, x_bf[0, 1])
-        project(1, 1, nc.scalar.copy, order=backwards)
-        project(2, 1, nc.vector.tensor_copy, order=backwards)
-        project(3, 1, nc.scalar.copy, order=backwards)
-        quantise_x(1, 1, 1, x_bf[1, 1])
-        x_codes[1] = keep.tile([P, 2 * PASSES * C], U32, name="x_codes1", align_bytes=64)
-        quantise_x(2, 0, 2 * PASSES, x_late[:].bitcast(BF16))
+        project(0, 0, nc.scalar.copy, forwards)
+        project(1, 0, nc.scalar.copy, backwards)
+        project(2, 0, nc.scalar.copy, forwards)
+        project(3, 0, nc.scalar.copy, forwards)
+        quantise_wu(1, 0)
+        quantise_wu(1, 1)
+        x_codes[0] = place("x_codes0", PAIR_SLOTS, 64)
+        quantise_x(0)
+        project(0, 1, nc.vector.tensor_copy, forwards)
+        quantise_x(1)
+        quantise_x(2)
+        project(1, 1, nc.scalar.copy, backwards)
+        project(2, 1, nc.vector.tensor_copy, backwards)
+        project(3, 1, nc.scalar.copy, backwards)
+        quantise_x(3)
+        quantise_x(4)
         expert(0)
         results[0] = keep.tile([P, T], F32, name="results0")
         results[1] = keep.tile([P, T], F32, name="results1")
-        results[2] = keep.tile([P, T], F32, name="results2", tag="x_late", align_bytes=64)
+        results[2] = keep.tile([P, T], F32, name="results2", tag="x_bf3", align_bytes=64)
         scatter_vector(2, 0, SHARE)
         scatter_vector(0, 0, C)
         expert(1)

@@ -34,6 +34,7 @@ SHARE = 64
 BIAS_BANK = BANKS - 1
 TILE_ORDER = ((2, 0, 3, 1), (3, 1, 0, 2), (0, 1, 2, 3), (2, 3, 0, 1))
 WU_LOADS = ((0, 0, P), (1, 0, P // 2), (1, P // 2, P))
+LINE = 256
 HALF = 2048
 
 
@@ -45,14 +46,14 @@ def tile_moe_prv_lin_silu_kernel(tc, uT, wu, w_words, w_scales, b, gate, offs, o
         psum = ctx.enter_context(tc.psum_pool(name="psum", bufs=1))
 
         offsets = keep.tile([P, T // PER_COLUMN], U16, name="offsets")
-        u_raw = [keep.tile([P, 2, T], F32, name=f"u_raw{h}", tag=f"u_raw{h}") for h in range(2)]
-        wu_raw = [keep.tile([P, PACK, PACK * (m1 - m0)], F32, name=f"wu_raw{i}", align_bytes=64) for i, (a, m0, m1) in enumerate(WU_LOADS)]
-        bias_rows = keep.tile([P, P * E], F32, name="bias_rows")
+        u_raw = [keep.tile([P, 2, T], F32, name=f"u_raw{h}", tag=f"u_raw{h}", align_bytes=LINE) for h in range(2)]
+        wu_raw = [keep.tile([P, PACK, PACK * (m1 - m0)], F32, name=f"wu_raw{i}", align_bytes=LINE) for i, (a, m0, m1) in enumerate(WU_LOADS)]
+        bias_rows = keep.tile([P, P * E], F32, name="bias_rows", align_bytes=LINE)
         identity = keep.tile([P, P], F32, name="identity")
         banks = [psum.tile([P, PACK, C], F32, name=f"bank{i}") for i in range(BANKS)]
-        w_codes = [keep.tile([P, PASSES, N], U32, name=f"w_codes{e}", tag=f"w_codes{e}", align_bytes=64) for e in range(E)]
-        w_planes = [keep.tile([P, N], U8, name=f"w_planes{g}", align_bytes=64) for g in range(2)]
-        gates = keep.tile([P, T], F32, name="gates")
+        w_codes = [keep.tile([P, PASSES, N], U32, name=f"w_codes{e}", tag=f"w_codes{e}", align_bytes=LINE) for e in range(E)]
+        w_planes = [keep.tile([P, N], U8, name=f"w_planes{g}", align_bytes=LINE) for g in range(2)]
+        gates = keep.tile([P, T], F32, name="gates", align_bytes=LINE)
 
         nc.scalar.dma_start(out=bias_rows[P - N_TILES : P, :], in_=b.rearrange("(nt p) e -> nt (p e)", p=P))
         warm_in = keep.tile([P, 1], F32, name="warm_in")
@@ -145,7 +146,7 @@ def tile_moe_prv_lin_silu_kernel(tc, uT, wu, w_words, w_scales, b, gate, offs, o
             in_=last_rows[:].rearrange("p j (c i) -> p c j i", i=PACK),
         )
         gather(1)
-        bias_all = keep.tile([P, E, N_TILES], F32, name="bias_all", tag="u_raw1")
+        bias_all = keep.tile([P, E, N_TILES], F32, name="bias_all", tag="u_raw1", align_bytes=LINE)
         nc.scalar.copy(out=bias_all[:], in_=banks[BIAS_BANK][:, :, P - N_TILES : P])
         weave(0)
         weave(1)
@@ -186,7 +187,7 @@ def tile_moe_prv_lin_silu_kernel(tc, uT, wu, w_words, w_scales, b, gate, offs, o
             round_wu(nc.vector.tensor_copy, 2, half, 0, P // 2)
 
         groups = (((0, 0), (1, 0)), ((2, 0), (3, 0)), ((0, 1),), ((1, 1),), ((2, 1), (3, 1)))
-        x_bf = [keep.tile([P, len(gr) * X_WORDS], U32, name=f"x_bf{i}", tag=f"x_bf{i}", align_bytes=64) for i, gr in enumerate(groups)]
+        x_bf = [keep.tile([P, len(gr) * X_WORDS], U32, name=f"x_bf{i}", tag=f"x_bf{i}", align_bytes=LINE) for i, gr in enumerate(groups)]
         x_scales = [keep.tile([P, len(gr) * C], U8, name=f"x_scales{i}", align_bytes=64) for i, gr in enumerate(groups)]
         x_codes = {}
         where = {ea: (i, n) for i, gr in enumerate(groups) for n, ea in enumerate(gr)}
@@ -268,9 +269,9 @@ def tile_moe_prv_lin_silu_kernel(tc, uT, wu, w_words, w_scales, b, gate, offs, o
         quantise_x(3)
         quantise_x(4)
         expert(0)
-        results[0] = keep.tile([P, T], F32, name="results0")
-        results[1] = keep.tile([P, T], F32, name="results1")
-        results[2] = keep.tile([P, T], F32, name="results2", tag="x_bf3", align_bytes=64)
+        results[0] = keep.tile([P, T], F32, name="results0", align_bytes=LINE)
+        results[1] = keep.tile([P, T], F32, name="results1", align_bytes=LINE)
+        results[2] = keep.tile([P, T], F32, name="results2", tag="x_bf3", align_bytes=LINE)
         scatter_vector(2, 0, SHARE)
         scatter_vector(0, 0, C)
         expert(1)
@@ -278,7 +279,7 @@ def tile_moe_prv_lin_silu_kernel(tc, uT, wu, w_words, w_scales, b, gate, offs, o
         scatter_vector(1, 0, 2 * C)
         expert(2)
         expert(3)
-        results[3] = keep.tile([P, T], F32, name="results3", tag="w_codes3", align_bytes=64)
+        results[3] = keep.tile([P, T], F32, name="results3", tag="w_codes3", align_bytes=LINE)
         scatter_scalar(3, 0, 2 * C)
         times_gate(2, SHARE, T)
         times_gate(3, 2 * C, T)

from contextlib import ExitStack

import concourse.mybir as mybir
from concourse.masks import make_identity

F, K, T, E, C, N = 512, 1024, 512, 4, 128, 512
FLOPS = 2 * F * K * T + 2 * K * N * E * C

F32 = mybir.dt.float32
BF16 = mybir.dt.bfloat16
I32 = mybir.dt.int32
U32 = mybir.dt.uint32
U16 = mybir.dt.uint16
U8 = mybir.dt.uint8
FP8X4 = mybir.dt.float8_e4m3fn_x4
SILU = mybir.ActivationFunctionType.Silu
COPY = mybir.ActivationFunctionType.Copy
MULT = mybir.AluOpType.mult
ADD = mybir.AluOpType.add

P = 128
PACK = 4
K_PASS = P * PACK
PASSES = K // K_PASS
N_TILES = N // P
BANKS = 8
PER_COLUMN = 16
PLANES_A_TILE = 4
PAIR_SLOTS = 2 * C
X_WORDS = C * PACK // 2
U_VECTOR = 336
U_GPSIMD = 224
SHARE = 64
BIAS_BANK = BANKS - 1
TILE_ORDER = ((2, 0, 3, 1), (3, 1, 0, 2), (0, 1, 2, 3), (2, 3, 0, 1))
WU_LOADS = ((0, 0, P), (1, 0, P // 2), (1, P // 2, P))
LINE = 256
HALF = 2048


def tile_moe_prv_lin_silu_kernel(tc, uT, wu, w_words, w_scales, b, gate, offs, out):
    nc = tc.nc
    with ExitStack() as ctx:
        keep = ctx.enter_context(tc.tile_pool(name="keep", bufs=1))
        placed = ctx.enter_context(tc.tile_pool(name="placed", bufs=1))
        psum = ctx.enter_context(tc.psum_pool(name="psum", bufs=1))

        offsets = keep.tile([P, T // PER_COLUMN], U16, name="offsets")
        u_raw = [keep.tile([P, 2, T], F32, name=f"u_raw{h}", tag=f"u_raw{h}", align_bytes=LINE) for h in range(2)]
        wu_raw = [keep.tile([P, PACK, PACK * (m1 - m0)], F32, name=f"wu_raw{i}", align_bytes=LINE) for i, (a, m0, m1) in enumerate(WU_LOADS)]
        bias_rows = keep.tile([P, P * E], F32, name="bias_rows", align_bytes=LINE)
        identity = keep.tile([P, P], F32, name="identity")
        banks = [psum.tile([P, PACK, C], F32, name=f"bank{i}") for i in range(BANKS)]
        w_codes = [keep.tile([P, PASSES, N], U32, name=f"w_codes{e}", tag=f"w_codes{e}", align_bytes=LINE) for e in range(E)]
        w_planes = [keep.tile([P, N], U8, name=f"w_planes{g}", align_bytes=LINE) for g in range(2)]
        gates = keep.tile([P, T], F32, name="gates", align_bytes=LINE)

        nc.scalar.dma_start(out=bias_rows[P - N_TILES : P, :], in_=b.rearrange("(nt p) e -> nt (p e)", p=P))
        warm_in = keep.tile([P, 1], F32, name="warm_in")
        warm_out = keep.tile([P, 1], F32, name="warm_out")
        nc.vector.memset(warm_in[:], 0.0)
        nc.scalar.activation(out=warm_out[:], in_=warm_in[:], func=SILU)
        nc.vector.memset(bias_rows[0 : P - N_TILES, :].bitcast(I32), 0)
        make_identity(nc, identity[:])
        for g in range(2):
            nc.vector.memset(w_planes[g][:].bitcast(I32), 0)

        u_rows = uT.rearrange("(p j) t -> p j t", j=PACK)
        wu_rows = wu.rearrange("(p j) k -> p j k", j=PACK)
        scale_rows = w_scales.rearrange("e a q n -> (e a) q n")

        def load_codes(e):
            nc.sync.dma_start(out=w_codes[e][:].bitcast(I32), in_=w_words[e].rearrange("a p n r -> p a (n r)").bitcast(I32))

        def load_planes(g):
            for quadrant in range(4):
                nc.sync.dma_start(
                    out=w_planes[g][32 * quadrant : 32 * quadrant + 4 * PLANES_A_TILE, :].bitcast(I32),
                    in_=scale_rows[PLANES_A_TILE * g : PLANES_A_TILE * (g + 1), 4 * quadrant : 4 * quadrant + 4, :].bitcast(I32),
                )

        for e in range(E):
            nc.tensor.transpose(banks[BIAS_BANK][:, e, :], bias_rows[:].rearrange("q (p e) -> q e p", e=E)[:, e, :], identity[:])

        nc.sync.dma_start(out=u_raw[0][:], in_=u_rows[:, 0:2, :])
        nc.sync.dma_start(offsets[:], offs)
        nc.sync.dma_start(out=u_raw[1][:], in_=u_rows[:, 2:4, :])
        for raw, (a, m0, m1) in zip(wu_raw, WU_LOADS):
            nc.sync.dma_start(out=raw[:], in_=wu_rows[:, :, a * K_PASS + PACK * m0 : a * K_PASS + PACK * m1])
        load_codes(0)
        load_planes(0)
        load_codes(1)
        nc.sync.dma_start(out=gates[:, 0 : 2 * C], in_=gate[0:P, 0 : 2 * C])
        load_codes(2)
        load_planes(1)
        load_codes(3)
        nc.sync.dma_start(out=gates[:, 2 * C : T], in_=gate[0:P, 2 * C : T])

        def place(name, words, offset):
            return placed.tile([P, words], U32, name=name, offset=offset, align_bytes=64)

        u_pairs = [keep.tile([P, T], U32, name="u_pairs0"), place("u_pairs1", T, HALF + HALF // 2)]
        gathered = [keep.tile([P, 2 * slots], U32, name=f"gathered{g}") for g, slots in enumerate((PAIR_SLOTS, C))]
        u_words = [keep.tile([P, T], U32, name=f"u_words{g}", align_bytes=64) for g in range(2)]
        u_codes = [keep.tile([P, PAIR_SLOTS], U32, name=f"u_codes{g}", align_bytes=64) for g in range(2)]
        u_scales = [keep.tile([P, PAIR_SLOTS], U8, name=f"u_scales{g}", align_bytes=64) for g in range(2)]

        def listed(window, s0, s1):
            return window.indirect(offsets[:, s0 // PER_COLUMN : s1 // PER_COLUMN])

        def u_views(h):
            return u_pairs[h][:].bitcast(BF16).rearrange("p (t j) -> p t j", j=2), u_raw[h][:].rearrange("p j t -> p t j")

        last_rows = keep.tile([P, PACK, C], F32, name="last_rows")

        def gather(h):
            for g, slots in enumerate((PAIR_SLOTS, C)):
                s0 = g * PAIR_SLOTS
                nc.vector.tensor_copy(out=gathered[g][:, h * slots : (h + 1) * slots], in_=listed(u_pairs[h][:], s0, s0 + slots))

        def gather_last(h):
            for j in range(2):
                nc.scalar.activation(last_rows[:, 2 * h + j, :], listed(u_raw[h][:, j, :], T - C, T), COPY)

        def weave(g):
            words = gathered[g].shape[1]
            nc.vector.tensor_copy(
                out=u_words[g][:, 0:words].bitcast(I32).rearrange("p (c h) -> p c h", h=2),
                in_=gathered[g][:].bitcast(I32).rearrange("p (h c) -> p c h", h=2),
            )

        def quantise_u(g):
            nc.vector.quantize_mx(out=u_codes[g][:].bitcast(FP8X4), scales=u_scales[g][:], in_=u_words[g][:].bitcast(BF16))

        dst, src = u_views(0)
        nc.scalar.copy(out=dst[:, U_VECTOR:, :], in_=src[:, U_VECTOR:, :])
        nc.vector.tensor_copy(out=dst[:, :U_VECTOR, :], in_=src[:, :U_VECTOR, :])
        gather_last(0)
        gather(0)
        dst, src = u_views(1)
        nc.scalar.copy(out=dst[:, U_GPSIMD:, :], in_=src[:, U_GPSIMD:, :])
        nc.gpsimd.tensor_scalar(dst[:, :U_GPSIMD, :], src[:, :U_GPSIMD, :], 1.0, 0.0, MULT, ADD)
        gather_last(1)
        nc.scalar.copy(
            out=u_words[1][:, X_WORDS:].bitcast(BF16).rearrange("p (c i j) -> p c j i", i=PACK, j=PACK),
            in_=last_rows[:].rearrange("p j (c i) -> p c j i", i=PACK),
        )
        gather(1)
        bias_all = keep.tile([P, E, N_TILES], F32, name="bias_all", tag="u_raw1", align_bytes=LINE)
        nc.scalar.copy(out=bias_all[:], in_=banks[BIAS_BANK][:, :, P - N_TILES : P])
        weave(0)
        weave(1)

        wu_bf = {
            (0, 0): place("wu_bf00", T, HALF),
            (0, 1): keep.tile([P, T], U32, name="wu_bf01", align_bytes=64),
        }
        wu_codes = [
            place("wu_codes0", T, 2 * HALF + 64)[:].rearrange("p (r m) -> p r m", r=PACK),
            keep.tile([P, PACK, P], U32, name="wu_codes1", align_bytes=64),
        ]
        wu_scales = [keep.tile([P, PACK, P], U8, name=f"wu_scales{a}", align_bytes=64) for a in range(PASSES)]

        def round_wu(copy, i, half, c0, c1):
            a, m0, m1 = WU_LOADS[i]
            dst = wu_bf[a, half][:].bitcast(BF16).rearrange("p (r m j) -> p m j r", r=2, j=PACK)[:, m0 + c0 : m0 + c1]
            copy(out=dst, in_=wu_raw[i][:].rearrange("p j (m r) -> p m j r", r=PACK)[:, c0:c1, :, 2 * half : 2 * half + 2])

        def quantise_wu(a, half):
            nc.vector.quantize_mx(
                out=wu_codes[a][:, 2 * half : 2 * half + 2, :].rearrange("p r m -> p (r m)").bitcast(FP8X4),
                scales=wu_scales[a][:, 2 * half : 2 * half + 2, :].rearrange("p r m -> p (r m)"),
                in_=wu_bf[a, half][:].bitcast(BF16),
            )

        round_wu(nc.scalar.copy, 0, 1, 0, P)
        round_wu(nc.vector.tensor_copy, 0, 0, 0, P)
        quantise_u(0)
        quantise_wu(0, 0)
        quantise_wu(0, 1)
        wu_bf[1, 0] = place("wu_bf10", T, 64)
        wu_bf[1, 1] = keep.tile([P, T], U32, name="wu_bf11", align_bytes=64)
        round_wu(nc.vector.tensor_copy, 1, 0, 0, P // 2)
        quantise_u(1)
        round_wu(nc.scalar.copy, 1, 1, 0, P // 2)
        for half in range(2):
            round_wu(nc.vector.tensor_copy, 2, half, 0, P // 2)

        groups = (((0, 0), (1, 0)), ((2, 0), (3, 0)), ((0, 1),), ((1, 1),), ((2, 1), (3, 1)))
        x_bf = [keep.tile([P, len(gr) * X_WORDS], U32, name=f"x_bf{i}", tag=f"x_bf{i}", align_bytes=LINE) for i, gr in enumerate(groups)]
        x_scales = [keep.tile([P, len(gr) * C], U8, name=f"x_scales{i}", align_bytes=64) for i, gr in enumerate(groups)]
        x_codes = {}
        where = {ea: (i, n) for i, gr in enumerate(groups) for n, ea in enumerate(gr)}

        def project(e, a, copy, order):
            bank = banks[a * E + e]
            for r in order:
                nc.tensor.matmul_mx(
                    out=bank[:, r, :],
                    lhsT=wu_codes[a][:, r, :].bitcast(FP8X4),
                    lhsT_scale=wu_scales[a][:, r, :],
                    rhs=u_codes[e // 2][:, (e % 2) * C : (e % 2 + 1) * C].bitcast(FP8X4),
                    rhs_scale=u_scales[e // 2][:, (e % 2) * C : (e % 2 + 1) * C],
                    start=True,
                    stop=True,
                )
            i, n = where[e, a]
            copy(
                out=x_bf[i][:, n * X_WORDS : (n + 1) * X_WORDS].bitcast(BF16).rearrange("p (c r) -> p c r", r=PACK),
                in_=bank[:].rearrange("p r c -> p c r"),
            )

        def quantise_x(i):
            if i not in x_codes:
                x_codes[i] = keep.tile([P, len(groups[i]) * C], U32, name=f"x_codes{i}", align_bytes=64)
            nc.vector.quantize_mx(out=x_codes[i][:].bitcast(FP8X4), scales=x_scales[i][:], in_=x_bf[i][:].bitcast(BF16))

        y = keep.tile([P, N_TILES, T], F32, name="y")

        def expert(e):
            for spot, nt in enumerate(TILE_ORDER[e]):
                cols = slice(nt * P, (nt + 1) * P)
                sums = banks[(e * N_TILES + spot) % BANKS][:, 0, :]
                for a in range(PASSES):
                    g, i = divmod(e * PASSES + a, PLANES_A_TILE)
                    xi, n = where[e, a]
                    nc.tensor.matmul_mx(
                        out=sums,
                        lhsT=w_codes[e][:, a, cols].bitcast(FP8X4),
                        lhsT_scale=w_planes[g][4 * i : P, cols],
                        rhs=x_codes[xi][:, n * C : (n + 1) * C].bitcast(FP8X4),
                        rhs_scale=x_scales[xi][:, n * C : (n + 1) * C],
                        start=(a == 0),
                        stop=(a == PASSES - 1),
                    )
                nc.scalar.activation(out=y[:, nt, e * C : (e + 1) * C], in_=sums, func=SILU, bias=bias_all[:, e, nt : nt + 1])

        results = {}
        gated = keep.tile([P, 2, T], F32, name="gated")

        def scatter_vector(nt, s0, s1):
            nc.vector.tensor_tensor(listed(results[nt][:], s0, s1), y[:, nt, s0:s1], gates[:, s0:s1], MULT)

        def times_gate(nt, s0, s1):
            nc.vector.tensor_tensor(gated[:, nt - 2, s0:s1], y[:, nt, s0:s1], gates[:, s0:s1], MULT)

        def scatter_scalar(nt, s0, s1):
            nc.scalar.activation(listed(results[nt][:], s0, s1), gated[:, nt - 2, s0:s1], COPY)

        def store(nt):
            nc.sync.dma_start(out=out[nt * P : (nt + 1) * P, :], in_=results[nt][:])

        forwards = range(PACK)
        backwards = range(PACK - 1, -1, -1)
        project(0, 0, nc.scalar.copy, forwards)
        project(1, 0, nc.scalar.copy, backwards)
        project(2, 0, nc.scalar.copy, forwards)
        project(3, 0, nc.scalar.copy, forwards)
        quantise_wu(1, 0)
        quantise_wu(1, 1)
        x_codes[0] = place("x_codes0", PAIR_SLOTS, 64)
        quantise_x(0)
        project(0, 1, nc.vector.tensor_copy, forwards)
        quantise_x(1)
        quantise_x(2)
        project(1, 1, nc.scalar.copy, backwards)
        project(2, 1, nc.vector.tensor_copy, backwards)
        project(3, 1, nc.scalar.copy, backwards)
        quantise_x(3)
        quantise_x(4)
        expert(0)
        results[0] = keep.tile([P, T], F32, name="results0", align_bytes=LINE)
        results[1] = keep.tile([P, T], F32, name="results1", align_bytes=LINE)
        results[2] = keep.tile([P, T], F32, name="results2", tag="x_bf3", align_bytes=LINE)
        scatter_vector(2, 0, SHARE)
        scatter_vector(0, 0, C)
        expert(1)
        times_gate(3, 0, 2 * C)
        scatter_vector(1, 0, 2 * C)
        expert(2)
        expert(3)
        results[3] = keep.tile([P, T], F32, name="results3", tag="w_codes3", align_bytes=LINE)
        scatter_scalar(3, 0, 2 * C)
        times_gate(2, SHARE, T)
        times_gate(3, 2 * C, T)
        scatter_scalar(2, SHARE, 2 * C)
        scatter_vector(0, 3 * C, T)
        scatter_vector(1, 2 * C, T)
        store(1)
        scatter_scalar(3, 2 * C, T)
        store(3)
        scatter_vector(0, C, 3 * C)
        store(0)
        scatter_scalar(2, 2 * C, T)
        store(2)
